import numpy as np, ml_dtypes
CORES = [9,25,41,57]
N = 4
BF = ml_dtypes.bfloat16
W, L, Q, RO, FU, SB, SC = 4096, 256, 1024, 3, 5, 1, 2
def pack(sect, mv, traj, amt, cap):
    return {"sect": np.ascontiguousarray(sect.reshape(N, 128, W)).astype(np.float32).astype(BF), "mv": np.ascontiguousarray(mv.reshape(N, 128, Q)).astype(np.int32),
            "traj": np.ascontiguousarray(traj.reshape(N, 128, L)).astype(np.int32), "amt": np.ascontiguousarray(amt.reshape(N, 128, L)).astype(np.float32).astype(BF),
            "cap": np.ascontiguousarray(cap.reshape(N, 128, 1)).astype(np.int32)}
def parts(rng):
    sect = (rng.random((N, 8, 16, W)) * 256 * rng.choice(np.array([0.5, 0.75, 1.0]), (N, 8, 1, W))).astype(np.int64)
    mv = rng.integers(0, W, (N, 8, 16, Q)); traj = rng.integers(0, W, (N, 8, 16, L))
    amt = (rng.random((N, 8, 16, L)) * rng.choice(np.array([8, 40, 100, 170, 256]), (N, 8, 1, L))).astype(np.int64)
    return sect, mv, traj, amt, rng.integers(230, 331, (N, 8, 16, 1))
def setup_inputs(rng):
    return pack(*parts(rng))
def setup_inputs_spread(rng):
    sect, mv, traj, amt, cap = parts(rng)
    sect = (np.exp2(3 + 5 * rng.random((N, 8, 1, W))) * rng.random((N, 8, 16, W))).astype(np.int64)
    amt = (np.exp2(4 + 4 * rng.random((N, 8, 1, L))) * rng.random((N, 8, 16, L))).astype(np.int64)
    traj = (W * rng.random((N, 8, 16, L)) ** 3).astype(np.int64); mv = (W * rng.random((N, 8, 16, Q)) ** 2).astype(np.int64)
    return pack(sect, mv, traj, amt, rng.integers(160, 401, (N, 8, 16, 1)))
def endmix(rng, n, top):
    k = rng.integers(0, 3, (N, 8, 1, n)); e = rng.integers(0, 2, (N, 8, 16, n))
    return top * np.where(k == 2, e, k)
def setup_inputs_ends(rng):
    sect = endmix(rng, W, 255); amt = endmix(rng, L, 255); mv = endmix(rng, Q, W - 1); traj = (W - 1) * rng.integers(0, 2, (N, 8, 16, L))
    cap = 160 + 240 * rng.integers(0, 2, (N, 8, 16, 1)); cap[:, 0] = 400; cap[:, 6:] = 160
    sect[:, 6, :, 0] = 255; sect[:, 6, :, W - 1] = 255; sect[:, 7, :, 0] = 0; sect[:, 7, :, W - 1] = 255
    amt[:, 6:, :, L - 2:] = 255; amt[:, 6:, :, 0] = 255; amt[:, 6:, :, 1] = 0
    traj[:, 6:, 0, L - 1] = 0; traj[:, 6:, 3, L - 1] = W - 1; traj[:, 6:, 13:, L - 1] = W - 1
    traj[:, 7, :15, L - 2] = 0; traj[:, 7, 15, L - 2] = W - 1; traj[:, 7, :, 1] = 0
    return pack(sect, mv, traj, amt, cap)
def setup_inputs_corners(rng):
    sect, mv, traj, amt, cap = parts(rng)
    c0 = rng.integers(160, 401, (1, 8, 16, 1)); c0[0, 0, 0] = 160; c0[0, 7, 15] = 400
    lo = np.maximum(c0 - 255, 0); hi = np.minimum(c0, 254)
    x0 = lo + (rng.random(c0.shape) * (hi - lo + 1)).astype(np.int64)
    cls = np.arange(W) % 4
    n1 = rng.choice(np.array([FU, FU + 1, 16]), (N, 8, 1, W)); n2 = rng.choice(np.array([0, FU - 1, FU, FU + 1, 16]), (N, 8, 1, W))
    n = np.where(cls == 0, 0, np.where(cls == 1, n1, n2))
    sh = rng.integers(0, 16, (N, 8, 1, W)) * rng.integers(0, 2, (N, 8, 1, W))
    over = (np.arange(16).reshape(1, 1, 16, 1) + sh) % 16 < n
    up = rng.integers(0, 3, (N, 8, 1, W)) * rng.integers(0, 2, (N, 8, 1, W))
    sect = np.where(over, np.minimum(x0 + 1 + up, 255), np.maximum(x0 - up, 0))
    kind = rng.integers(0, 6, (N, 8, 1, L)); kind[..., 0] = 1; kind[..., L - 1] = 2; kind[..., L - 2] = 5
    k = np.arange(16).reshape(1, 1, 16, 1); one = np.ones((N, 8, 16, L), np.int64)
    cl = np.where(kind == 0, 0 * one, np.where(kind == 1, one * (k == 0), np.where(kind == 2, one * (k == 15), np.where(kind == 3, rng.integers(2, 4, one.shape), np.where(kind == 4, rng.integers(0, 4, one.shape), one)))))
    traj = 4 * rng.integers(0, W // 4, (N, 8, 16, L)) + cl
    amt = np.where(kind == 4, amt, c0 - x0)
    mv[..., ::5] = (W - 1) * rng.integers(0, 2, mv[..., ::5].shape)
    return pack(sect, mv, traj, amt, np.broadcast_to(c0, (N, 8, 16, 1)))
def setup_inputs_crowd(rng):
    sect, mv, traj, amt, cap = parts(rng)
    for g in (0, 1, 2):
        sect[:, g] = rng.integers(200, 256, (N, 16, W)); amt[:, g] = rng.integers(170, 256, (N, 16, L))
    cap[:, 1] = rng.integers(300, 331, (N, 16, 1))
    pl = rng.integers(0, W, (N, 8, 1, 1)); pl[0, 0] = W - 1; pl[1, 0] = 0; traj[:, :4] = pl[:, :4]
    few = np.array([0, W - 1, W // 2, 3])
    traj[:, 4] = few[rng.integers(0, 4, (N, 16, L))]; mv[:, 4] = few[rng.integers(0, 4, (N, 16, Q))]
    traj[:, 5] = rng.integers(0, W, (N, 16, 1))
    for q in range(N):
        v = int(rng.integers(0, L)); amt[q, 1, :, v] = 0
        traj[q, 2:4, :, v] = (pl[q, 2:4, 0] + 1 + rng.integers(0, W - 1, (2, 16))) % W
        traj[q, 6] = rng.permutation(W)[:L][None, :]
    return pack(sect, mv, traj, amt, cap)
def setup_inputs_fine(rng):
    sect, mv, traj, amt, cap = parts(rng); o = rng.permutation(8); w4 = W >> 2
    for n, (base, e, share) in enumerate(((215, 20, 0.4), (240, 12, 0.4), (247, 6, 0.1))):
        g = int(o[n]); h = rng.integers(-e, e + 1, (N, 8, W)); x = np.concatenate([base + h, base - h], axis=1)
        x[:, 0] += rng.integers(1, 3, (N, W)) * (rng.random((N, W)) < share)
        x[:, :, :w4] = rng.integers(0, 21, (N, 16, w4))
        sect[:, g] = x; amt[:, g] = rng.integers(250, 256, (N, 16, L)); cap[:, g] = 160
        traj[:, g, 0] = rng.integers(0, w4, (N, L)); traj[:, g, 1:] = rng.integers(w4, W, (N, 15, L))
    for n in (3, 4):
        g = int(o[n]); hot = (rng.permutation(16) < FU).reshape(1, 16, 1)
        sect[:, g] = np.where(hot, rng.integers(200, 256, (N, 16, W)), rng.integers(0, 21, (N, 16, W)))
        amt[:, g] = np.where(hot, rng.integers(120, 256, (N, 16, L)), rng.integers(0, 21, (N, 16, L)))
        cap[:, g] = rng.integers(280, 311, (N, 16, 1))
        for q in range(0, N, 2): amt[q, g, :, int(rng.integers(0, L))] = 0
    for n in (5, 6):
        g = int(o[n]); x = rng.integers(80, 121, (N, 16, W)); x[:, :, 1::2] = rng.integers(0, 21, (N, 16, W >> 1)); sect[:, g] = x
        cap[:, g] = 400; cap[int(rng.integers(0, N)), g] = 160
        traj[:, g] = 2 * rng.integers(0, W >> 1, (N, 16, L))
        for q in range(N):
            traj[q, g, 0] = 2 * rng.permutation(W >> 1)[:L]
            a = rng.integers(100, 119, 16); a[0] += (int(np.sum(a)) + n + 1) & 1
            amt[q, g] = a[np.argsort(rng.random((16, L)), axis=0)]
    return pack(sect, mv, traj, amt, cap)
def check_inputs(d):
    bad = []
    for k, lo, hi in (("sect", 0, 255), ("mv", 0, W - 1), ("traj", 0, W - 1), ("amt", 0, 255), ("cap", 160, 400)):
        v = np.asarray(d[k]).astype(np.float64)
        if not (np.min(v) >= lo and np.max(v) <= hi): bad.append("range of " + k)
        elif not np.all(v == np.floor(v)): bad.append("whole numbers of " + k)
    return bad
def picks(x, ix):
    return np.take_along_axis(x, ix.reshape(8, 1, 16 * L), 2).reshape(8, 16, 16, L)
def full(x, z, c, th):
    return np.add.reduce((x + z[:, :, None, :] > c).astype(np.int64), axis=1) >= th
def reference(sect, mv, traj, amt, cap):
    X = sect.astype(np.float32).astype(np.int64).reshape(N, 8, 16, W); z = amt.astype(np.float32).astype(np.int64).reshape(N, 8, 16, L)
    t = traj.astype(np.int64).reshape(N, 8, 16, L); man = mv.astype(np.int64).reshape(N, 8, 16, Q); cp = cap.astype(np.int64).reshape(N, 8, 16, 1, 1)
    odd = np.zeros((N, 8, 1, 1), np.int64); kk = np.arange(16).reshape(1, 16, 1); shadows = []
    for rnd in range(RO):
        for c, g, s, a in shadows: X[c, g][:, s] = X[c, g][:, s] - a
        shadows = []; th = FU + odd; cut = []; verdict = []
        for r in range(N):
            b = (r + SB) % N; x = picks(X[b], t[r])
            fm = full(np.maximum.accumulate(x, axis=2), z[r], cp[b], th[r])
            j = np.where(np.any(fm, axis=1), np.argmax(fm, axis=1), 16)
            p = np.take_along_axis(t[r], np.minimum(j, 15)[:, None, :], 1)[:, 0]
            lead = np.zeros((8, L), bool)
            for g in range(8):
                i = np.unique(p[g], return_index=True)[1]; lead[g, i] = True
                X[b, g][:, p[g, i]] = np.minimum(X[b, g][:, p[g, i]] + (z[r, g][:, i] >> 2), 255)
            cut.append((j, p, lead))
        for r in range(N):
            c = (r + SC) % N; j, p, lead = cut[r]; y = picks(X[c], t[r])
            fy = full(y, z[r], cp[c], th[r]) & (kk >= j[:, None, :]); refused = np.any(fy, axis=1)
            score = np.add.reduce(np.maximum(y + z[r][:, :, None, :] - cp[c], 0), axis=1)
            m = np.argmax(np.where(fy, score, -1), axis=1)
            tm = np.take_along_axis(t[r], m[:, None, :], 1)
            nn = np.take_along_axis(man[c], tm & (Q - 1), 2)
            ym = np.take_along_axis(y, m[:, None, None, :], 2)[:, :, 0]
            ok = lead & (j < 16) & ~refused
            for g in range(8):
                i = np.flatnonzero(ok[g]); s = p[g, i]; a = z[r, g][:, i] >> 2
                X[c, g][:, s] = np.minimum(X[c, g][:, s] + a, 255); shadows.append((c, g, s, a))
            verdict.append((refused, nn, ym))
        for r in range(N):
            j = cut[r][0]; refused, nn, ym = verdict[r]; rf = refused[:, None, :]
            fw = full(picks(X[r], nn), z[r], cp[r], th[r])
            u = np.add.reduce(z[r], axis=1)[:, None, :]
            t[r] = np.where(rf, np.where((kk >= j[:, None, :]) & ~fw, nn, t[r]), (5 * t[r] + u + 1) & (W - 1))
            z[r] = np.where(rf, (z[r] + ym) >> 1, z[r])
            odd[r] = (np.add.reduce(refused.astype(np.int64), axis=1) & 1).reshape(8, 1, 1)
    return {"ysect": X.reshape(N, 128, W).astype(np.float32).astype(BF), "ytraj": t.reshape(N, 128, L).astype(np.float32), "yamt": z.reshape(N, 128, L).astype(np.float32).astype(BF)}

@@ -1,0 +1,649 @@
+import numpy as np
+from concourse.mybir import AluOpType as A, ActivationFunctionType as AF
+
+W, L, Q, RO = 4096, 256, 1024, 3
+BF, F32, F16, I32, U16 = "bfloat16", "float32", "float16", "int32", "uint16"
+MAGIC = 12582912.0
+EST = {"cyc": 0.00104, "gat": 1.56, "sca": 3.8, "pe": 0.6, "wait": 0.08, "hop": 3.0, "issue": 0.5, "dma": 2.0,
+       "bw": 40e3, "slack": 0.1, "fill": 0.5}
+C4 = [(0, 64), (64, 128), (128, 192), (192, 256)]
+G4 = [(a, b, "s") for a, b in C4]
+GV = [(0, 32, "v"), (32, 64, "s")] + G4[1:]
+S3 = [(0, 128), (128, 192), (192, 256)]
+PLAN = {"cgat0": GV, "cgat": G4, "jgat": GV, "hgat": G4, "cchk": C4, "jchk": C4, "hchk": C4,
+        "cexp": [(0, 128), (128, 256)], "gx": 0, "seg0": [(0, 128), (128, 256)], "cseg": S3, "jseg": S3, "hseg": C4}
+SPREAD = [{}, {"gat": 1.15, "sca": 2.5, "hop": 3.5, "wait": 0.05}, {"gat": 1.95, "sca": 5.0, "hop": 2.5, "pe": 1.0},
+          {"hop": 4.5, "wait": 0.15, "pe": 0.4, "issue": 0.8}]
+SEARCH = [900, 1]
+FOUND = []
+
+
+def _scratch():
+    s = {}
+
+    def sb(name, n, dt):
+        s[name] = ("sbuf", [128, n], dt)
+    sb("X", W + L, BF); sb("X2", W + L, BF); sb("MV", W, I32); sb("XG", W, BF); sb("ST", W, BF); sb("VJ", W, F16)
+    sb("D1", W, BF); sb("EQ", 16 * L, BF); sb("T32", L, I32); sb("CAPI", 8, I32); sb("Z0", 272, BF); sb("ZJ0", 272, BF)
+    for r in range(RO):
+        for nm in ("ZC", "ZO", "ZH"):
+            sb(nm + str(r), 272, BF)
+        for nm in ("TU", "TC", "TJ", "VS", "VH"):
+            sb(nm + str(r), L, U16)
+        for nm in ("GE", "GJ", "GH", "AP", "AH"):
+            sb(nm + str(r), L, BF)
+        for nm in ("OS", "OJ"):
+            sb(nm + str(r), 16, U16)
+    sb("OY", 16, U16); sb("RS", 16, F16); sb("P16", L, U16)
+    for nm in ("TCC", "TCH", "PROD", "BASE"):
+        sb(nm, L, F16)
+    for nm in ("TF", "RR", "RJ", "PM", "TTS", "KEY", "KEYT", "DD", "SC2", "TRX", "NF", "NS"):
+        sb(nm, L, F32)
+    sb("SCB", 272, F32); sb("FL", L, I32)
+    for nm in ("THR1", "QB", "QC", "NQC", "QJ", "NL", "GG", "MN", "AA", "NA", "UND", "YM", "RF",
+               "DM", "KEEP", "SD", "C256", "C32"):
+        sb(nm, L, BF)
+    sb("IO1", 160, F32)
+    for nm in ("WK", "IW", "IW0", "IW1"):
+        sb(nm, 160, BF)
+    for nm in ("BO", "NBO", "R15", "R64", "DF", "NI", "I5", "I4", "IK", "IN32", "IP32", "B8K"):
+        sb(nm, 128, BF)
+    for nm in ("BOF", "NBOF"):
+        sb(nm, 128, F32)
+    sb("COL", 16, F32)
+    sb("COLI", 8, I32)
+    for b in range(8):
+        s["B" + str(b)] = ("psum", [128, 512], F32)
+    return s
+
+
+SCRATCH = _scratch()
+SEMAPHORES = (["sv", "ss", "sp", "sg", "sent", "lt", "lz", "lc", "lxa", "lxb", "lm", "ox", "oz", "ot", "zj"]
+              + [nm + str(r) for r in range(RO)
+                 for nm in ("ta", "tb", "tc", "td", "tj", "gj", "gh", "oj", "va", "vb", "vc", "vd", "cx", "ah", "zc",
+                            "zh")])
+
+
+def times(op, est):
+    kind, n = op["ck"]
+    if kind in ("gat", "sca"):
+        return 0.05 + n * est[kind] * est["cyc"], 0.0
+    if kind == "pe":
+        return n * est["pe"] * est["cyc"], 0.0
+    if kind == "pool":
+        return 0.2 + 2 * n * est["cyc"], 0.0
+    if kind == "dma":
+        return 0.1, est["dma"] + n / 200.0
+    if kind == "send":
+        return est["issue"], est["hop"] - est["issue"] + n / est["bw"]
+    return n * est["cyc"], 0.0
+
+
+def link(ops):
+    hist = {}
+    for i, op in enumerate(ops):
+        deps = set()
+        for kind, views in (("r", op["rd"]), ("w", op["wr"])):
+            for name, mask in views:
+                for (j, kj, mj) in hist.get(name, []):
+                    if mask & mj and (kind == "w" or kj == "w"):
+                        deps.add(j)
+        for name, mask in op["wr"]:
+            hist[name] = [(j, kj, mj & ~mask) for (j, kj, mj) in hist.get(name, []) if mj & ~mask]
+        for kind, views in (("r", op["rd"]), ("w", op["wr"])):
+            for name, mask in views:
+                hist.setdefault(name, []).append((i, kind, mask))
+        op["data"] = deps
+        op["pre"] = deps | ({op["after"]} if op["after"] is not None else set())
+        op["banks"] = set(x[0] for x in op["rd"] + op["wr"] if SCRATCH[x[0]][0] == "psum")
+        op["post"] = []
+    for i, op in enumerate(ops):
+        for j in op["pre"]:
+            ops[j]["post"].append(i)
+
+
+def schedule(ops, est, urgent):
+    n = len(ops)
+    tm = [times(op, est) for op in ops]
+    eng = [op["eng"] for op in ops]
+
+    def gap(j, i):
+        return 0.0 if eng[j] == "p" == eng[i] else tm[j][1] + (0.0 if eng[i] == "x" else est["wait"])
+
+    way = [0.0] * n
+    for i in range(n - 1, -1, -1):
+        way[i] = tm[i][0] + max([tm[i][1]] + [gap(i, k) + way[k] for k in ops[i]["post"]])
+    prio = [way[i] + urgent.get(ops[i]["tag"], 0.0) for i in range(n)]
+    free = {e: 0.0 for e in "vspgyx"}
+    cand = {e: [] for e in free}
+    left = [len(op["pre"]) for op in ops]
+    at = [0.0] * n
+    banks, opened, order, turn, start = {}, {}, [], [set() for _ in ops], [0.0] * n
+    for i in range(n):
+        if not left[i]:
+            cand[eng[i]].append(i)
+
+    def ready(i):
+        t = at[i]
+        for b in ops[i]["banks"]:
+            for e, (j, end) in banks.get(b, {}).items():
+                if e != eng[i]:
+                    t = max(t, end + est["wait"])
+        return t
+
+    while len(order) < n:
+        best = None
+        for e in free:
+            cs = [(ready(i), i) for i in cand[e]
+                  if not (ops[i]["grp"] and ops[i]["grp"][0] and any(opened.get(b) for b in ops[i]["banks"]))]
+            if not cs:
+                continue
+            now = max(free[e], min(cs)[0])
+            pick = top = max(cs, key=lambda c: prio[c[1]])
+            if top[0] > now:
+                av = sorted([c for c in cs if c[0] <= now], key=lambda c: -prio[c[1]])
+                fit = [c for c in av if now + tm[c[1]][0] <= top[0] + est["slack"]]
+                if fit:
+                    pick = fit[0]
+                elif top[0] - now > est["fill"] * tm[av[0][1]][0]:
+                    pick = av[0]
+            t = max(free[e], pick[0])
+            if best is None or t < best[0]:
+                best = (t, e, pick[1])
+        t, e, i = best
+        cand[e].remove(i)
+        order.append(i)
+        start[i] = t
+        end = t + tm[i][0]
+        if e != "x":
+            free[e] = end
+        for b in ops[i]["banks"]:
+            for e2, (j, _e) in banks.get(b, {}).items():
+                if e2 != e:
+                    turn[i].add(j)
+            banks.setdefault(b, {})[e] = (i, end)
+            if ops[i]["grp"]:
+                opened[b] = not ops[i]["grp"][1]
+        for k in ops[i]["post"]:
+            at[k] = max(at[k], end + gap(i, k))
+            left[k] -= 1
+            if not left[k]:
+                cand[eng[k]].append(k)
+    return order, turn, start
+
+
+def replay(ops, order, turn, est):
+    tm = [times(op, est) for op in ops]
+    end, free = [0.0] * len(ops), {}
+    for i in order:
+        e = ops[i]["eng"]
+        t = 0.0 if e == "x" else free.get(e, 0.0)
+        for j in ops[i]["pre"]:
+            t = max(t, end[j] + (0.0 if ops[j]["eng"] == "p" == e else tm[j][1] + (0.0 if e == "x" else est["wait"])))
+        for j in turn[i]:
+            t = max(t, end[j] + est["wait"])
+        end[i] = free[e] = t + tm[i][0]
+    return max(end[i] + tm[i][1] for i in order)
+
+
+def best_order(ops):
+    rng = np.random.RandomState(SEARCH[1])
+    ests = [dict(EST, **v) for v in SPREAD]
+    tags = sorted(set(op["tag"] for op in ops if op["eng"] != "x"))
+    steps = [-3.0, -1.5, -0.7, 0.7, 1.5, 3.0]
+    best = None
+    urgent = {}
+    for it in range(SEARCH[0] + 1):
+        u = dict(urgent)
+        if it and rng.rand() < 0.4:
+            p, d = tags[rng.randint(len(tags))][:-3], steps[rng.randint(6)]
+            for t in tags:
+                if t[:-3] == p:
+                    u[t] = u.get(t, 0.0) + d
+        elif it:
+            for _ in range((1, 2, 4)[rng.randint(3)]):
+                t = tags[rng.randint(len(tags))]
+                u[t] = u.get(t, 0.0) + steps[rng.randint(6)]
+        order, turn, _start = schedule(ops, EST, u)
+        took = [replay(ops, order, turn, est) for est in ests]
+        if best is None or sum(took) < sum(best[0]):
+            best, urgent = (took, order, turn), u
+    return best
+
+
+def rank_program(g, core, T, topo):
+    rank = T.rank_of(core)
+    if rank is None:
+        return
+    n = len(T.cores)
+    nxt1, nxt2, prv1, prv2 = (T.cores[(rank + d) % n] for d in (1, 2, -1, -2))
+    queue = {"v": g.vector, "s": g.scalar, "p": g.tensor, "g": g, "y": g.sync}
+    ops, part = [], [""]
+
+    def R(name, a=None, b=None, st=1):
+        name = {"QH": "QB", "TT0": "DD", "FM": "RR", "IO2": "KEY"}.get(name, name)
+        t = T[name]
+        if a is None:
+            a, b = 0, t.shape[1]
+        cols = range(a, b, st)
+        mask = ((1 << b) - (1 << a)) if st == 1 else sum(1 << c for c in cols)
+        return (t[:, a:b] if st == 1 else t[:, a:b:st], name, mask, len(cols), None)
+
+    def ind(win, off):
+        return (win[0].indirect(off[0]), win[1], win[2], 16 * off[3], off)
+
+    def ap(x):
+        return x[0] if isinstance(x, tuple) else x
+
+    def add(eng, fn, outs, ins, ck, sem=None, grp=None, after=None):
+        rd, wr = [], []
+        for x in ins:
+            if isinstance(x, tuple):
+                rd.append(x[1:3])
+                if x[4]:
+                    rd.append(x[4][1:3])
+        for x in outs:
+            wr.append(x[1:3])
+            if x[4]:
+                rd.append(x[4][1:3])
+        ops.append({"eng": eng, "fn": fn, "rd": rd, "wr": wr, "sem": sem, "need": False, "ck": ck, "grp": grp,
+                    "after": after, "tag": part[0] + eng + (wr or rd)[0][0][:2]})
+        return len(ops) - 1
+
+    def work(o, ins, rate=None):
+        if o[4]:
+            return ("sca", o[3])
+        if ins and ins[0][4]:
+            return ("gat", o[3])
+        if rate is None:
+            rate = 0.5 if all(SCRATCH[x[1]][2] in (BF, F16, U16) for x in [o] + ins) else 1.0
+        return ("vec", max(64, o[3] * rate))
+
+    def tt(o, a, b, op):
+        rate = 1.0 if "psum" in (SCRATCH[a[1]][0], SCRATCH[b[1]][0]) else 2.0
+        add("v", lambda: g.vector.tensor_tensor(o[0], a[0], b[0], op), [o], [a, b], work(o, [a, b], rate))
+
+    def ts(o, a, s1, op0, s2=None, op1=None):
+        if op1 is None:
+            add("v", lambda: g.vector.tensor_scalar(o[0], a[0], ap(s1), None, op0), [o], [a, s1], work(o, [a]))
+        else:
+            add("v", lambda: g.vector.tensor_scalar(o[0], a[0], ap(s1), ap(s2), op0, op1), [o], [a, s1, s2],
+                work(o, [a]))
+
+    def cp(o, a):
+        add("v", lambda: g.vector.tensor_copy(o[0], a[0]), [o], [a], work(o, [a]))
+
+    def gcp(o, a):
+        add("g", lambda: g.affine_select(o[0], a[0], [[0, o[3]]], A.is_gt, 0.0, 1, 0), [o], [a], ("pool", o[3]))
+
+    def scan(o, d0, d1, op0, op1):
+        add("v", lambda: g.vector.tensor_tensor_scan(o[0], d0[0], d1[0], 0.0, op0, op1), [o], [d0, d1],
+            work(o, [d0, d1]))
+
+    def vtr(o, a):
+        add("v", lambda: g.vector.transpose(o[0], a[0]), [o], [a], work(o, [a]))
+
+    def mset(o, c):
+        add("v", lambda: g.vector.memset(o[0], c), [o], [], work(o, []))
+
+    def act(o, a, f, bias=0.0, scale=1.0, acc=None):
+        if acc is None:
+            add("s", lambda: g.scalar.activation(o[0], a[0], f, bias=ap(bias), scale=scale), [o], [a, bias],
+                work(o, [a], 1.0))
+        else:
+            add("s", lambda: g.scalar.activation(o[0], a[0], f, bias=ap(bias), scale=scale, accum_out=acc[0]),
+                [o, acc], [a, bias], work(o, [a], 1.0))
+
+    def mm(o, terms, after=None):
+        for i, t in enumerate(terms):
+            lt, rh = t[:2]
+            oo = t[2] if len(t) > 2 else o
+            first, end = i == 0, i == len(terms) - 1
+            add("p", lambda lt=lt, rh=rh, oo=oo, first=first, end=end: g.tensor.matmul(oo[0], lt[0], rh[0], first, end),
+                [oo], [lt, rh], ("pe", max(64, rh[3]) * (4 if SCRATCH[rh[1]][2] == F32 else 1)),
+                grp=(first, end), after=(after if first else len(ops) - 1))
+        return len(ops) - 1
+
+    def iota(o, pat, base, cm, isint=False):
+        if isint:
+            add("g", lambda: g.iota(o[0], pat, base, cm), [o], [], ("pool", o[3]))
+        else:
+            add("g", lambda: g.iota(o[0], pat, base, cm, allow_small_or_imprecise_dtypes=True), [o], [], ("pool", o[3]))
+
+    totals = {}
+
+    def dma(eng, out, in_, sem, val, outs, ins, kib):
+        totals[sem] = val
+        add(eng, lambda: queue[eng].dma_start(out, in_).then_inc(T.sem[sem], 16), outs, ins, ("dma", kib), (sem, val))
+
+    sent = [0]
+
+    def send(src, dst, to, frm, sem):
+        rid, pid = topo.addr(to)[:2]
+        mask = topo.mask(core, to)
+        sent[0] += len(topo.engines(core, to))
+        i = add("g", lambda: g.remote_dma(dst[0], src[0], T.sem[sem], T.sem.sent, pid, rid, mask), [], [src],
+                ("send", src[3] * 256), ("sent", 0))
+        val = len(topo.engines(frm, core))
+        totals[sem] = val
+        add("x", None, [dst], [], ("vec", 0), (sem, val), after=i)
+
+    col = lambda j: R("COL", j, j + 1)
+    PMC, CAPF, C255, NE15, EQ15, H0, H1, PG, GC, CNT = (col(j) for j in range(10))
+    IDN = R("IW", 16, 144)
+    LK = [R("WK", 15 - k, 143 - k) for k in range(16)]
+    TSEM, VSEM = ("ta", "tb", "tc", "td"), ("va", "vb", "vc", "vd")
+
+    part[0] = "in"
+    dma("y", T.T32[:], T.traj[:], "lt", 16, [R("T32")], [], 128)
+    dma("s", T.Z0[:, 0:L], T.amt[:], "lz", 16, [R("Z0", 0, L)], [], 64)
+    dma("y", T.CAPI[:, 0:1], T.cap[:], "lc", 16, [R("CAPI", 0, 1)], [], 1)
+    dma("s", T.X[:, 0:W // 2], T.sect[:, 0:W // 2], "lxa", 16, [R("X", 0, W // 2)], [], 1024)
+    dma("y", T.X[:, W // 2:W], T.sect[:, W // 2:W], "lxb", 16, [R("X", W // 2, W)], [], 1024)
+    iota(R("COLI", 0, 1), [[0, 1]], 0, 1, True)
+    iota(R("IO1"), [[1, 160]], 0, -1)
+    iota(R("IO2"), [[0, 16], [1, 16]], 0, 0)
+    iota(R("PM", 0, 128), [[16, 8], [0, 16]], 0, 0)
+    iota(R("TRX"), [[1, L]], W + 2048, 0)
+    mset(R("Z0", L, 272), 0.0)
+    for r in range(RO):
+        mset(R("ZO%d" % r, L, 272), 0.0)
+    mset(R("X", W, W + L), 0.0); mset(R("SCB", 0, 8), 0.0); mset(R("C256"), 256.0); mset(R("C32"), -1.0 / 32)
+    ts(R("COLI", 1, 2), R("COLI", 0, 1), 15, A.bitwise_and)
+    ts(R("COLI", 2, 3), R("COLI", 0, 1), 112, A.bitwise_and)
+    ts(R("COLI", 3, 4), R("COLI", 0, 1), 16, A.bitwise_and)
+    cp(R("TU0"), R("T32"))
+    for i, (a, b) in enumerate(PLAN["seg0"]):
+        part[0] = "in%d" % i
+        send(R("TU0", a, b), R("TC0", a, b), nxt1, prv1, TSEM[i] + "0")
+    part[0] = "in"
+    send(R("Z0"), R("ZC0"), nxt1, prv1, "zc0")
+    part[0] = "inj"
+    send(R("TU0"), R("TJ0"), nxt2, prv2, "tj0")
+    send(R("Z0"), R("ZJ0"), nxt2, prv2, "zj")
+    part[0] = "in"
+    cp(PMC, R("COLI", 1, 2)); cp(PG, R("COLI", 2, 3))
+    ts(H0, R("COLI", 3, 4), 0.0, A.is_equal); ts(H1, R("COLI", 3, 4), 0.0, A.not_equal)
+    ts(NE15, R("COLI", 1, 2), 15.0, A.not_equal); ts(EQ15, R("COLI", 1, 2), 15.0, A.is_equal)
+    cp(CAPF, R("CAPI", 0, 1)); ts(C255, R("CAPI", 0, 1), -1.0, A.mult, 255.0, A.add)
+    ts(R("WK"), R("IO1"), PMC, A.add, 15.0, A.is_equal)
+    ts(R("IW"), R("IO1"), 16.0, A.is_equal)
+    ts(R("BO"), R("PM", 0, 128), PG, A.is_equal)
+    ts(R("DM"), R("IO2"), PMC, A.is_equal)
+    ts(R("KEEP"), R("IO2"), 0.0, A.not_equal)
+    tt(R("TRX"), R("TRX"), R("DM"), A.mult)
+    tt(R("DF"), IDN, R("IW", 15, 143), A.subtract)
+    ts(R("R15"), R("BO"), EQ15, A.mult)
+    ts(R("IW0"), R("IW"), H0, A.mult); ts(R("IW1"), R("IW"), H1, A.mult)
+    ts(R("DF"), R("DF"), NE15, A.mult)
+    ts(R("SD"), R("KEEP"), 8192.03125, A.mult, -8192.0, A.add)
+    ts(R("TCH"), R("T32"), -2048.0, A.add)
+    for nm, src, sc in (("NBO", R("BO"), -1.0), ("NI", IDN, -1.0), ("I5", IDN, 5.0), ("I4", IDN, 4.0),
+                        ("IK", IDN, -4096.0), ("IN32", IDN, -32.0), ("IP32", IDN, 32.0), ("BOF", R("BO"), 1.0),
+                        ("NBOF", R("BO"), -16.0), ("R64", R("R15"), 64.0), ("B8K", R("BO"), 8192.0)):
+        act(R(nm), src, AF.Identity, scale=sc)
+
+    def gather(win, offs, parts, bias, name):
+        for a, b, e in parts:
+            part[0] = name + str(a)
+            o, src = R("XG", 16 * a, 16 * b), ind(win, R(offs, a, b))
+            if e == "s":
+                act(o, src, AF.Identity, bias=bias)
+            elif bias:
+                ts(o, src, bias, A.add)
+            else:
+                cp(o, src)
+
+    def cut_prep(z):
+        part[0] = "cp"
+        act(R("RR"), R(z, 0, L), AF.Relu, bias=C255)
+        act(R("THR1"), R("RR"), AF.Relu, bias=256.0, scale=-1.0)
+        act(R("B0", 0, L), R("THR1"), AF.Identity, bias=-1.0)
+        act(R("B0", L, 2 * L), R("THR1"), AF.Identity)
+
+    def cnt_at(segs, a, b):
+        i = [lo <= a < hi for lo, hi in segs].index(True)
+        return R("B4" if i % 2 == 0 else "B5", a, b)
+
+    cut_prep("ZC0")
+    for r in range(RO):
+        s = str(r)
+        last = r == RO - 1
+        zc, zj, zh = "ZC" + s, ("ZJ0" if r == 0 else "ZO%d" % (r - 1)), ("Z0" if r == 0 else "ZH%d" % (r - 1))
+        xa, xb = ("X", "X2") if r % 2 == 0 else ("X2", "X")
+        XW, XT = R(xa, 0, W), R(xa)
+
+        def c_scan(a, b):
+            part[0] = "cs%d" % a
+            x0 = R("XG", 16 * a, 16 * b, 16)
+            tt(x0, x0, R("B0", a, b), A.max)
+            tt(R("D1", 16 * a, 16 * b, 16), x0, R("B0", L + a, L + b), A.min)
+            scan(R("ST", 16 * a, 16 * b), R("XG", 16 * a, 16 * b), R("D1", 16 * a, 16 * b), A.max, A.min)
+            mm(cnt_at(PLAN["cseg"], a, b),
+               [(LK[k], R("ST", 16 * a + k, 16 * b, 16)) for k in range(16)] + [(R("NBO"), R("THR1", a, b))])
+
+        def c_place(a, b):
+            part[0] = "cq%d" % a
+            ts(R("TCC", a, b), R("TC" + s, a, b), -2048.0, A.add)
+            ts(R("GE" + s, a, b), cnt_at(PLAN["cseg"], a, b), R(zc, L, L + 1), A.subtract, -11.0, A.is_ge)
+            sel = mm(R("B6", a, b), [(R("DF"), R("GE" + s, a, b))])
+            tt(R("PROD", a, b), R("B6", a, b), R("TCC", a, b), A.mult)
+            bank = "B7" if PLAN["cseg"].index((a, b)) % 2 == 0 else "B3"
+            place = [(R("BO"), R("C256", a, b)), (R("R15"), R("TCC", a, b)), (R("BO"), R("PROD", a, b))]
+            got = mm(R(bank, a, b), place, sel)
+            tt(R("PM", a, b), R(bank, a, b), R("DM", a, b), A.mult)
+            scan(R("SCB", a + 1, b + 1), R("KEEP", a, b), R("PM", a, b), A.mult, A.add)
+            wide = "P16" if b - a > 64 else bank
+            if b - a > 64:
+                cp(R("P16", a, b), R(bank, a, b))
+            terms = [t + (R("B1", L + a, L + b),) for t in place]
+            for u in list(range(a // 16)) + [15] + list(range(a // 16, b // 16 - 1)):
+                if u == 15:
+                    tt(R("EQ", 15 * L + a, 15 * L + b), R(bank, a, b), R("SCB", a, b), A.is_equal)
+                    lo = a
+                else:
+                    lo = max(a, 16 * (u + 1))
+                    ts(R("EQ", u * L + lo, u * L + b), R(wide, lo, b), R("SCB", 16 * u + 16, 16 * u + 17), A.is_equal)
+                terms.append((R("B8K"), R("EQ", u * L + lo, u * L + b), R("B1", L + lo, L + b)))
+            mm(None, terms, got)
+            u, v = a // 16, b // 16
+            tt(R("NF", a, b), R("B1", L + a, L + b), R("TRX", a, b), A.min)
+            scan(R("NS", a, b), R("KEEP", a, b), R("NF", a, b), A.mult, A.add)
+            ts(R("OS" + s, u, v), R("NS", a + 15, b, 16), -2048.0, A.add)
+            tt(R("MN", a, b), ind(XT, R("OS" + s, u, v)), R("NQC", a, b), A.min)
+            tt(ind(XT, R("OS" + s, u, v)), R("MN", a, b), R("QC", a, b), A.add)
+
+        gather(XW, "TC" + s, PLAN["cgat0" if r == 0 else "cgat"], 0.0, "cg")
+        part[0] = "cz"
+        act(R("QB"), R(zc, 0, L), AF.Identity, bias=159.625, scale=0.25)
+        act(R("NQC"), R("QB"), AF.Identity, bias=415.0, scale=-1.0)
+        act(R("QC"), R("QB"), AF.Identity, bias=-160.0)
+        for a, b in PLAN["cexp"]:
+            part[0] = "cx%d" % a
+            for k in range(1, 16):
+                (gcp if r and k <= PLAN["gx"] else cp)(R("D1", 16 * a + k, 16 * b, 16), R("THR1", a, b))
+        for a, b in PLAN["cchk"]:
+            c_scan(a, b)
+        for a, b in PLAN["cseg"]:
+            c_place(a, b)
+        part[0] = "co"
+        send(R("GE" + s), R("GJ" + s), nxt1, prv1, "gj" + s)
+        send(R("OS" + s), R("OJ" + s), nxt1, prv1, "oj" + s)
+        part[0] = "ch"
+        send(R("GE" + s), R("GH" + s), prv1, nxt1, "gh" + s)
+        dma("y", T[xb][:], T[xa][:], "cx" + s, 16, [R(xb)], [XT], 1024)
+        if r == 0:
+            for j in range(4):
+                dma("y", T.MV[:, j * Q:(j + 1) * Q], T.mv[:], "lm", 64, [R("MV", j * Q, (j + 1) * Q)], [R("ZJ0")], 2048)
+        part[0] = "jp"
+        ts(R("TT0"), R("TJ" + s), 2.0 ** -17, A.mult)
+        vtr(R("TTS"), R("TT0"))
+        ts(GC, R(zj, L, L + 1), -1.0 / 16, A.mult, 1.6875, A.add)
+        act(R("RJ"), R(zj, 0, L), AF.Relu, bias=C255)
+        act(R("B1", 0, L), R("RJ"), AF.Identity, bias=127.0625, scale=-1.0)
+        act(R("RJ"), R("RJ"), AF.Identity, bias=-127.0)
+        act(R("QB"), R(zj, 0, L), AF.Identity, bias=159.625, scale=0.25)
+        act(R("QJ"), R("QB"), AF.Identity, bias=-160.0)
+        part[0] = "hp"
+        act(R("B2", 0, L), R(zh, 0, L), AF.Identity, bias=CAPF, scale=-1.0)
+        EF = R("B2", L, 2 * L)
+        mm(EF, [(R("I5"), R("TCH")), (R("BO"), R(zh, 0, L))])
+        act(R("QH"), EF, AF.Identity, bias=162.0 + 3.0 / 8192, scale=1.0 / 4096)
+        mm(EF, [(R("IK"), R("QH")), (R("I4"), R("TCH")), (R("BO"), R(zh, 0, L))])
+        act(EF, EF, AF.Identity, bias=663553.0)
+
+        def j_cmp(a, b):
+            part[0] = "jc%d" % a
+            for k in range(16):
+                tt(R("VJ", k * L + a, k * L + b), R("XG", 16 * a + k, 16 * b, 16), R("B1", a, b), A.max)
+            mm(cnt_at(PLAN["jseg"], a, b),
+               [(LK[0], R("VJ", a, b)), (R("BOF"), R("RJ", a, b))]
+               + [(LK[k], R("VJ", k * L + a, k * L + b)) for k in range(1, 16)])
+
+        def j_verdict(a, b, sem):
+            part[0] = "jk%d" % a
+            tot, u0 = cnt_at(PLAN["jseg"], a, b), R("B3", a, b)
+            u, v = a // 16, b // 16
+            ts(R("FL", a, b), tot, -1.46875, A.add)
+            tt(u0, tot, R("FL", a, b), A.subtract)
+            tt(u0, u0, R("GG", a, b), A.is_le)
+            tt(R("KEY", a, b), u0, R("FL", a, b), A.mult)
+            part[0] = "jw%d" % a
+            mm(R("B7", a, b), [(R("NBOF"), R("KEY", a, b)), (R("R64"), R("GJ" + s, a, b))])
+            mm(R("B7", L + a, L + b), [(R("BOF"), R("KEY", a, b))])
+            tt(R("MN", a, b), R("B7", a, b), R("QJ", a, b), A.min)
+            ts(R("AA", a, b), R("MN", a, b), 0.0, A.max)
+            ts(R("NA", a, b), R("MN", a, b), -1.0, A.mult, 255.0, A.add)
+            tt(R("UND", a, b), ind(XT, R("OJ" + s, u, v)), R("NA", a, b), A.min)
+            tt(ind(XT, R("OJ" + s, u, v)), R("UND", a, b), R("AA", a, b), A.add)
+            part[0] = "ja%d" % a
+            pm, w = R("B3", a, b), R("B3", L + a, L + b)
+            vtr(R("KEYT", a, b), R("KEY", a, b))
+            scan(pm, R("SD", a, b), R("KEYT", a, b), A.add, A.max)
+            tt(w, pm, R("KEYT", a, b), A.subtract)
+            tt(R("DD", a, b), R("TTS", a, b), w, A.subtract)
+            scan(R("SC2", a, b), w, R("DD", a, b), A.min, A.max)
+            ts(R("RS", u, v), R("SC2", a + 15, b, 16), 2.0 ** 17, A.mult, -2048.0, A.add)
+            for hp in range(2):
+                mm(R("B6", u + hp, v, 2),
+                   [(R("IW%d" % hp, 16 - 16 * (h - hp), 144 - 16 * (h - hp)), R("RS", u + h, v, 2)) for h in range(2)])
+            ts(R("OY", u, v), R("B6", u, v), 2048.0, A.add)
+            cp(R("VS" + s, a, b), ind(R("MV"), R("OY", u, v)))
+            send(R("VS" + s, a, b), R("VH" + s, a, b), prv2, nxt2, sem)
+
+        gather(XW, "TJ" + s, PLAN["jgat"], -128.0, "jg")
+        part[0] = "jp"
+        add("s", lambda s=s: g.scalar.activation(T.GG[:], T["GJ" + s][:], AF.Identity, scale=GC[0]),
+            [R("GG")], [R("GJ" + s), GC], ("vec", L))
+        for a, b in PLAN["jchk"]:
+            j_cmp(a, b)
+        for (a, b), sem in zip(PLAN["jseg"], VSEM):
+            j_verdict(a, b, sem + s)
+        part[0] = "jz"
+        act(R("RF"), R("B7", L, 2 * L), AF.Sign, acc=CNT)
+        act(R("AP" + s), R("RF"), AF.Identity, bias=1.0, scale=-1.0)
+        send(R("AP" + s), R("AH" + s), prv2, nxt2, "ah" + s)
+        act(R("YM"), ind(R(xb, 0, W), R("OY")), AF.Identity)
+        HZ = R("B6", L, 2 * L)
+        mm(HZ, [(IDN, R("YM")), (R("BO"), R("C32")), (R("NI"), R(zj, 0, L))])
+        act(R("FM"), HZ, AF.Identity, bias=MAGIC, scale=0.5)
+        act(HZ, R("FM"), AF.Identity, bias=-MAGIC)
+        tt(R("B3", L, 2 * L), HZ, R("RF"), A.mult)
+        tt(R("ZO" + s, 0, L), R("B3", L, 2 * L), R(zj, 0, L), A.add)
+        if last:
+            dma("y", T.ysect[:], T[xa][:, 0:W], "ox", 16, [], [XW], 1024)
+        else:
+            cp(R("COLI", 4, 5), CNT)
+            ts(R("COLI", 5, 6), R("COLI", 4, 5), 1, A.bitwise_and)
+            cp(R("ZO" + s, L, L + 1), R("COLI", 5, 6))
+            send(R("ZO" + s), R("ZC%d" % (r + 1)), prv1, nxt1, "zc%d" % (r + 1))
+            part[0] = "ju"
+            cp(ind(R(xb), R("OJ" + s)), R("UND"))
+        part[0] = "jh"
+        send(R("ZO" + s), R("ZH" + s), prv2, nxt2, "zh" + s)
+
+        def h_cmp(a, b):
+            part[0] = "hc%d" % a
+            for k in range(16):
+                tt(R("ST", k * L + a, k * L + b), R("XG", 16 * a + k, 16 * b, 16), R("B2", a, b), A.is_gt)
+            mm(cnt_at(PLAN["hseg"], a, b),
+               [(LK[k], R("ST", k * L + a, k * L + b)) for k in range(16)]
+               + [(R("IN32"), R("GH" + s, a, b)), (R("IP32"), R("AH" + s, a, b))])
+
+        def h_new(a, b, sem):
+            part[0] = "hn%d" % a
+            u, dif = R("B3", a, b), R("B1", L + a, L + b)
+            ts(R("PROD", a, b), R("VH" + s, a, b), -2048.0, A.add)
+            mm(dif, [(IDN, R("PROD", a, b)), (R("NI"), R("TCH", a, b))])
+            ts(R("NL", a, b), cnt_at(PLAN["hseg"], a, b), R(zh, L, L + 1), A.subtract, -27.0, A.is_lt)
+            tt(u, dif, R("NL", a, b), A.mult)
+            tt(R("TCH", a, b), u, R("BASE", a, b), A.add)
+            if last:
+                ts(R("TF", a, b), R("TCH", a, b), 2048.0, A.add)
+                dma("y", T.ytraj[:, a:b], T.TF[:, a:b], "ot", 16 * len(PLAN["hseg"]), [], [R("TF", a, b)], 64)
+            else:
+                nx = str(r + 1)
+                ts(R("TU" + nx, a, b), R("TCH", a, b), 2048.0, A.add)
+                send(R("TU" + nx, a, b), R("TC" + nx, a, b), nxt1, prv1, sem + nx)
+
+        gather(XW, "VH" + s, PLAN["hgat"], 0.0, "hg")
+        part[0] = "hb"
+        tt(R("B3", L, 2 * L), EF, R("AH" + s), A.mult)
+        tt(R("BASE"), R("B3", L, 2 * L), R("TCH"), A.add)
+        for a, b in PLAN["hchk"]:
+            h_cmp(a, b)
+        for (a, b), sem in zip(PLAN["hseg"], TSEM):
+            h_new(a, b, sem)
+        part[0] = "hz"
+        if last:
+            dma("y", T.yamt[:], T["ZH" + s][:, 0:L], "oz", 16, [], [R("ZH" + s, 0, L)], 64)
+        else:
+            nx = str(r + 1)
+            send(R("TU" + nx), R("TJ" + nx), nxt2, prv2, "tj" + nx)
+            cut_prep("ZC" + nx)
+
+    link(ops)
+    if not FOUND:
+        FOUND.append(best_order(ops))
+    _took, order, turn = FOUND[0]
+
+    place = {i: p for p, i in enumerate(order)}
+    known = {e: {} for e in "vspgyx"}
+    for i in order:
+        op = ops[i]
+        kn = known[op["eng"]]
+        keep = []
+        for j in sorted(op["data"] | turn[i], key=lambda j: -place[j]):
+            src = ops[j]["sem"][0] if ops[j]["sem"] else ops[j]["eng"]
+            if src == "sent" or (src == "p" and op["eng"] == "p") or op["eng"] == "x" or kn.get(src, -1) >= place[j]:
+                continue
+            keep.append(j)
+            ops[j]["need"] = True
+            kn[src] = place[j]
+            for key, v in ops[j]["knew"].items():
+                kn[key] = max(kn.get(key, -1), v)
+        op["deps"] = keep
+        op["knew"] = {} if op["eng"] == "x" else dict(kn)
+    count = {"v": 0, "s": 0, "p": 0, "g": 0}
+    for i in order:
+        op = ops[i]
+        if op["sem"] is None and op["need"]:
+            count[op["eng"]] += 1
+            op["sig"] = ("s" + op["eng"], count[op["eng"]])
+        else:
+            op["sig"] = op["sem"]
+    for i in order:
+        op = ops[i]
+        if op["fn"] is None:
+            continue
+        for j in op["deps"]:
+            queue[op["eng"]].wait_ge(T.sem[ops[j]["sig"][0]], ops[j]["sig"][1])
+        ins = op["fn"]()
+        if op["sem"] is None and op["need"]:
+            ins.then_inc(T.sem[op["sig"][0]], 1)
+    for e in count:
+        totals["s" + e] = count[e]
+    totals["sent"] = sent[0]
+    for name in SEMAPHORES:
+        if totals.get(name, 0):
+            g.wait_ge(T.sem[name], totals[name])

@@ -1,21 +1,36 @@
+import math
 import numpy as np
 from concourse.mybir import AluOpType as A, ActivationFunctionType as AF
 
 W, L, Q, RO = 4096, 256, 1024, 3
 BF, F32, F16, I32, U16 = "bfloat16", "float32", "float16", "int32", "uint16"
 MAGIC = 12582912.0
-EST = {"cyc": 0.00104, "gat": 1.56, "sca": 3.8, "pe": 0.6, "wait": 0.08, "hop": 3.0, "issue": 0.5, "dma": 2.0,
-       "bw": 40e3, "slack": 0.1, "fill": 0.5}
-C4 = [(0, 64), (64, 128), (128, 192), (192, 256)]
-G4 = [(a, b, "s") for a, b in C4]
-GV = [(0, 32, "v"), (32, 64, "s")] + G4[1:]
-S3 = [(0, 128), (128, 192), (192, 256)]
-PLAN = {"cgat0": GV, "cgat": G4, "jgat": GV, "hgat": G4, "cchk": C4, "jchk": C4, "hchk": C4,
-        "cexp": [(0, 128), (128, 256)], "gx": 0, "seg0": [(0, 128), (128, 256)], "cseg": S3, "jseg": S3, "hseg": C4}
-SPREAD = [{}, {"gat": 1.15, "sca": 2.5, "hop": 3.5, "wait": 0.05}, {"gat": 1.95, "sca": 5.0, "hop": 2.5, "pe": 1.0},
-          {"hop": 4.5, "wait": 0.15, "pe": 0.4, "issue": 0.8}]
-SEARCH = [900, 1]
+BIG = 1048576.0
+EST = {"cyc": 0.00095, "gat": 1.56, "sca": 3.8, "pe": 0.55, "wait": 0.12, "hop": 3.0, "issue": 0.4, "dma": 2.0,
+       "bw": 40e3, "rows": 0.3}
+SPREAD = [{}, {"gat": 1.15, "sca": 2.5, "hop": 3.5, "wait": 0.07}, {"gat": 1.95, "sca": 5.0, "hop": 2.5, "pe": 0.9},
+          {"hop": 4.5, "wait": 0.2, "pe": 0.45, "issue": 0.7}]
+S2 = [(128, 256), (0, 128)]
+S4 = [(192, 256), (128, 192), (64, 128), (0, 64)]
+S5 = [(192, 256), (128, 192), (64, 128), (32, 64), (0, 32)]
+
+
+def by(segs, engines):
+    return [(a, b, e) for (a, b), e in zip(segs, engines)]
+
+
+GV = [(224, 256, "s"), (192, 224, "v")] + by(S5[1:], "ssss")
+PLAN = {"cgat0": GV, "cgat": by(S5, "sssss"), "jgat": GV, "hgat": by(S4, "fsss"), "cchk": S5, "jchk": S4,
+        "cseg": S4, "jseg": S4, "hseg": S4, "zseg": by(S4, "mmcc"),
+        "cexp0": by(S2, "vv"), "cexp": by(S2, "vv"), "hexp": "g", "seg0": S2,
+        "ge": "vvvv", "nl": "vvvv", "jd": "ssss"}
+DUE = {"first": 8.0, "cut": 8.5, "judge": 8.0, "home": 7.0, "cq": 2.8, "ja": 3.8, "jw": 2.0, "jz": 5.0, "hn": 2.5}
+PLAN["grain"] = 1
+SEARCH = {"seed": 1, "warm": 0.5, "dues": 3000, "moves": 1500, "heat": 0.3}
 FOUND = []
+MATS = ("BO", "NBO", "R15", "E15", "R64", "NR64", "DF", "NI", "I5", "I4", "IK", "IN32", "IP32", "NB8K", "I64", "I512",
+        "IN256", "B16")
+ROWS = ("DM", "NDM", "NDM2", "RST", "CSP", "SD", "ONE", "C32", "CE")
 
 
 def _scratch():
@@ -24,33 +39,35 @@ def _scratch():
     def sb(name, n, dt):
         s[name] = ("sbuf", [128, n], dt)
     sb("X", W + L, BF); sb("X2", W + L, BF); sb("MV", W, I32); sb("XG", W, BF); sb("ST", W, BF); sb("VJ", W, F16)
-    sb("D1", W, BF); sb("EQ", 16 * L, BF); sb("T32", L, I32); sb("CAPI", 8, I32); sb("Z0", 272, BF); sb("ZJ0", 272, BF)
+    sb("D1", W, BF); sb("DH", W, BF); sb("SF", W, BF); sb("EQ", 16 * L, BF); sb("T32", L, I32); sb("CAPI", 8, I32)
+    sb("Z0", 272, BF); sb("ZJ0", 272, BF)
     for r in range(RO):
         for nm in ("ZC", "ZO", "ZH"):
             sb(nm + str(r), 272, BF)
-        for nm in ("TU", "TC", "TJ", "VS", "VH"):
+        for nm in ("TU", "TC", "TJ"):
             sb(nm + str(r), L, U16)
-        for nm in ("GE", "GJ", "GH", "AP", "AH"):
+        for nm in ("VS", "VH"):
+            sb(nm + str(r), 2 * L, U16)
+        for nm in ("GE", "GJ", "GH"):
             sb(nm + str(r), L, BF)
         for nm in ("OS", "OJ"):
             sb(nm + str(r), 16, U16)
-    sb("OY", 16, U16); sb("RS", 16, F16); sb("P16", L, U16)
+    sb("OY", 16, U16); sb("OR", 16, U16); sb("RS", 16, F16); sb("PH", 2 * L, F16)
     for nm in ("TCC", "TCH", "PROD", "BASE"):
         sb(nm, L, F16)
-    for nm in ("TF", "RR", "RJ", "PM", "TTS", "KEY", "KEYT", "DD", "SC2", "TRX", "NF", "NS"):
+    for nm in ("TF", "RR", "RJ", "RH", "PM", "TT0", "TTS", "KEY", "KEYT", "DD", "SC2", "NS", "FM"):
         sb(nm, L, F32)
-    sb("SCB", 272, F32); sb("FL", L, I32)
-    for nm in ("THR1", "QB", "QC", "NQC", "QJ", "NL", "GG", "MN", "AA", "NA", "UND", "YM", "RF",
-               "DM", "KEEP", "SD", "C256", "C32"):
+    sb("SCB", 320, F32); sb("FL", L, I32)
+    for nm in ("THR1", "THH", "QB", "QB2", "QC", "NQC", "QJ", "QH", "NL", "GG", "MN", "OLD", "EE", "U1", "DJ", "RU", "YM",
+               "RF", "RJB", "HF"):
         sb(nm, L, BF)
     sb("IO1", 160, F32)
     for nm in ("WK", "IW", "IW0", "IW1"):
         sb(nm, 160, BF)
-    for nm in ("BO", "NBO", "R15", "R64", "DF", "NI", "I5", "I4", "IK", "IN32", "IP32", "B8K"):
-        sb(nm, 128, BF)
+    sb("CM", 128 * len(MATS), BF); sb("CR", L * len(ROWS), BF)
     for nm in ("BOF", "NBOF"):
         sb(nm, 128, F32)
-    sb("COL", 16, F32)
+    sb("COL", 24, F32); sb("COLB", 16, BF)
     sb("COLI", 8, I32)
     for b in range(8):
         s["B" + str(b)] = ("psum", [128, 512], F32)
@@ -58,10 +75,9 @@ def _scratch():
 
 
 SCRATCH = _scratch()
+TSEM, VSEM, ZSEM = (tuple(x + y for y in "abcde") for x in "tvz")
 SEMAPHORES = (["sv", "ss", "sp", "sg", "sent", "lt", "lz", "lc", "lxa", "lxb", "lm", "ox", "oz", "ot", "zj"]
-              + [nm + str(r) for r in range(RO)
-                 for nm in ("ta", "tb", "tc", "td", "tj", "gj", "gh", "oj", "va", "vb", "vc", "vd", "cx", "ah", "zc",
-                            "zh")])
+              + [nm + str(r) for r in range(RO) for nm in TSEM + VSEM + ZSEM + ("tj", "gj", "gh", "oj", "cx", "zh")])
 
 
 def times(op, est):
@@ -71,7 +87,7 @@ def times(op, est):
     if kind == "pe":
         return n * est["pe"] * est["cyc"], 0.0
     if kind == "pool":
-        return 0.2 + 2 * n * est["cyc"], 0.0
+        return 0.17 + 2 * n * est["cyc"], 0.0
     if kind == "dma":
         return 0.1, est["dma"] + n / 200.0
     if kind == "send":
@@ -96,119 +112,190 @@ def link(ops):
         op["data"] = deps
         op["pre"] = deps | ({op["after"]} if op["after"] is not None else set())
         op["banks"] = set(x[0] for x in op["rd"] + op["wr"] if SCRATCH[x[0]][0] == "psum")
-        op["post"] = []
-    for i, op in enumerate(ops):
-        for j in op["pre"]:
-            ops[j]["post"].append(i)
 
 
-def schedule(ops, est, urgent):
-    n = len(ops)
+def lag(ops, tm, est, j, i):
+    if ops[i]["eng"] == "x":
+        return tm[j][1]
+    if j not in ops[i]["data"] or ops[j]["eng"] == "p" == ops[i]["eng"]:
+        return 0.0
+    return tm[j][1] + est["wait"]
+
+
+def jobs_of(ops, est):
     tm = [times(op, est) for op in ops]
-    eng = [op["eng"] for op in ops]
+    head, off, length = [], [], {}
+    for i, op in enumerate(ops):
+        h = head[-1] if op["grp"] and not op["grp"][0] else i
+        head.append(h)
+        off.append(length.get(h, 0.0))
+        length[h] = off[-1] + tm[i][0]
+    edge, banks = {h: {} for h in length}, {h: set() for h in length}
+    for i, op in enumerate(ops):
+        banks[head[i]] |= op["banks"]
+        for j in op["pre"]:
+            if head[j] != head[i]:
+                d = off[j] + tm[j][0] + lag(ops, tm, est, j, i) - off[i]
+                edge[head[i]][head[j]] = max(edge[head[i]].get(head[j], d), d)
+    return head, {h: (ops[h]["eng"], length[h], list(edge[h].items()), sorted(banks[h]), length[h] + tm[h][1],
+                      ops[h]["ck"][1] / est["bw"] + est["rows"] if ops[h]["ck"][0] == "send" else 0.0) for h in length}
 
-    def gap(j, i):
-        return 0.0 if eng[j] == "p" == eng[i] else tm[j][1] + (0.0 if eng[i] == "x" else est["wait"])
 
-    way = [0.0] * n
-    for i in range(n - 1, -1, -1):
-        way[i] = tm[i][0] + max([tm[i][1]] + [gap(i, k) + way[k] for k in ops[i]["post"]])
-    prio = [way[i] + urgent.get(ops[i]["tag"], 0.0) for i in range(n)]
-    free = {e: 0.0 for e in "vspgyx"}
-    cand = {e: [] for e in free}
-    left = [len(op["pre"]) for op in ops]
-    at = [0.0] * n
-    banks, opened, order, turn, start = {}, {}, [], [set() for _ in ops], [0.0] * n
-    for i in range(n):
-        if not left[i]:
-            cand[eng[i]].append(i)
-
-    def ready(i):
-        t = at[i]
-        for b in ops[i]["banks"]:
-            for e, (j, end) in banks.get(b, {}).items():
-                if e != eng[i]:
-                    t = max(t, end + est["wait"])
-        return t
-
-    while len(order) < n:
-        best = None
-        for e in free:
-            cs = [(ready(i), i) for i in cand[e]
-                  if not (ops[i]["grp"] and ops[i]["grp"][0] and any(opened.get(b) for b in ops[i]["banks"]))]
-            if not cs:
-                continue
-            now = max(free[e], min(cs)[0])
-            pick = top = max(cs, key=lambda c: prio[c[1]])
-            if top[0] > now:
-                av = sorted([c for c in cs if c[0] <= now], key=lambda c: -prio[c[1]])
-                fit = [c for c in av if now + tm[c[1]][0] <= top[0] + est["slack"]]
-                if fit:
-                    pick = fit[0]
-                elif top[0] - now > est["fill"] * tm[av[0][1]][0]:
-                    pick = av[0]
-            t = max(free[e], pick[0])
-            if best is None or t < best[0]:
-                best = (t, e, pick[1])
-        t, e, i = best
-        cand[e].remove(i)
-        order.append(i)
-        start[i] = t
-        end = t + tm[i][0]
-        if e != "x":
-            free[e] = end
-        for b in ops[i]["banks"]:
-            for e2, (j, _e) in banks.get(b, {}).items():
-                if e2 != e:
-                    turn[i].add(j)
-            banks.setdefault(b, {})[e] = (i, end)
-            if ops[i]["grp"]:
-                opened[b] = not ops[i]["grp"][1]
-        for k in ops[i]["post"]:
-            at[k] = max(at[k], end + gap(i, k))
+def place_jobs(jobs, sons, key, wait):
+    left = {h: len(jobs[h][2]) for h in jobs}
+    busy, start, rank = {}, {}, {}
+    cand = sorted((h for h in jobs if not left[h]), key=key.get)
+    while cand:
+        h = cand.pop(0)
+        e, n, before, banks, _tail, lt = jobs[h]
+        hold = [] if e == "x" else [(e, 0.0, n, 0.0, None)]
+        hold += [(b, 0.0, n, wait, e) for b in banks] + ([("link", n, lt, 0.0, None)] if lt else [])
+        t = max([0.0] + [start[j] + d for j, d in before])
+        moved = True
+        while moved:
+            moved = False
+            for res, o, d, gap, who in hold:
+                spans = busy.setdefault(res, [])
+                lo, hi = 0, len(spans)
+                while lo < hi:
+                    mid = (lo + hi) // 2
+                    if spans[mid][1] + gap <= t + o:
+                        lo = mid + 1
+                    else:
+                        hi = mid
+                while lo < len(spans) and spans[lo][0] < t + o + d + gap - 1e-9:
+                    if who is None or spans[lo][2] != who:
+                        t, moved = spans[lo][1] + gap - o + 1e-7, True
+                    lo += 1
+        start[h] = t
+        rank[h] = max([t] + [rank[j] + 1e-6 for j, d in before])
+        for res, o, d, gap, who in hold:
+            spans = busy[res]
+            lo = len(spans)
+            while lo and spans[lo - 1][0] > t + o:
+                lo -= 1
+            spans.insert(lo, (t + o, t + o + d, who))
+        for k in sons[h]:
             left[k] -= 1
             if not left[k]:
-                cand[eng[k]].append(k)
-    return order, turn, start
+                lo = 0
+                while lo < len(cand) and key[cand[lo]] <= key[k]:
+                    lo += 1
+                cand.insert(lo, k)
+    return sorted(jobs, key=rank.get)
 
 
-def replay(ops, order, turn, est):
-    tm = [times(op, est) for op in ops]
-    end, free = [0.0] * len(ops), {}
-    for i in order:
-        e = ops[i]["eng"]
-        t = 0.0 if e == "x" else free.get(e, 0.0)
-        for j in ops[i]["pre"]:
-            t = max(t, end[j] + (0.0 if ops[j]["eng"] == "p" == e else tm[j][1] + (0.0 if e == "x" else est["wait"])))
-        for j in turn[i]:
-            t = max(t, end[j] + est["wait"])
-        end[i] = free[e] = t + tm[i][0]
-    return max(end[i] + tm[i][1] for i in order)
+def run_jobs(seq, jobs, wait):
+    free, used, start, why = {}, {}, {}, {}
+    wire, worst, final = 0.0, 0.0, None
+    for h in seq:
+        e, n, before, banks, tail, lt = jobs[h]
+        t, w = free.get(e, (0.0, None))
+        for j, d in before:
+            if start[j] + d > t:
+                t, w = start[j] + d, j
+        for b in banks:
+            for e2, (t2, j) in used.setdefault(b, {}).items():
+                if e2 != e and t2 + wait > t:
+                    t, w = t2 + wait, j
+        for b in banks:
+            used[b][e] = (t + n, h)
+        if e != "x":
+            free[e] = (t + n, h)
+        if lt:
+            t = max(t, wire - n)
+            wire = t + n + lt
+        start[h], why[h] = t, w
+        if t + tail > worst:
+            worst, final = t + tail, h
+    return worst, why, final
 
 
-def best_order(ops):
-    rng = np.random.RandomState(SEARCH[1])
+def find_order(ops):
+    rng = np.random.RandomState(SEARCH["seed"])
     ests = [dict(EST, **v) for v in SPREAD]
-    tags = sorted(set(op["tag"] for op in ops if op["eng"] != "x"))
-    steps = [-3.0, -1.5, -0.7, 0.7, 1.5, 3.0]
-    best = None
-    urgent = {}
-    for it in range(SEARCH[0] + 1):
-        u = dict(urgent)
-        if it and rng.rand() < 0.4:
-            p, d = tags[rng.randint(len(tags))][:-3], steps[rng.randint(6)]
-            for t in tags:
-                if t[:-3] == p:
-                    u[t] = u.get(t, 0.0) + d
+    views = [jobs_of(ops, est)[1] for est in ests]
+    head, jobs = jobs_of(ops, EST)
+    dads = {h: set(j for j, d in jobs[h][2]) for h in jobs}
+    sons = {h: set() for h in jobs}
+    for h in jobs:
+        for j in dads[h]:
+            sons[j].add(h)
+
+    def score(seq):
+        got = [run_jobs(seq, view, est["wait"]) for view, est in zip(views, ests)]
+        return sum(x[0] for x in got), seq, got
+
+    names = sorted(set(op["due"][0] for op in ops if op["due"]))
+    kind = {h: ops[h]["kind"] for h in jobs}
+
+    def held_up(got):
+        _t, why, h = got[rng.randint(len(got))]
+        arcs = []
+        while why[h] is not None:
+            if why[h] not in dads[h]:
+                arcs.append((why[h], h))
+            h = why[h]
+        return arcs[rng.randint(len(arcs))]
+
+    best, cur, shift = None, None, {}
+    for it in range(SEARCH["dues"] + 1):
+        trial = dict(shift)
+        if it and rng.rand() < 0.25:
+            nm = names[rng.randint(len(names))]
+            trial[nm] = trial.get(nm, 0.0) + rng.randn()
         elif it:
-            for _ in range((1, 2, 4)[rng.randint(3)]):
-                t = tags[rng.randint(len(tags))]
-                u[t] = u.get(t, 0.0) + steps[rng.randint(6)]
-        order, turn, _start = schedule(ops, EST, u)
-        took = [replay(ops, order, turn, est) for est in ests]
-        if best is None or sum(took) < sum(best[0]):
-            best, urgent = (took, order, turn), u
-    return best
+            v, u = held_up(cur[2])
+            if rng.rand() < 0.5:
+                trial[kind[u]] = trial.get(kind[u], 0.0) - max(0.0, kept[u] - kept[v]) - rng.rand() ** 2
+            else:
+                trial[kind[v]] = trial.get(kind[v], 0.0) + max(0.0, kept[u] - kept[v]) + rng.rand() ** 2
+        key = {h: 1e3 for h in jobs}
+        for i, op in enumerate(ops):
+            if op["due"]:
+                key[head[i]] = op["due"][1] + trial.get(op["due"][0], 0.0)
+        for h in sorted(jobs, reverse=True):
+            key[h] += trial.get(kind[h], 0.0)
+            for j, d in jobs[h][2]:
+                key[j] = min(key[j], key[h] - d)
+        got = score(place_jobs(jobs, sons, key, EST["wait"]))
+        if cur is None or got[0] <= cur[0] - SEARCH["warm"] * (1.0 - it / SEARCH["dues"]) * math.log(1.0 - rng.rand()):
+            cur, shift, kept = got, trial, key
+        if best is None or got[0] < best[0]:
+            best = got
+    now, seq, got = best
+    for it in range(SEARCH["moves"]):
+        v, u = held_up(got)
+        a, b = seq.index(v), seq.index(u)
+        more = (0, 0, 3, 10, 30)[rng.randint(5)]
+        if rng.rand() < 0.5:
+            a, move = max(0, a - more), {u}
+            for w in reversed(seq[a:b]):
+                if sons[w] & move:
+                    move.add(w)
+            mid = [w for w in seq[a:b + 1] if w in move] + [w for w in seq[a:b + 1] if w not in move]
+        else:
+            b, move = min(len(seq) - 1, b + more), {v}
+            for w in seq[a + 1:b + 1]:
+                if dads[w] & move:
+                    move.add(w)
+            mid = [w for w in seq[a:b + 1] if w not in move] + [w for w in seq[a:b + 1] if w in move]
+        new = score(seq[:a] + mid + seq[b + 1:])
+        if new[0] <= now - SEARCH["heat"] * (1.0 - it / SEARCH["moves"]) * math.log(1.0 - rng.rand()):
+            now, seq, got = new
+            if now < best[0]:
+                best = new
+    members = {}
+    for i in range(len(ops)):
+        members.setdefault(head[i], []).append(i)
+    order = [i for h in best[1] for i in members[h]]
+    seen, turn = {}, [set() for _ in ops]
+    for i in order:
+        for b in ops[i]["banks"]:
+            at = seen.setdefault(b, {})
+            turn[i] |= set(j for e, j in at.items() if e != ops[i]["eng"])
+            at[ops[i]["eng"]] = i
+    return [x[0] for x in best[2]], order, turn
 
 
 def rank_program(g, core, T, topo):
@@ -218,16 +305,25 @@ def rank_program(g, core, T, topo):
     n = len(T.cores)
     nxt1, nxt2, prv1, prv2 = (T.cores[(rank + d) % n] for d in (1, 2, -1, -2))
     queue = {"v": g.vector, "s": g.scalar, "p": g.tensor, "g": g, "y": g.sync}
-    ops, part = [], [""]
+    ops, step = [], ["in"]
 
     def R(name, a=None, b=None, st=1):
-        name = {"QH": "QB", "TT0": "DD", "FM": "RR", "IO2": "KEY"}.get(name, name)
+        name = {"IO2": "KEY", "IO3": "KEYT"}.get(name, name)
+        if name in MATS:
+            name, a, b = "CM", 128 * MATS.index(name), 128 * MATS.index(name) + 128
+        if name in ROWS:
+            name, a, b = "CR", L * ROWS.index(name) + (a or 0), L * ROWS.index(name) + (b or L)
+        if name[0] == "Z" and a is not None:
+            a, b = a + 16, b + 16
         t = T[name]
         if a is None:
             a, b = 0, t.shape[1]
         cols = range(a, b, st)
         mask = ((1 << b) - (1 << a)) if st == 1 else sum(1 << c for c in cols)
         return (t[:, a:b] if st == 1 else t[:, a:b:st], name, mask, len(cols), None)
+
+    def parity(z):
+        return R(z, -16, -15)
 
     def ind(win, off):
         return (win[0].indirect(off[0]), win[1], win[2], 16 * off[3], off)
@@ -247,8 +343,19 @@ def rank_program(g, core, T, topo):
             if x[4]:
                 rd.append(x[4][1:3])
         ops.append({"eng": eng, "fn": fn, "rd": rd, "wr": wr, "sem": sem, "need": False, "ck": ck, "grp": grp,
-                    "after": after, "tag": part[0] + eng + (wr or rd)[0][0][:2]})
+                    "after": after, "due": None,
+                    "kind": (step[0], eng, (wr or rd)[0][0][:1 + (wr or rd)[0][0][1:2].isalpha()],
+                             (wr or rd)[0][1].bit_length() // PLAN["grain"])})
         return len(ops) - 1
+
+    def due(name, t):
+        ops[-1]["due"] = (name, t)
+
+    turns = {}
+
+    def in_turn(kind):
+        ops[-1]["after"] = turns.get(kind)
+        turns[kind] = len(ops) - 1
 
     def work(o, ins, rate=None):
         if o[4]:
@@ -276,8 +383,8 @@ def rank_program(g, core, T, topo):
     def gcp(o, a):
         add("g", lambda: g.affine_select(o[0], a[0], [[0, o[3]]], A.is_gt, 0.0, 1, 0), [o], [a], ("pool", o[3]))
 
-    def scan(o, d0, d1, op0, op1):
-        add("v", lambda: g.vector.tensor_tensor_scan(o[0], d0[0], d1[0], 0.0, op0, op1), [o], [d0, d1],
+    def scan(o, d0, d1, op0, op1, first=0.0):
+        add("v", lambda: g.vector.tensor_tensor_scan(o[0], d0[0], d1[0], first, op0, op1), [o], [d0, d1],
             work(o, [d0, d1]))
 
     def vtr(o, a):
@@ -288,11 +395,18 @@ def rank_program(g, core, T, topo):
 
     def act(o, a, f, bias=0.0, scale=1.0, acc=None):
         if acc is None:
-            add("s", lambda: g.scalar.activation(o[0], a[0], f, bias=ap(bias), scale=scale), [o], [a, bias],
+            add("s", lambda: g.scalar.activation(o[0], a[0], f, bias=ap(bias), scale=ap(scale)), [o], [a, bias, scale],
                 work(o, [a], 1.0))
         else:
-            add("s", lambda: g.scalar.activation(o[0], a[0], f, bias=ap(bias), scale=scale, accum_out=acc[0]),
-                [o, acc], [a, bias], work(o, [a], 1.0))
+            add("s", lambda: g.scalar.activation(o[0], a[0], f, bias=ap(bias), scale=ap(scale), accum_out=acc[0]),
+                [o, acc], [a, bias, scale], ("vec", max(64, o[3]) + 30))
+
+    def copy_on(e, o, a):
+        if e == "s":
+            act(o, a, AF.Identity)
+        else:
+            (cp if e == "v" else gcp)(o, a)
+        in_turn("spread" + e + o[1])
 
     def mm(o, terms, after=None):
         for i, t in enumerate(terms):
@@ -315,6 +429,7 @@ def rank_program(g, core, T, topo):
     def dma(eng, out, in_, sem, val, outs, ins, kib):
         totals[sem] = val
         add(eng, lambda: queue[eng].dma_start(out, in_).then_inc(T.sem[sem], 16), outs, ins, ("dma", kib), (sem, val))
+        in_turn("dma" + eng)
 
     sent = [0]
 
@@ -329,39 +444,32 @@ def rank_program(g, core, T, topo):
         add("x", None, [dst], [], ("vec", 0), (sem, val), after=i)
 
     col = lambda j: R("COL", j, j + 1)
-    PMC, CAPF, C255, NE15, EQ15, H0, H1, PG, GC, CNT = (col(j) for j in range(10))
+    PMC, CAPF, C255, NE15, EQ15, H0, H1, PG, GC, SBC, SBH = (col(j) for j in range(11))
     IDN = R("IW", 16, 144)
     LK = [R("WK", 15 - k, 143 - k) for k in range(16)]
-    TSEM, VSEM = ("ta", "tb", "tc", "td"), ("va", "vb", "vc", "vd")
 
-    part[0] = "in"
     dma("y", T.T32[:], T.traj[:], "lt", 16, [R("T32")], [], 128)
-    dma("s", T.Z0[:, 0:L], T.amt[:], "lz", 16, [R("Z0", 0, L)], [], 64)
+    dma("s", R("Z0", 0, L)[0], T.amt[:], "lz", 16, [R("Z0", 0, L)], [], 64)
     dma("y", T.CAPI[:, 0:1], T.cap[:], "lc", 16, [R("CAPI", 0, 1)], [], 1)
-    dma("s", T.X[:, 0:W // 2], T.sect[:, 0:W // 2], "lxa", 16, [R("X", 0, W // 2)], [], 1024)
-    dma("y", T.X[:, W // 2:W], T.sect[:, W // 2:W], "lxb", 16, [R("X", W // 2, W)], [], 1024)
+    dma("y", T.X[:, L:L + W], T.sect[:], "lxa", 16, [R("X", L, L + W)], [], 1024)
     iota(R("COLI", 0, 1), [[0, 1]], 0, 1, True)
     iota(R("IO1"), [[1, 160]], 0, -1)
     iota(R("IO2"), [[0, 16], [1, 16]], 0, 0)
     iota(R("PM", 0, 128), [[16, 8], [0, 16]], 0, 0)
-    iota(R("TRX"), [[1, L]], W + 2048, 0)
-    mset(R("Z0", L, 272), 0.0)
+    iota(R("IO3"), [[-16, 16], [0, 16]], 240, 0)
+    mset(R("Z0", -16, 0), -256.0)
     for r in range(RO):
-        mset(R("ZO%d" % r, L, 272), 0.0)
-    mset(R("X", W, W + L), 0.0); mset(R("SCB", 0, 8), 0.0); mset(R("C256"), 256.0); mset(R("C32"), -1.0 / 32)
+        mset(R("ZO%d" % r, -16, 0), -256.0)
+    mset(R("X", 0, L), 0.0); mset(R("SCB"), -BIG); mset(R("ONE"), 1.0); mset(R("C32"), -1.0 / 32); mset(R("CE"), 41472.0)
     ts(R("COLI", 1, 2), R("COLI", 0, 1), 15, A.bitwise_and)
     ts(R("COLI", 2, 3), R("COLI", 0, 1), 112, A.bitwise_and)
     ts(R("COLI", 3, 4), R("COLI", 0, 1), 16, A.bitwise_and)
     cp(R("TU0"), R("T32"))
     for i, (a, b) in enumerate(PLAN["seg0"]):
-        part[0] = "in%d" % i
         send(R("TU0", a, b), R("TC0", a, b), nxt1, prv1, TSEM[i] + "0")
-    part[0] = "in"
-    send(R("Z0"), R("ZC0"), nxt1, prv1, "zc0")
-    part[0] = "inj"
+    send(R("Z0"), R("ZC0"), nxt1, prv1, "za0")
     send(R("TU0"), R("TJ0"), nxt2, prv2, "tj0")
     send(R("Z0"), R("ZJ0"), nxt2, prv2, "zj")
-    part[0] = "in"
     cp(PMC, R("COLI", 1, 2)); cp(PG, R("COLI", 2, 3))
     ts(H0, R("COLI", 3, 4), 0.0, A.is_equal); ts(H1, R("COLI", 3, 4), 0.0, A.not_equal)
     ts(NE15, R("COLI", 1, 2), 15.0, A.not_equal); ts(EQ15, R("COLI", 1, 2), 15.0, A.is_equal)
@@ -370,154 +478,178 @@ def rank_program(g, core, T, topo):
     ts(R("IW"), R("IO1"), 16.0, A.is_equal)
     ts(R("BO"), R("PM", 0, 128), PG, A.is_equal)
     ts(R("DM"), R("IO2"), PMC, A.is_equal)
-    ts(R("KEEP"), R("IO2"), 0.0, A.not_equal)
-    tt(R("TRX"), R("TRX"), R("DM"), A.mult)
+    ts(R("RST"), R("IO2"), 0.0, A.is_equal, -BIG, A.mult)
+    ts(R("SD"), R("IO2"), 0.0, A.not_equal, 8192.0, A.mult)
+    ts(R("IO3"), R("IO3"), PMC, A.add)
+    tt(R("CSP"), R("IO3"), R("SD"), A.max)
+    ts(R("SD"), R("RST"), 1.0 / 128, A.mult, 1.0 / 32, A.add)
     tt(R("DF"), IDN, R("IW", 15, 143), A.subtract)
     ts(R("R15"), R("BO"), EQ15, A.mult)
     ts(R("IW0"), R("IW"), H0, A.mult); ts(R("IW1"), R("IW"), H1, A.mult)
     ts(R("DF"), R("DF"), NE15, A.mult)
-    ts(R("SD"), R("KEEP"), 8192.03125, A.mult, -8192.0, A.add)
+    ts(R("E15"), IDN, EQ15, A.mult)
     ts(R("TCH"), R("T32"), -2048.0, A.add)
     for nm, src, sc in (("NBO", R("BO"), -1.0), ("NI", IDN, -1.0), ("I5", IDN, 5.0), ("I4", IDN, 4.0),
                         ("IK", IDN, -4096.0), ("IN32", IDN, -32.0), ("IP32", IDN, 32.0), ("BOF", R("BO"), 1.0),
-                        ("NBOF", R("BO"), -16.0), ("R64", R("R15"), 64.0), ("B8K", R("BO"), 8192.0)):
+                        ("NBOF", R("BO"), -16.0), ("R64", R("R15"), 64.0), ("NB8K", R("BO"), -8192.0),
+                        ("NR64", R("R15"), -64.0), ("I64", IDN, 64.0), ("I512", IDN, 512.0), ("IN256", IDN, -256.0),
+                        ("B16", R("BO"), 1.0 / 16)):
         act(R(nm), src, AF.Identity, scale=sc)
+    act(R("NDM"), R("DM"), AF.Identity, bias=-16384.0, scale=16384.0)
+    act(R("NDM2"), R("DM"), AF.Identity, bias=-14080.0, scale=16384.0)
 
-    def gather(win, offs, parts, bias, name):
+    def gather(win, offs, parts, bias, name, t0):
+        clock, done = {"s": t0, "v": t0}, {}
         for a, b, e in parts:
-            part[0] = name + str(a)
-            o, src = R("XG", 16 * a, 16 * b), ind(win, R(offs, a, b))
+            o, src = R("XG", 16 * a, 16 * b), ind(win, offs(a, b))
             if e == "s":
                 act(o, src, AF.Identity, bias=bias)
+            elif e == "f":
+                tt(R("SF", 16 * a, 16 * b), src, R("DH", 16 * a, 16 * b), A.is_gt)
             elif bias:
                 ts(o, src, bias, A.add)
             else:
                 cp(o, src)
+            e = ops[-1]["eng"]
+            in_turn("gather" + e)
+            due(name + str(a), clock[e])
+            clock[e] += times(ops[-1], EST)[0]
+            done.update({lane: clock[e] for lane in range(a, b)})
+        return done
 
-    def cut_prep(z):
-        part[0] = "cp"
-        act(R("RR"), R(z, 0, L), AF.Relu, bias=C255)
-        act(R("THR1"), R("RR"), AF.Relu, bias=256.0, scale=-1.0)
-        act(R("B0", 0, L), R("THR1"), AF.Identity, bias=-1.0)
-        act(R("B0", L, 2 * L), R("THR1"), AF.Identity)
+    def cut_prep(z, segs, plan):
+        for a, b in segs:
+            act(R("RR", a, b), R(z, a, b), AF.Relu, bias=C255)
+            act(R("THR1", a, b), R("RR", a, b), AF.Identity, bias=256.0, scale=-1.0)
+            act(R("B0", a, b), R("RR", a, b), AF.Identity, bias=255.0, scale=-1.0)
+            act(R("B0", L + a, L + b), R("RR", a, b), AF.Identity, bias=256.0, scale=-1.0)
+        if "s" in PLAN["ge"]:
+            act(SBC, parity(z), AF.Identity, bias=-256.0 * 244.5, scale=-256.0)
+        for a, b, e in plan:
+            for k in range(1, 16):
+                copy_on(e[k % len(e)], R("D1", 16 * a + k, 16 * b, 16), R("THR1", a, b))
+
+    def seg_of(segs, a):
+        return [s[0] <= a < s[1] for s in segs].index(True)
 
     def cnt_at(segs, a, b):
-        i = [lo <= a < hi for lo, hi in segs].index(True)
-        return R("B4" if i % 2 == 0 else "B5", a, b)
+        return R("B3" if seg_of(segs, a) % 2 == 0 else "B4", a, b)
 
-    cut_prep("ZC0")
+    cut_prep("ZC0", [(0, L)], PLAN["cexp0"])
     for r in range(RO):
         s = str(r)
         last = r == RO - 1
         zc, zj, zh = "ZC" + s, ("ZJ0" if r == 0 else "ZO%d" % (r - 1)), ("Z0" if r == 0 else "ZH%d" % (r - 1))
         xa, xb = ("X", "X2") if r % 2 == 0 else ("X2", "X")
-        XW, XT = R(xa, 0, W), R(xa)
+        XW, XT = R(xa, L, L + W), R(xa)
+        tc = DUE["first"] + r * (DUE["cut"] + DUE["judge"] + DUE["home"])
+        tj = tc + DUE["cut"]
+        th = tj + DUE["judge"]
 
         def c_scan(a, b):
-            part[0] = "cs%d" % a
             x0 = R("XG", 16 * a, 16 * b, 16)
             tt(x0, x0, R("B0", a, b), A.max)
             tt(R("D1", 16 * a, 16 * b, 16), x0, R("B0", L + a, L + b), A.min)
             scan(R("ST", 16 * a, 16 * b), R("XG", 16 * a, 16 * b), R("D1", 16 * a, 16 * b), A.max, A.min)
             mm(cnt_at(PLAN["cseg"], a, b),
-               [(LK[k], R("ST", 16 * a + k, 16 * b, 16)) for k in range(16)] + [(R("NBO"), R("THR1", a, b))])
+               [(R("NBO"), R("THR1", a, b))] + [(LK[k], R("ST", 16 * a + k, 16 * b, 16)) for k in range(16)])
 
-        def c_place(a, b):
-            part[0] = "cq%d" % a
+        def c_place(i, a, b):
+            u, v, o = a // 16, b // 16, 8 * (len(PLAN["cseg"]) - i)
             ts(R("TCC", a, b), R("TC" + s, a, b), -2048.0, A.add)
-            ts(R("GE" + s, a, b), cnt_at(PLAN["cseg"], a, b), R(zc, L, L + 1), A.subtract, -11.0, A.is_ge)
-            sel = mm(R("B6", a, b), [(R("DF"), R("GE" + s, a, b))])
-            tt(R("PROD", a, b), R("B6", a, b), R("TCC", a, b), A.mult)
-            bank = "B7" if PLAN["cseg"].index((a, b)) % 2 == 0 else "B3"
-            place = [(R("BO"), R("C256", a, b)), (R("R15"), R("TCC", a, b)), (R("BO"), R("PROD", a, b))]
-            got = mm(R(bank, a, b), place, sel)
-            tt(R("PM", a, b), R(bank, a, b), R("DM", a, b), A.mult)
-            scan(R("SCB", a + 1, b + 1), R("KEEP", a, b), R("PM", a, b), A.mult, A.add)
-            wide = "P16" if b - a > 64 else bank
-            if b - a > 64:
-                cp(R("P16", a, b), R(bank, a, b))
-            terms = [t + (R("B1", L + a, L + b),) for t in place]
-            for u in list(range(a // 16)) + [15] + list(range(a // 16, b // 16 - 1)):
-                if u == 15:
-                    tt(R("EQ", 15 * L + a, 15 * L + b), R(bank, a, b), R("SCB", a, b), A.is_equal)
+            if PLAN["ge"][i] == "s":
+                act(R("GE" + s, a, b), cnt_at(PLAN["cseg"], a, b), AF.Sigmoid, bias=SBC, scale=256.0)
+            else:
+                ts(R("GE" + s, a, b), cnt_at(PLAN["cseg"], a, b), parity(zc), A.subtract, 245.0, A.is_ge)
+            mm(R("B5", a, b), [(R("E15"), R("ONE", a, b)), (R("DF"), R("GE" + s, a, b))])
+            tt(R("PROD", a, b), R("B5", a, b), R("TCC", a, b), A.mult)
+            place = (R("BO"), R("PROD", a, b))
+            got = mm(R("B6", a, b), [(IDN, R("NDM", a, b)), place])
+            mm(R("B6", L + a, L + b), [place], got)
+            held = lambda lo, hi: R("SCB", o + lo, o + hi)
+            scan(held(a + 1, b + 1), R("RST", a, b), R("B6", a, b), A.add, A.max, -BIG)
+            terms = [(IDN, R("NDM2", a, b)), place]
+            for w in [15] + list(range(u, v - 1)):
+                if w == 15:
+                    tt(R("EQ", 15 * L + a, 15 * L + b), R("B6", L + a, L + b), held(a, b), A.is_equal)
                     lo = a
                 else:
-                    lo = max(a, 16 * (u + 1))
-                    ts(R("EQ", u * L + lo, u * L + b), R(wide, lo, b), R("SCB", 16 * u + 16, 16 * u + 17), A.is_equal)
-                terms.append((R("B8K"), R("EQ", u * L + lo, u * L + b), R("B1", L + lo, L + b)))
-            mm(None, terms, got)
-            u, v = a // 16, b // 16
-            tt(R("NF", a, b), R("B1", L + a, L + b), R("TRX", a, b), A.min)
-            scan(R("NS", a, b), R("KEEP", a, b), R("NF", a, b), A.mult, A.add)
-            ts(R("OS" + s, u, v), R("NS", a + 15, b, 16), -2048.0, A.add)
-            tt(R("MN", a, b), ind(XT, R("OS" + s, u, v)), R("NQC", a, b), A.min)
-            tt(ind(XT, R("OS" + s, u, v)), R("MN", a, b), R("QC", a, b), A.add)
+                    lo = 16 * (w + 1)
+                    ts(R("EQ", w * L + lo, w * L + b), R("B6", L + lo, L + b), held(lo, lo + 1), A.is_equal)
+                terms.append((R("NB8K"), R("EQ", w * L + lo, w * L + b), R("B7", lo, b)))
+            mm(R("B7", a, b), terms)
+            scan(R("NS", a, b), R("CSP", a, b), R("B7", a, b), A.min, A.max, BIG)
+            cp(R("OS" + s, u, v), R("NS", a + 15, b, 16))
+            due("cq%d" % a, done[a] + DUE["cq"])
+            if a == 0:
+                ts(R("OR", u, v), R("SCB", o + a + 16, o + b + 1, 16), 2304.0, A.add)
+            tt(R("MN", a, b), ind(XT, R("OR" if a == 0 else "OS" + s, u, v)), R("NQC", a, b), A.min)
 
-        gather(XW, "TC" + s, PLAN["cgat0" if r == 0 else "cgat"], 0.0, "cg")
-        part[0] = "cz"
+        step[0] = "c"
+        done = gather(XW, lambda a, b: R("TC" + s, a, b), PLAN["cgat0" if r == 0 else "cgat"], 0.0, "cg", tc)
         act(R("QB"), R(zc, 0, L), AF.Identity, bias=159.625, scale=0.25)
         act(R("NQC"), R("QB"), AF.Identity, bias=415.0, scale=-1.0)
         act(R("QC"), R("QB"), AF.Identity, bias=-160.0)
-        for a, b in PLAN["cexp"]:
-            part[0] = "cx%d" % a
-            for k in range(1, 16):
-                (gcp if r and k <= PLAN["gx"] else cp)(R("D1", 16 * a + k, 16 * b, 16), R("THR1", a, b))
         for a, b in PLAN["cchk"]:
             c_scan(a, b)
+        for i, (a, b) in enumerate(PLAN["cseg"]):
+            c_place(i, a, b)
         for a, b in PLAN["cseg"]:
-            c_place(a, b)
-        part[0] = "co"
+            tt(ind(XT, R("OS" + s, a // 16, b // 16)), R("MN", a, b), R("QC", a, b), A.add)
         send(R("GE" + s), R("GJ" + s), nxt1, prv1, "gj" + s)
         send(R("OS" + s), R("OJ" + s), nxt1, prv1, "oj" + s)
-        part[0] = "ch"
         send(R("GE" + s), R("GH" + s), prv1, nxt1, "gh" + s)
         dma("y", T[xb][:], T[xa][:], "cx" + s, 16, [R(xb)], [XT], 1024)
         if r == 0:
             for j in range(4):
-                dma("y", T.MV[:, j * Q:(j + 1) * Q], T.mv[:], "lm", 64, [R("MV", j * Q, (j + 1) * Q)], [R("ZJ0")], 2048)
-        part[0] = "jp"
+                dma("s", T.MV[:, j * Q:(j + 1) * Q], T.mv[:], "lm", 64, [R("MV", j * Q, (j + 1) * Q)], [R("ZJ0")],
+                    512 * (j + 1))
         ts(R("TT0"), R("TJ" + s), 2.0 ** -17, A.mult)
         vtr(R("TTS"), R("TT0"))
-        ts(GC, R(zj, L, L + 1), -1.0 / 16, A.mult, 1.6875, A.add)
+        act(GC, parity(zj), AF.Identity, bias=1.6875 - 16.0, scale=-1.0 / 16)
         act(R("RJ"), R(zj, 0, L), AF.Relu, bias=C255)
         act(R("B1", 0, L), R("RJ"), AF.Identity, bias=127.0625, scale=-1.0)
-        act(R("RJ"), R("RJ"), AF.Identity, bias=-127.0)
-        act(R("QB"), R(zj, 0, L), AF.Identity, bias=159.625, scale=0.25)
-        act(R("QJ"), R("QB"), AF.Identity, bias=-160.0)
-        part[0] = "hp"
+        act(R("RJB"), R("RJ"), AF.Identity, bias=-127.0)
+        act(R("QB2"), R(zj, 0, L), AF.Identity, bias=159.625, scale=0.25)
+        act(R("QJ"), R("QB2"), AF.Identity, bias=-224.0)
         act(R("B2", 0, L), R(zh, 0, L), AF.Identity, bias=CAPF, scale=-1.0)
-        EF = R("B2", L, 2 * L)
-        mm(EF, [(R("I5"), R("TCH")), (R("BO"), R(zh, 0, L))])
-        act(R("QH"), EF, AF.Identity, bias=162.0 + 3.0 / 8192, scale=1.0 / 4096)
-        mm(EF, [(R("IK"), R("QH")), (R("I4"), R("TCH")), (R("BO"), R(zh, 0, L))])
-        act(EF, EF, AF.Identity, bias=663553.0)
+        EF = lambda a, b: R("B2", L + a, L + b)
+        mm(EF(0, L), [(R("I5"), R("TCH")), (R("BO"), R(zh, 0, L))])
+        act(R("QH"), EF(0, L), AF.Identity, bias=162.0 + 3.0 / 8192, scale=1.0 / 4096)
+        mm(EF(0, L), [(R("IK"), R("QH")), (R("BO"), R("CE")), (R("I4"), R("TCH")), (R("BO"), R(zh, 0, L)),
+                      (R("B16"), R("ONE"))])
+        if "s" in PLAN["nl"]:
+            act(SBH, parity(zh), AF.Identity, bias=256.0 * 228.5, scale=256.0)
+        for a, b in PLAN.get("hspread") or [x[:2] for x in PLAN["hgat"] if x[2] == "f"]:
+            act(R("RH", a, b), R(zh, a, b), AF.Relu, bias=C255)
+            act(R("THH", a, b), R("RH", a, b), AF.Identity, bias=255.0, scale=-1.0)
+            for k in range(16):
+                copy_on(PLAN["hexp"][k % len(PLAN["hexp"])], R("DH", 16 * a + k, 16 * b, 16), R("THH", a, b))
 
         def j_cmp(a, b):
-            part[0] = "jc%d" % a
             for k in range(16):
                 tt(R("VJ", k * L + a, k * L + b), R("XG", 16 * a + k, 16 * b, 16), R("B1", a, b), A.max)
+                in_turn("judge")
             mm(cnt_at(PLAN["jseg"], a, b),
-               [(LK[0], R("VJ", a, b)), (R("BOF"), R("RJ", a, b))]
-               + [(LK[k], R("VJ", k * L + a, k * L + b)) for k in range(1, 16)])
+               [(R("BO"), R("RJB", a, b))] + [(LK[k], R("VJ", k * L + a, k * L + b)) for k in range(16)])
 
-        def j_verdict(a, b, sem):
-            part[0] = "jk%d" % a
-            tot, u0 = cnt_at(PLAN["jseg"], a, b), R("B3", a, b)
+        def j_verdict(i, a, b, sem):
+            tot, u0 = cnt_at(PLAN["jseg"], a, b), R("B1", L + a, L + b)
             u, v = a // 16, b // 16
             ts(R("FL", a, b), tot, -1.46875, A.add)
             tt(u0, tot, R("FL", a, b), A.subtract)
             tt(u0, u0, R("GG", a, b), A.is_le)
             tt(R("KEY", a, b), u0, R("FL", a, b), A.mult)
-            part[0] = "jw%d" % a
-            mm(R("B7", a, b), [(R("NBOF"), R("KEY", a, b)), (R("R64"), R("GJ" + s, a, b))])
+            mm(R("B5", L + a, L + b), [(IDN, R("QJ", a, b)), (R("NI"), R("EE", a, b)), (R("R64"), R("GJ" + s, a, b)),
+                                       (R("NBOF"), R("KEY", a, b))])
+            if PLAN["jd"][i] == "s":
+                act(R("DJ", a, b), R("B5", L + a, L + b), AF.Relu)
+            else:
+                ts(R("DJ", a, b), R("B5", L + a, L + b), 0.0, A.max)
+            due("jw%d" % a, done[a] + DUE["jw"])
             mm(R("B7", L + a, L + b), [(R("BOF"), R("KEY", a, b))])
-            tt(R("MN", a, b), R("B7", a, b), R("QJ", a, b), A.min)
-            ts(R("AA", a, b), R("MN", a, b), 0.0, A.max)
-            ts(R("NA", a, b), R("MN", a, b), -1.0, A.mult, 255.0, A.add)
-            tt(R("UND", a, b), ind(XT, R("OJ" + s, u, v)), R("NA", a, b), A.min)
-            tt(ind(XT, R("OJ" + s, u, v)), R("UND", a, b), R("AA", a, b), A.add)
-            part[0] = "ja%d" % a
-            pm, w = R("B3", a, b), R("B3", L + a, L + b)
+            ts(R("VS" + s, a + b, 2 * b), R("B7", L + a, L + b), 0.0, A.is_equal, 2048.0, A.add)
+            pm, w = R("B0", a, b), R("B0", L + a, L + b)
             vtr(R("KEYT", a, b), R("KEY", a, b))
             scan(pm, R("SD", a, b), R("KEYT", a, b), A.add, A.max)
             tt(w, pm, R("KEYT", a, b), A.subtract)
@@ -528,83 +660,120 @@ def rank_program(g, core, T, topo):
                 mm(R("B6", u + hp, v, 2),
                    [(R("IW%d" % hp, 16 - 16 * (h - hp), 144 - 16 * (h - hp)), R("RS", u + h, v, 2)) for h in range(2)])
             ts(R("OY", u, v), R("B6", u, v), 2048.0, A.add)
-            cp(R("VS" + s, a, b), ind(R("MV"), R("OY", u, v)))
-            send(R("VS" + s, a, b), R("VH" + s, a, b), prv2, nxt2, sem)
+            cp(R("VS" + s, 2 * a, a + b), ind(R("MV"), R("OY", u, v)))
+            send(R("VS" + s, 2 * a, 2 * b), R("VH" + s, 2 * a, 2 * b), prv2, nxt2, sem)
+            due("ja%d" % a, done[a] + DUE["ja"] + EST["hop"])
 
-        gather(XW, "TJ" + s, PLAN["jgat"], -128.0, "jg")
-        part[0] = "jp"
-        add("s", lambda s=s: g.scalar.activation(T.GG[:], T["GJ" + s][:], AF.Identity, scale=GC[0]),
-            [R("GG")], [R("GJ" + s), GC], ("vec", L))
+        def j_amounts(i, a, b):
+            count, hz = col(12 + 2 * i), R("B6", L + a, L + b)
+            act(R("RF", a, b), R("B7", L + a, L + b), AF.Sign, acc=count)
+            if i and not last:
+                act(col(13 + 2 * i), count, AF.Identity, bias=col(11 + 2 * i) if i > 1 else col(12))
+                count = col(13 + 2 * i)
+            mm(hz, [(R("BO"), R("C32", a, b)), (IDN, R(zj, a, b)), (R("I512"), R("RF", a, b)), (IDN, R("YM", a, b))])
+            act(R("FM", a, b), hz, AF.Identity, bias=MAGIC - 256.0, scale=0.5)
+            act(R("HF", a, b), R("FM", a, b), AF.Identity, bias=-MAGIC)
+            mm(R("B5", a, b), [(IDN, R(zj, a, b)), (R("IN256"), R("RF", a, b))])
+            tt(R("ZO" + s, a, b), R("B5", a, b), R("HF", a, b), A.max)
+            if not last:
+                if a == 0:
+                    act(R("COLB", 0, 1), count, AF.Identity, bias=127.875, scale=0.5)
+                    act(parity("ZO" + s), R("COLB", 0, 1), AF.Identity, bias=count, scale=-2.0)
+                lo = a or -16
+                send(R("ZO" + s, lo, b), R("ZC%d" % (r + 1), lo, b), prv1, nxt1, ZSEM[i] + str(r + 1))
+                due("jz%d" % a, done[a] + DUE["jz"] + EST["hop"])
+
+        def y_m(where):
+            for a, b, e in PLAN["zseg"]:
+                if e == where:
+                    act(R("YM", a, b), ind(XW if e == "m" else R(xb, L, L + W), R("OY", a // 16, b // 16)), AF.Identity)
+
+        step[0] = "j"
+        done = gather(XW, lambda a, b: R("TJ" + s, a, b), PLAN["jgat"], -128.0, "jg", tj)
+        act(R("GG"), R("GJ" + s), AF.Identity, scale=GC)
+        act(R("OLD"), ind(XT, R("OJ" + s)), AF.Identity)
+        mm(R("B7", 0, L), [(IDN, R("QJ")), (IDN, R("OLD"))])
+        act(R("EE"), R("B7", 0, L), AF.Relu, bias=-191.0)
         for a, b in PLAN["jchk"]:
             j_cmp(a, b)
-        for (a, b), sem in zip(PLAN["jseg"], VSEM):
-            j_verdict(a, b, sem + s)
-        part[0] = "jz"
-        act(R("RF"), R("B7", L, 2 * L), AF.Sign, acc=CNT)
-        act(R("AP" + s), R("RF"), AF.Identity, bias=1.0, scale=-1.0)
-        send(R("AP" + s), R("AH" + s), prv2, nxt2, "ah" + s)
-        act(R("YM"), ind(R(xb, 0, W), R("OY")), AF.Identity)
-        HZ = R("B6", L, 2 * L)
-        mm(HZ, [(IDN, R("YM")), (R("BO"), R("C32")), (R("NI"), R(zj, 0, L))])
-        act(R("FM"), HZ, AF.Identity, bias=MAGIC, scale=0.5)
-        act(HZ, R("FM"), AF.Identity, bias=-MAGIC)
-        tt(R("B3", L, 2 * L), HZ, R("RF"), A.mult)
-        tt(R("ZO" + s, 0, L), R("B3", L, 2 * L), R(zj, 0, L), A.add)
+        for i, ((a, b), sem) in enumerate(zip(PLAN["jseg"], VSEM)):
+            j_verdict(i, a, b, sem + s)
+        y_m("m")
+        for a, b in PLAN["jseg"]:
+            tt(ind(XT, R("OJ" + s, a // 16, b // 16)), R("OLD", a, b), R("DJ", a, b), A.add)
+        y_m("c")
+        for i, (a, b, e) in enumerate(PLAN["zseg"]):
+            j_amounts(i, a, b)
         if last:
-            dma("y", T.ysect[:], T[xa][:, 0:W], "ox", 16, [], [XW], 1024)
+            dma("y", T.ysect[:], T[xa][:, L:L + W], "ox", 16, [], [XW, R("VH" + s, 0, 2)], 1024)
         else:
-            cp(R("COLI", 4, 5), CNT)
-            ts(R("COLI", 5, 6), R("COLI", 4, 5), 1, A.bitwise_and)
-            cp(R("ZO" + s, L, L + 1), R("COLI", 5, 6))
-            send(R("ZO" + s), R("ZC%d" % (r + 1)), prv1, nxt1, "zc%d" % (r + 1))
-            part[0] = "ju"
-            cp(ind(R(xb), R("OJ" + s)), R("UND"))
-        part[0] = "jh"
+            mm(R("B7", 0, L), [(IDN, R("OLD")), (R("NI"), R("EE"))])
+            act(R("U1"), R("B7", 0, L), AF.Identity)
+            mm(R("B7", 0, L), [(IDN, R("EE")), (R("NR64"), R("GJ" + s)), (R("I64"), R("RF"))])
+            act(R("RU"), R("B7", 0, L), AF.Relu)
+            for a, b in PLAN["cseg"]:
+                tt(ind(R(xb), R("OJ" + s, a // 16, b // 16)), R("U1", a, b), R("RU", a, b), A.add)
         send(R("ZO" + s), R("ZH" + s), prv2, nxt2, "zh" + s)
 
-        def h_cmp(a, b):
-            part[0] = "hc%d" % a
-            for k in range(16):
-                tt(R("ST", k * L + a, k * L + b), R("XG", 16 * a + k, 16 * b, 16), R("B2", a, b), A.is_gt)
-            mm(cnt_at(PLAN["hseg"], a, b),
-               [(LK[k], R("ST", k * L + a, k * L + b)) for k in range(16)]
-               + [(R("IN32"), R("GH" + s, a, b)), (R("IP32"), R("AH" + s, a, b))])
+        def voff(a, b):
+            lo = PLAN["jseg"][seg_of(PLAN["jseg"], a)][0]
+            return lo + a, lo + b
 
-        def h_new(a, b, sem):
-            part[0] = "hn%d" % a
-            u, dif = R("B3", a, b), R("B1", L + a, L + b)
-            ts(R("PROD", a, b), R("VH" + s, a, b), -2048.0, A.add)
-            mm(dif, [(IDN, R("PROD", a, b)), (R("NI"), R("TCH", a, b))])
-            ts(R("NL", a, b), cnt_at(PLAN["hseg"], a, b), R(zh, L, L + 1), A.subtract, -27.0, A.is_lt)
+        def aoff(a, b):
+            hi = PLAN["jseg"][seg_of(PLAN["jseg"], a)][1]
+            return hi + a, hi + b
+
+        def h_cmp(a, b, e):
+            if e == "f":
+                flags = [R("SF", 16 * a + k, 16 * b, 16) for k in range(16)]
+            else:
+                flags = [R("VJ", k * L + a, k * L + b) for k in range(16)]
+                for k in range(16):
+                    tt(flags[k], R("XG", 16 * a + k, 16 * b, 16), R("B2", a, b), A.is_gt)
+                    in_turn("home")
+            mm(cnt_at(PLAN["hseg"], a, b),
+               [(R("IN32"), R("GH" + s, a, b)), (R("IP32"), R("PH", *aoff(a, b)))]
+               + [(LK[k], flags[k]) for k in range(16)])
+
+        def h_new(i, a, b, sem):
+            u, dif = R("B1", L + a, L + b), R("B5" if i % 2 else "B6", a, b)
+            mm(dif, [(IDN, R("PH", *voff(a, b))), (R("NI"), R("TCH", a, b))])
+            tt(u, EF(a, b), R("PH", *aoff(a, b)), A.mult)
+            tt(R("BASE", a, b), u, R("TCH", a, b), A.add)
+            if PLAN["nl"][i] == "s":
+                act(R("NL", a, b), cnt_at(PLAN["hseg"], a, b), AF.Sigmoid, bias=SBH, scale=-256.0)
+            else:
+                ts(R("NL", a, b), cnt_at(PLAN["hseg"], a, b), parity(zh), A.subtract, 229.0, A.is_lt)
             tt(u, dif, R("NL", a, b), A.mult)
             tt(R("TCH", a, b), u, R("BASE", a, b), A.add)
             if last:
                 ts(R("TF", a, b), R("TCH", a, b), 2048.0, A.add)
                 dma("y", T.ytraj[:, a:b], T.TF[:, a:b], "ot", 16 * len(PLAN["hseg"]), [], [R("TF", a, b)], 64)
+                due("hn%d" % a, done[a] + DUE["hn"])
             else:
                 nx = str(r + 1)
                 ts(R("TU" + nx, a, b), R("TCH", a, b), 2048.0, A.add)
                 send(R("TU" + nx, a, b), R("TC" + nx, a, b), nxt1, prv1, sem + nx)
+                due("hn%d" % a, done[a] + DUE["hn"] + EST["hop"])
 
-        gather(XW, "VH" + s, PLAN["hgat"], 0.0, "hg")
-        part[0] = "hb"
-        tt(R("B3", L, 2 * L), EF, R("AH" + s), A.mult)
-        tt(R("BASE"), R("B3", L, 2 * L), R("TCH"), A.add)
-        for a, b in PLAN["hchk"]:
-            h_cmp(a, b)
-        for (a, b), sem in zip(PLAN["hseg"], TSEM):
-            h_new(a, b, sem)
-        part[0] = "hz"
+        step[0] = "h"
+        done = gather(XW, lambda a, b: R("VH" + s, *voff(a, b)), PLAN["hgat"], 0.0, "hg", th)
+        for a, b in PLAN["jseg"]:
+            ts(R("PH", 2 * a, 2 * b), R("VH" + s, 2 * a, 2 * b), -2048.0, A.add)
+        for a, b, e in PLAN["hgat"]:
+            h_cmp(a, b, e)
         if last:
-            dma("y", T.yamt[:], T["ZH" + s][:, 0:L], "oz", 16, [], [R("ZH" + s, 0, L)], 64)
-        else:
+            dma("s", T.yamt[:], R("ZH" + s, 0, L)[0], "oz", 16, [], [R("ZH" + s, 0, L)], 64)
+        for i, ((a, b), sem) in enumerate(zip(PLAN["hseg"], TSEM)):
+            h_new(i, a, b, sem)
+        if not last:
             nx = str(r + 1)
             send(R("TU" + nx), R("TJ" + nx), nxt2, prv2, "tj" + nx)
-            cut_prep("ZC" + nx)
+            cut_prep("ZC" + nx, [x[:2] for x in PLAN["zseg"]], PLAN["cexp"])
 
     link(ops)
     if not FOUND:
-        FOUND.append(best_order(ops))
+        FOUND.append(find_order(ops))
     _took, order, turn = FOUND[0]
 
     place = {i: p for p, i in enumerate(order)}

@@ -6,10 +6,10 @@ W, L, Q, RO = 4096, 256, 1024, 3
 BF, F32, F16, I32, U16 = "bfloat16", "float32", "float16", "int32", "uint16"
 MAGIC = 12582912.0
 BIG = 1048576.0
-EST = {"cyc": 0.00095, "gat": 1.56, "sca": 3.8, "pe": 0.55, "wait": 0.12, "hop": 3.0, "issue": 0.4, "dma": 2.0,
-       "bw": 40e3, "rows": 0.3}
-SPREAD = [{}, {"gat": 1.15, "sca": 2.5, "hop": 3.5, "wait": 0.07}, {"gat": 1.95, "sca": 5.0, "hop": 2.5, "pe": 0.9},
-          {"hop": 4.5, "wait": 0.2, "pe": 0.45, "issue": 0.7}]
+EST = {"cyc": 0.0009, "gat": 1.56, "sca": 3.8, "pe": 0.8, "wait": 0.12, "hop": 3.0, "issue": 0.4, "dma": 2.0,
+       "bw": 40e3, "rows": 0.5}
+SPREAD = [{}, {"gat": 1.15, "sca": 2.5, "hop": 3.5, "wait": 0.07, "pe": 1.0},
+          {"gat": 1.95, "sca": 5.0, "hop": 2.5, "pe": 0.55}, {"hop": 4.5, "wait": 0.2, "issue": 0.7, "pe": 0.55}]
 S2 = [(128, 256), (0, 128)]
 S4 = [(192, 256), (128, 192), (64, 128), (0, 64)]
 S5 = [(192, 256), (128, 192), (64, 128), (32, 64), (0, 32)]
@@ -20,16 +20,25 @@ def by(segs, engines):
 
 
 GV = [(224, 256, "s"), (192, 224, "v")] + by(S5[1:], "ssss")
-PLAN = {"cgat0": GV, "cgat": by(S5, "sssss"), "jgat": GV, "hgat": by(S4, "fsss"), "cchk": S5, "jchk": S4,
-        "cseg": S4, "jseg": S4, "hseg": S4, "zseg": by(S4, "mmcc"),
-        "cexp0": by(S2, "vv"), "cexp": by(S2, "vv"), "hexp": "g", "seg0": S2,
-        "ge": "vvvv", "nl": "vvvv", "jd": "ssss"}
-DUE = {"first": 8.0, "cut": 8.5, "judge": 8.0, "home": 7.0, "cq": 2.8, "ja": 3.8, "jw": 2.0, "jz": 5.0, "hn": 2.5}
+E5 = [(224, 256), (160, 224), (96, 160), (32, 96), (0, 32)]
+Q4 = [(0, 1024), (1024, 2048), (2048, 3072), (3072, 4096)]
+PLAN = {"cgat0": GV, "cgat": by(S5, "sssss"), "jgat": GV, "jchk": by(S4, "ssss"), "hgat": by(S4, "fsss"), "cchk": S5,
+        "cseg": S4, "jseg": S4, "hseg": S4, "zseg": by(S2, "mc"),
+        "cexp0": by(S2, "vv"), "cexp": by(S2, "vv"), "hexp": "g", "jexp": "g", "seg0": S2,
+        "ge": "vvvvv", "nl": "vvvvv", "jd": "sssss", "less": [], "more": by(Q4, "svss")}
+DUE = {"first": 8.0, "cut": 10.0, "judge": 8.0, "home": 8.0, "cg": 7.0, "jg": 6.5, "hg": 6.5,
+       "cq": 3.0, "ja": 4.0, "jw": 2.0, "jz": 4.5, "hn": 2.5}
+PLAN["hgat2"] = by(S4, "fsfs")
+PLAN["cgat"] = by(S5, "sssvs")
+PLAN["cgat0"] = GV[:4] + by(S5[3:], "vs")
 PLAN["grain"] = 1
-SEARCH = {"seed": 1, "warm": 0.5, "dues": 3000, "moves": 1500, "heat": 0.3}
+PLAN["join"] = 2
+PLAN["keep0"] = "s"
+SEARCH = {"seed": 1, "many": 1, "pull": 0.6, "far": 2.0, "mix": 0.2, "warm": 0.4, "tries": 3, "dues": 1200, "moves": 9000,
+          "heat": 0.1}
 FOUND = []
 MATS = ("BO", "NBO", "R15", "E15", "R64", "NR64", "DF", "NI", "I5", "I4", "IK", "IN32", "IP32", "NB8K", "I64", "I512",
-        "IN256", "B16")
+        "IN256", "NI64", "MJ")
 ROWS = ("DM", "NDM", "NDM2", "RST", "CSP", "SD", "ONE", "C32", "CE")
 
 
@@ -40,7 +49,8 @@ def _scratch():
         s[name] = ("sbuf", [128, n], dt)
     sb("X", W + L, BF); sb("X2", W + L, BF); sb("MV", W, I32); sb("XG", W, BF); sb("ST", W, BF); sb("VJ", W, F16)
     sb("D1", W, BF); sb("DH", W, BF); sb("SF", W, BF); sb("EQ", 16 * L, BF); sb("T32", L, I32); sb("CAPI", 8, I32)
-    sb("Z0", 272, BF); sb("ZJ0", 272, BF)
+    sb("Z0", 272, BF); sb("ZJ0", 272, BF); sb("VF", W, F16); sb("DX", W, F16); sb("TJF", L, F16)
+    sb("XL", 2048, BF); sb("JS", 64, F32); sb("J16", 64, F16)
     for r in range(RO):
         for nm in ("ZC", "ZO", "ZH"):
             sb(nm + str(r), 272, BF)
@@ -53,21 +63,20 @@ def _scratch():
         for nm in ("OS", "OJ"):
             sb(nm + str(r), 16, U16)
     sb("OY", 16, U16); sb("OR", 16, U16); sb("RS", 16, F16); sb("PH", 2 * L, F16)
-    for nm in ("TCC", "TCH", "PROD", "BASE"):
+    sb("TCHX", 2 * L, F16); sb("NLX", 2 * L, BF); sb("NBOF", 128, F32)
+    for nm in ("TCC", "PROD"):
         sb(nm, L, F16)
     for nm in ("TF", "RR", "RJ", "RH", "PM", "TT0", "TTS", "KEY", "KEYT", "DD", "SC2", "NS", "FM"):
         sb(nm, L, F32)
     sb("SCB", 320, F32); sb("FL", L, I32)
-    for nm in ("THR1", "THH", "QB", "QB2", "QC", "NQC", "QJ", "QH", "NL", "GG", "MN", "OLD", "EE", "U1", "DJ", "RU", "YM",
+    for nm in ("THR1", "THH", "QB", "QB2", "QC", "NQC", "QJ", "QH", "GG", "MN", "OLD", "EE", "U1", "DJ", "RU", "YM",
                "RF", "RJB", "HF"):
         sb(nm, L, BF)
     sb("IO1", 160, F32)
     for nm in ("WK", "IW", "IW0", "IW1"):
         sb(nm, 160, BF)
     sb("CM", 128 * len(MATS), BF); sb("CR", L * len(ROWS), BF)
-    for nm in ("BOF", "NBOF"):
-        sb(nm, 128, F32)
-    sb("COL", 24, F32); sb("COLB", 16, BF)
+    sb("BOF", 128, F32); sb("COL", 24, F32); sb("COLB", 16, BF)
     sb("COLI", 8, I32)
     for b in range(8):
         s["B" + str(b)] = ("psum", [128, 512], F32)
@@ -89,7 +98,7 @@ def times(op, est):
     if kind == "pool":
         return 0.17 + 2 * n * est["cyc"], 0.0
     if kind == "dma":
-        return 0.1, est["dma"] + n / 200.0
+        return 0.1, est["dma"] + n / 280.0
     if kind == "send":
         return est["issue"], est["hop"] - est["issue"] + n / est["bw"]
     return n * est["cyc"], 0.0
@@ -126,7 +135,7 @@ def jobs_of(ops, est):
     tm = [times(op, est) for op in ops]
     head, off, length = [], [], {}
     for i, op in enumerate(ops):
-        h = head[-1] if op["grp"] and not op["grp"][0] else i
+        h = head[-1] if op["grp"] and not op["grp"][0] or op["join"] else i
         head.append(h)
         off.append(length.get(h, 0.0))
         length[h] = off[-1] + tm[i][0]
@@ -141,59 +150,61 @@ def jobs_of(ops, est):
                       ops[h]["ck"][1] / est["bw"] + est["rows"] if ops[h]["ck"][0] == "send" else 0.0) for h in length}
 
 
-def place_jobs(jobs, sons, key, wait):
-    left = {h: len(jobs[h][2]) for h in jobs}
+def place_jobs(jobs, holds, key):
     busy, start, rank = {}, {}, {}
-    cand = sorted((h for h in jobs if not left[h]), key=key.get)
-    while cand:
-        h = cand.pop(0)
-        e, n, before, banks, _tail, lt = jobs[h]
-        hold = [] if e == "x" else [(e, 0.0, n, 0.0, None)]
-        hold += [(b, 0.0, n, wait, e) for b in banks] + ([("link", n, lt, 0.0, None)] if lt else [])
-        t = max([0.0] + [start[j] + d for j, d in before])
+    for h in sorted(jobs, key=key.get):
+        before = jobs[h][2]
+        hold = holds[h]
+        t = top = 0.0
+        for j, d in before:
+            if start[j] + d > t:
+                t = start[j] + d
+            if rank[j] > top:
+                top = rank[j]
         moved = True
         while moved:
             moved = False
             for res, o, d, gap, who in hold:
                 spans = busy.setdefault(res, [])
-                lo, hi = 0, len(spans)
-                while lo < hi:
-                    mid = (lo + hi) // 2
-                    if spans[mid][1] + gap <= t + o:
-                        lo = mid + 1
-                    else:
-                        hi = mid
-                while lo < len(spans) and spans[lo][0] < t + o + d + gap - 1e-9:
-                    if who is None or spans[lo][2] != who:
-                        t, moved = spans[lo][1] + gap - o + 1e-7, True
-                    lo += 1
+                lo = hi = len(spans)
+                if lo and spans[-1][1] + gap > t + o:
+                    lo = max(0, hi - 64)
+                    if spans[lo][1] + gap > t + o:
+                        lo = 0
+                    while lo < hi:
+                        mid = (lo + hi) // 2
+                        if spans[mid][1] + gap <= t + o:
+                            lo = mid + 1
+                        else:
+                            hi = mid
+                    end = len(spans)
+                    while lo < end and spans[lo][0] < t + o + d + gap - 1e-9:
+                        if who is None or spans[lo][2] != who:
+                            t, moved = spans[lo][1] + gap - o + 1e-7, len(hold) > 1
+                        lo += 1
         start[h] = t
-        rank[h] = max([t] + [rank[j] + 1e-6 for j, d in before])
+        rank[h] = max(t, top + 1e-6)
         for res, o, d, gap, who in hold:
             spans = busy[res]
             lo = len(spans)
             while lo and spans[lo - 1][0] > t + o:
                 lo -= 1
             spans.insert(lo, (t + o, t + o + d, who))
-        for k in sons[h]:
-            left[k] -= 1
-            if not left[k]:
-                lo = 0
-                while lo < len(cand) and key[cand[lo]] <= key[k]:
-                    lo += 1
-                cand.insert(lo, k)
     return sorted(jobs, key=rank.get)
 
 
 def run_jobs(seq, jobs, wait):
-    free, used, start, why = {}, {}, {}, {}
+    free, used, start, why, ready = {}, {}, {}, {}, {}
     wire, worst, final = 0.0, 0.0, None
     for h in seq:
         e, n, before, banks, tail, lt = jobs[h]
-        t, w = free.get(e, (0.0, None))
+        t, w = 0.0, None
         for j, d in before:
             if start[j] + d > t:
                 t, w = start[j] + d, j
+        ready[h] = t
+        if e in free and free[e][0] > t:
+            t, w = free[e]
         for b in banks:
             for e2, (t2, j) in used.setdefault(b, {}).items():
                 if e2 != e and t2 + wait > t:
@@ -208,7 +219,7 @@ def run_jobs(seq, jobs, wait):
         start[h], why[h] = t, w
         if t + tail > worst:
             worst, final = t + tail, h
-    return worst, why, final
+    return worst, why, final, start, ready
 
 
 def find_order(ops):
@@ -222,50 +233,67 @@ def find_order(ops):
         for j in dads[h]:
             sons[j].add(h)
 
-    def score(seq):
-        got = [run_jobs(seq, view, est["wait"]) for view, est in zip(views, ests)]
+    holds = {h: ([] if e == "x" else [(e, 0.0, n, 0.0, None)]) + [(b, 0.0, n, EST["wait"], e) for b in banks]
+             + ([("link", n, lt, 0.0, None)] if lt else []) for h, (e, n, _b, banks, _t, lt) in jobs.items()}
+    backward = [(h, ops[h]["kind"], [(j, max(d, 1e-4)) for j, d in jobs[h][2]]) for h in sorted(jobs, reverse=True)]
+    dues = [(head[i], op["due"]) for i, op in enumerate(ops) if op["due"]]
+
+    def score(seq, than=None):
+        got = []
+        for v, (view, est) in enumerate(zip(views, ests)):
+            got.append(run_jobs(seq, view, est["wait"]))
+            if than and got[v][0] > than[2][v][0] + 1.5:
+                return 1e9, seq, got
         return sum(x[0] for x in got), seq, got
 
     names = sorted(set(op["due"][0] for op in ops if op["due"]))
     kind = {h: ops[h]["kind"] for h in jobs}
 
     def held_up(got):
-        _t, why, h = got[rng.randint(len(got))]
+        _t, why, h, start, ready = got[rng.randint(len(got))]
         arcs = []
         while why[h] is not None:
             if why[h] not in dads[h]:
-                arcs.append((why[h], h))
+                arcs.append((why[h], h, min(start[h] - ready[h], SEARCH["far"])))
             h = why[h]
-        return arcs[rng.randint(len(arcs))]
+        p = np.cumsum([x[2] + 0.05 for x in arcs])
+        return arcs[int(np.searchsorted(p, rng.rand() * p[-1]))]
 
-    best, cur, shift = None, None, {}
-    for it in range(SEARCH["dues"] + 1):
+    best = None
+    for it in list(range(SEARCH["dues"] + 1)) * SEARCH["tries"]:
+        if not it:
+            cur, shift = None, {}
         trial = dict(shift)
-        if it and rng.rand() < 0.25:
+        if it and rng.rand() < SEARCH["mix"]:
             nm = names[rng.randint(len(names))]
             trial[nm] = trial.get(nm, 0.0) + rng.randn()
         elif it:
-            v, u = held_up(cur[2])
-            if rng.rand() < 0.5:
-                trial[kind[u]] = trial.get(kind[u], 0.0) - max(0.0, kept[u] - kept[v]) - rng.rand() ** 2
-            else:
-                trial[kind[v]] = trial.get(kind[v], 0.0) + max(0.0, kept[u] - kept[v]) + rng.rand() ** 2
-        key = {h: 1e3 for h in jobs}
-        for i, op in enumerate(ops):
-            if op["due"]:
-                key[head[i]] = op["due"][1] + trial.get(op["due"][0], 0.0)
-        for h in sorted(jobs, reverse=True):
-            key[h] += trial.get(kind[h], 0.0)
-            for j, d in jobs[h][2]:
-                key[j] = min(key[j], key[h] - d)
-        got = score(place_jobs(jobs, sons, key, EST["wait"]))
+            for _ in range(1 + rng.randint(SEARCH["many"])):
+                v, u, late = held_up(cur[2])
+                if rng.rand() < SEARCH["pull"]:
+                    trial[kind[u]] = trial.get(kind[u], 0.0) - max(0.0, kept[u] - kept[v]) - rng.rand() * late
+                else:
+                    trial[kind[v]] = trial.get(kind[v], 0.0) + max(0.0, kept[u] - kept[v]) + rng.rand() ** 2
+        key = dict.fromkeys(jobs, 1e3)
+        for h, (nm, t) in dues:
+            key[h] = t + trial.get(nm, 0.0)
+        for h, kd, before in backward:
+            t = key[h] = key[h] + trial.get(kd, 0.0)
+            for j, d in before:
+                if t - d < key[j]:
+                    key[j] = t - d
+        for h, kd, before in backward[::-1]:
+            for j, d in before:
+                if key[j] >= key[h]:
+                    key[h] = key[j] + 1e-6
+        got = score(place_jobs(jobs, holds, key), cur)
         if cur is None or got[0] <= cur[0] - SEARCH["warm"] * (1.0 - it / SEARCH["dues"]) * math.log(1.0 - rng.rand()):
             cur, shift, kept = got, trial, key
         if best is None or got[0] < best[0]:
             best = got
     now, seq, got = best
     for it in range(SEARCH["moves"]):
-        v, u = held_up(got)
+        v, u, _late = held_up(got)
         a, b = seq.index(v), seq.index(u)
         more = (0, 0, 3, 10, 30)[rng.randint(5)]
         if rng.rand() < 0.5:
@@ -309,6 +337,8 @@ def rank_program(g, core, T, topo):
 
     def R(name, a=None, b=None, st=1):
         name = {"IO2": "KEY", "IO3": "KEYT"}.get(name, name)
+        if name in ("TCH", "NL"):
+            name, a, b, st = name + "X", 2 * (a or 0) + 1, 2 * (b or L), 2
         if name in MATS:
             name, a, b = "CM", 128 * MATS.index(name), 128 * MATS.index(name) + 128
         if name in ROWS:
@@ -343,7 +373,7 @@ def rank_program(g, core, T, topo):
             if x[4]:
                 rd.append(x[4][1:3])
         ops.append({"eng": eng, "fn": fn, "rd": rd, "wr": wr, "sem": sem, "need": False, "ck": ck, "grp": grp,
-                    "after": after, "due": None,
+                    "after": after, "due": None, "join": False,
                     "kind": (step[0], eng, (wr or rd)[0][0][:1 + (wr or rd)[0][0][1:2].isalpha()],
                              (wr or rd)[0][1].bit_length() // PLAN["grain"])})
         return len(ops) - 1
@@ -353,8 +383,9 @@ def rank_program(g, core, T, topo):
 
     turns = {}
 
-    def in_turn(kind):
+    def in_turn(kind, k=0):
         ops[-1]["after"] = turns.get(kind)
+        ops[-1]["join"] = k % PLAN["join"] > 0 and turns.get(kind) == len(ops) - 2 and ops[-1]["eng"] != "g"
         turns[kind] = len(ops) - 1
 
     def work(o, ins, rate=None):
@@ -401,12 +432,18 @@ def rank_program(g, core, T, topo):
             add("s", lambda: g.scalar.activation(o[0], a[0], f, bias=ap(bias), scale=ap(scale), accum_out=acc[0]),
                 [o, acc], [a, bias, scale], ("vec", max(64, o[3]) + 30))
 
-    def copy_on(e, o, a):
+    def copy_on(e, o, a, k=0):
         if e == "s":
             act(o, a, AF.Identity)
         else:
             (cp if e == "v" else gcp)(o, a)
-        in_turn("spread" + e + o[1])
+        in_turn("spread" + e + o[1], k)
+
+    def moved(e, o, a, c):
+        if e == "s":
+            act(o, a, AF.Identity, bias=c)
+        else:
+            ts(o, a, c, A.add)
 
     def mm(o, terms, after=None):
         for i, t in enumerate(terms):
@@ -448,10 +485,15 @@ def rank_program(g, core, T, topo):
     IDN = R("IW", 16, 144)
     LK = [R("WK", 15 - k, 143 - k) for k in range(16)]
 
+    SH = 128.0 if PLAN["less"] else 0.0
     dma("y", T.T32[:], T.traj[:], "lt", 16, [R("T32")], [], 128)
     dma("s", R("Z0", 0, L)[0], T.amt[:], "lz", 16, [R("Z0", 0, L)], [], 64)
     dma("y", T.CAPI[:, 0:1], T.cap[:], "lc", 16, [R("CAPI", 0, 1)], [], 1)
-    dma("y", T.X[:, L:L + W], T.sect[:], "lxa", 16, [R("X", L, L + W)], [], 1024)
+    for h, sem in enumerate(("lxa", "lxb")):
+        a, b = h * W // 2, (h + 1) * W // 2
+        dma("y", T.X[:, L + a:L + b], T.sect[:, a:b], sem, 16, [R("X", L + a, L + b)], [], 512 * (h + 1))
+    for a, b, e in PLAN["less"]:
+        moved(e, R("X", L + a, L + b), R("X", L + a, L + b), -128.0)
     iota(R("COLI", 0, 1), [[0, 1]], 0, 1, True)
     iota(R("IO1"), [[1, 160]], 0, -1)
     iota(R("IO2"), [[0, 16], [1, 16]], 0, 0)
@@ -460,20 +502,26 @@ def rank_program(g, core, T, topo):
     mset(R("Z0", -16, 0), -256.0)
     for r in range(RO):
         mset(R("ZO%d" % r, -16, 0), -256.0)
-    mset(R("X", 0, L), 0.0); mset(R("SCB"), -BIG); mset(R("ONE"), 1.0); mset(R("C32"), -1.0 / 32); mset(R("CE"), 41472.0)
+    mset(R("X", 0, L), 0.0); mset(R("SCB"), -BIG); mset(R("ONE"), 1.0); mset(R("C32"), -1.0 / 32); mset(R("NLX"), 0.0)
     ts(R("COLI", 1, 2), R("COLI", 0, 1), 15, A.bitwise_and)
     ts(R("COLI", 2, 3), R("COLI", 0, 1), 112, A.bitwise_and)
     ts(R("COLI", 3, 4), R("COLI", 0, 1), 16, A.bitwise_and)
     cp(R("TU0"), R("T32"))
+    opening = []
     for i, (a, b) in enumerate(PLAN["seg0"]):
-        send(R("TU0", a, b), R("TC0", a, b), nxt1, prv1, TSEM[i] + "0")
-    send(R("Z0"), R("ZC0"), nxt1, prv1, "za0")
-    send(R("TU0"), R("TJ0"), nxt2, prv2, "tj0")
-    send(R("Z0"), R("ZJ0"), nxt2, prv2, "zj")
+        opening += [(R("TU0", a, b), R("TC0", a, b), nxt1, prv1, TSEM[i] + "0"),
+                    (R("Z0", a or -16, b), R("ZC0", a or -16, b), nxt1, prv1, ZSEM[i] + "0")]
+    opening += [(R("Z0"), R("ZJ0"), nxt2, prv2, "zj"), (R("TU0"), R("TJ0"), nxt2, prv2, "tj0")]
+    for i, m in enumerate(opening):
+        send(*m)
+        ops[-2]["after"] = len(ops) - 4 if i else None
     cp(PMC, R("COLI", 1, 2)); cp(PG, R("COLI", 2, 3))
     ts(H0, R("COLI", 3, 4), 0.0, A.is_equal); ts(H1, R("COLI", 3, 4), 0.0, A.not_equal)
     ts(NE15, R("COLI", 1, 2), 15.0, A.not_equal); ts(EQ15, R("COLI", 1, 2), 15.0, A.is_equal)
-    cp(CAPF, R("CAPI", 0, 1)); ts(C255, R("CAPI", 0, 1), -1.0, A.mult, 255.0, A.add)
+    ts(col(21), R("COLI", 1, 2), 0.0, A.is_equal, 1025.0, A.mult); tt(col(20), col(21), NE15, A.subtract)
+    ts(col(22), R("COLI", 1, 2), 1.0, A.is_equal, 663552.0, A.mult); tt(col(23), col(22), EQ15, A.add)
+    act(R("CE"), R("ONE"), AF.Identity, scale=col(23))
+    ts(CAPF, R("CAPI", 0, 1), -SH, A.add); ts(C255, R("CAPI", 0, 1), -1.0, A.mult, 255.0, A.add)
     ts(R("WK"), R("IO1"), PMC, A.add, 15.0, A.is_equal)
     ts(R("IW"), R("IO1"), 16.0, A.is_equal)
     ts(R("BO"), R("PM", 0, 128), PG, A.is_equal)
@@ -491,43 +539,46 @@ def rank_program(g, core, T, topo):
     ts(R("TCH"), R("T32"), -2048.0, A.add)
     for nm, src, sc in (("NBO", R("BO"), -1.0), ("NI", IDN, -1.0), ("I5", IDN, 5.0), ("I4", IDN, 4.0),
                         ("IK", IDN, -4096.0), ("IN32", IDN, -32.0), ("IP32", IDN, 32.0), ("BOF", R("BO"), 1.0),
-                        ("NBOF", R("BO"), -16.0), ("R64", R("R15"), 64.0), ("NB8K", R("BO"), -8192.0),
-                        ("NR64", R("R15"), -64.0), ("I64", IDN, 64.0), ("I512", IDN, 512.0), ("IN256", IDN, -256.0),
-                        ("B16", R("BO"), 1.0 / 16)):
+                        ("NI64", IDN, -64.0), ("NBOF", R("BO"), -16.0), ("R64", R("R15"), 64.0), ("NB8K", R("BO"), -8192.0),
+                        ("NR64", R("R15"), -64.0), ("I64", IDN, 64.0), ("I512", IDN, 512.0), ("IN256", IDN, -256.0)):
         act(R(nm), src, AF.Identity, scale=sc)
     act(R("NDM"), R("DM"), AF.Identity, bias=-16384.0, scale=16384.0)
     act(R("NDM2"), R("DM"), AF.Identity, bias=-14080.0, scale=16384.0)
 
-    def gather(win, offs, parts, bias, name, t0):
-        clock, done = {"s": t0, "v": t0}, {}
+    if PLAN["keep0"]:
+        mset(R("XL", 1024, 2048), 0.0)
+        iota(R("JS"), [[16, 64]], 15, 0)
+        cp(R("J16"), R("JS"))
+        ts(R("MJ"), R("BO"), col(20), A.mult)
+
+    def held_in(name, a):
+        return "XL" if PLAN["keep0"] and name == "cg" and a < PLAN["cseg"][-1][1] else "XG"
+
+    def gather(win, offs, parts, fused, name, t0):
+        clock, done = t0, {}
         for a, b, e in parts:
-            o, src = R("XG", 16 * a, 16 * b), ind(win, offs(a, b))
-            if e == "s":
-                act(o, src, AF.Identity, bias=bias)
-            elif e == "f":
-                tt(R("SF", 16 * a, 16 * b), src, R("DH", 16 * a, 16 * b), A.is_gt)
-            elif bias:
-                ts(o, src, bias, A.add)
+            o, src = R(held_in(name, a), 16 * a, 16 * b), ind(win, offs(a, b))
+            if e == "f":
+                tt(R(fused[0], 16 * a, 16 * b), src, R(fused[1], 16 * a, 16 * b), fused[2])
             else:
-                cp(o, src)
-            e = ops[-1]["eng"]
-            in_turn("gather" + e)
-            due(name + str(a), clock[e])
-            clock[e] += times(ops[-1], EST)[0]
-            done.update({lane: clock[e] for lane in range(a, b)})
+                moved(e, o, src, SH - 128.0 if name == "jg" else 0.0)
+            in_turn("gather" + ops[-1]["eng"])
+            due(name + str(a), clock)
+            clock += DUE[name] * (b - a) / L
+            done.update({lane: clock for lane in range(a, b)})
         return done
 
     def cut_prep(z, segs, plan):
         for a, b in segs:
             act(R("RR", a, b), R(z, a, b), AF.Relu, bias=C255)
-            act(R("THR1", a, b), R("RR", a, b), AF.Identity, bias=256.0, scale=-1.0)
-            act(R("B0", a, b), R("RR", a, b), AF.Identity, bias=255.0, scale=-1.0)
-            act(R("B0", L + a, L + b), R("RR", a, b), AF.Identity, bias=256.0, scale=-1.0)
+            act(R("THR1", a, b), R("RR", a, b), AF.Identity, bias=256.0 - SH, scale=-1.0)
+            act(R("B0", a, b), R("RR", a, b), AF.Identity, bias=255.0 - SH, scale=-1.0)
+            act(R("B0", L + a, L + b), R("RR", a, b), AF.Identity, bias=256.0 - SH, scale=-1.0)
         if "s" in PLAN["ge"]:
             act(SBC, parity(z), AF.Identity, bias=-256.0 * 244.5, scale=-256.0)
         for a, b, e in plan:
             for k in range(1, 16):
-                copy_on(e[k % len(e)], R("D1", 16 * a + k, 16 * b, 16), R("THR1", a, b))
+                copy_on(e[k % len(e)], R("D1", 16 * a + k, 16 * b, 16), R("THR1", a, b), k - 1)
 
     def seg_of(segs, a):
         return [s[0] <= a < s[1] for s in segs].index(True)
@@ -535,7 +586,7 @@ def rank_program(g, core, T, topo):
     def cnt_at(segs, a, b):
         return R("B3" if seg_of(segs, a) % 2 == 0 else "B4", a, b)
 
-    cut_prep("ZC0", [(0, L)], PLAN["cexp0"])
+    cut_prep("ZC0", PLAN["seg0"], PLAN["cexp0"])
     for r in range(RO):
         s = str(r)
         last = r == RO - 1
@@ -547,15 +598,18 @@ def rank_program(g, core, T, topo):
         th = tj + DUE["judge"]
 
         def c_scan(a, b):
-            x0 = R("XG", 16 * a, 16 * b, 16)
+            xg = held_in("cg", a)
+            x0 = R(xg, 16 * a, 16 * b, 16)
+            if xg == "XL":
+                copy_on(PLAN["keep0"], R("XL", 1025 + 16 * a, 1025 + 16 * b - 15, 16), x0)
             tt(x0, x0, R("B0", a, b), A.max)
             tt(R("D1", 16 * a, 16 * b, 16), x0, R("B0", L + a, L + b), A.min)
-            scan(R("ST", 16 * a, 16 * b), R("XG", 16 * a, 16 * b), R("D1", 16 * a, 16 * b), A.max, A.min)
-            mm(cnt_at(PLAN["cseg"], a, b),
-               [(R("NBO"), R("THR1", a, b))] + [(LK[k], R("ST", 16 * a + k, 16 * b, 16)) for k in range(16)])
+            scan(R("ST", 16 * a, 16 * b), R(xg, 16 * a, 16 * b), R("D1", 16 * a, 16 * b), A.max, A.min)
 
         def c_place(i, a, b):
             u, v, o = a // 16, b // 16, 8 * (len(PLAN["cseg"]) - i)
+            mm(cnt_at(PLAN["cseg"], a, b),
+               [(R("NBO"), R("THR1", a, b))] + [(LK[k], R("ST", 16 * a + k, 16 * b, 16)) for k in range(16)])
             ts(R("TCC", a, b), R("TC" + s, a, b), -2048.0, A.add)
             if PLAN["ge"][i] == "s":
                 act(R("GE" + s, a, b), cnt_at(PLAN["cseg"], a, b), AF.Sigmoid, bias=SBC, scale=256.0)
@@ -581,14 +635,20 @@ def rank_program(g, core, T, topo):
             scan(R("NS", a, b), R("CSP", a, b), R("B7", a, b), A.min, A.max, BIG)
             cp(R("OS" + s, u, v), R("NS", a + 15, b, 16))
             due("cq%d" % a, done[a] + DUE["cq"])
+            if a == 0 and PLAN["keep0"]:
+                mm(R("B5", L, L + b), [(IDN, R("J16", 0, b)), (IDN, R("NDM", 0, b)), (R("MJ"), R("GE" + s, 0, b))])
+                scan(R("JS", 0, b), R("RST", 0, b), R("B5", L, L + b), A.add, A.max, -BIG)
+                cp(R("OR", u, v), R("JS", 15, b, 16))
+                tt(R("MN", a, b), ind(R("XL"), R("OR", u, v)), R("NQC", a, b), A.min)
+                return
             if a == 0:
                 ts(R("OR", u, v), R("SCB", o + a + 16, o + b + 1, 16), 2304.0, A.add)
             tt(R("MN", a, b), ind(XT, R("OR" if a == 0 else "OS" + s, u, v)), R("NQC", a, b), A.min)
 
         step[0] = "c"
-        done = gather(XW, lambda a, b: R("TC" + s, a, b), PLAN["cgat0" if r == 0 else "cgat"], 0.0, "cg", tc)
+        done = gather(XW, lambda a, b: R("TC" + s, a, b), PLAN["cgat0" if r == 0 else "cgat"], None, "cg", tc)
         act(R("QB"), R(zc, 0, L), AF.Identity, bias=159.625, scale=0.25)
-        act(R("NQC"), R("QB"), AF.Identity, bias=415.0, scale=-1.0)
+        act(R("NQC"), R("QB"), AF.Identity, bias=415.0 - SH, scale=-1.0)
         act(R("QC"), R("QB"), AF.Identity, bias=-160.0)
         for a, b in PLAN["cchk"]:
             c_scan(a, b)
@@ -604,6 +664,7 @@ def rank_program(g, core, T, topo):
             for j in range(4):
                 dma("s", T.MV[:, j * Q:(j + 1) * Q], T.mv[:], "lm", 64, [R("MV", j * Q, (j + 1) * Q)], [R("ZJ0")],
                     512 * (j + 1))
+        hgat = PLAN["hgat2" if last else "hgat"]
         ts(R("TT0"), R("TJ" + s), 2.0 ** -17, A.mult)
         vtr(R("TTS"), R("TT0"))
         act(GC, parity(zj), AF.Identity, bias=1.6875 - 16.0, scale=-1.0 / 16)
@@ -616,22 +677,34 @@ def rank_program(g, core, T, topo):
         EF = lambda a, b: R("B2", L + a, L + b)
         mm(EF(0, L), [(R("I5"), R("TCH")), (R("BO"), R(zh, 0, L))])
         act(R("QH"), EF(0, L), AF.Identity, bias=162.0 + 3.0 / 8192, scale=1.0 / 4096)
-        mm(EF(0, L), [(R("IK"), R("QH")), (R("BO"), R("CE")), (R("I4"), R("TCH")), (R("BO"), R(zh, 0, L)),
-                      (R("B16"), R("ONE"))])
+        mm(EF(0, L), [(R("IK"), R("QH")), (R("BO"), R("CE")), (R("I4"), R("TCH")), (R("BO"), R(zh, 0, L))])
         if "s" in PLAN["nl"]:
             act(SBH, parity(zh), AF.Identity, bias=256.0 * 228.5, scale=256.0)
-        for a, b in PLAN.get("hspread") or [x[:2] for x in PLAN["hgat"] if x[2] == "f"]:
+        for a, b in PLAN.get("hspread2" if last else "hspread") or [x[:2] for x in hgat if x[2] == "f"]:
             act(R("RH", a, b), R(zh, a, b), AF.Relu, bias=C255)
-            act(R("THH", a, b), R("RH", a, b), AF.Identity, bias=255.0, scale=-1.0)
+            act(R("THH", a, b), R("RH", a, b), AF.Identity, bias=255.0 - SH, scale=-1.0)
             for k in range(16):
                 copy_on(PLAN["hexp"][k % len(PLAN["hexp"])], R("DH", 16 * a + k, 16 * b, 16), R("THH", a, b))
+        for a, b in PLAN.get("jspread") or [x[:2] for x in PLAN["jgat"] if x[2] == "f"]:
+            ts(R("TJF", a, b), R("RJ", a, b), -1.0, A.mult, 127.0625, A.add)
+            for k in range(0 if SH or r == 0 else 1, 16):
+                copy_on(PLAN["jexp"][k % len(PLAN["jexp"])], R("DX", 16 * a + k, 16 * b, 16), R("TJF", a, b))
 
-        def j_cmp(a, b):
-            for k in range(16):
-                tt(R("VJ", k * L + a, k * L + b), R("XG", 16 * a + k, 16 * b, 16), R("B1", a, b), A.max)
-                in_turn("judge")
-            mm(cnt_at(PLAN["jseg"], a, b),
-               [(R("BO"), R("RJB", a, b))] + [(LK[k], R("VJ", k * L + a, k * L + b)) for k in range(16)])
+        def j_cmp(a, b, e):
+            if e == "f":
+                tops = [R("VF", 16 * a + k, 16 * b, 16) for k in range(16)]
+            elif e == "y":
+                y0 = R("XG", 16 * a, 16 * b, 16)
+                tops = [R("VJ", a, b)] + [R("VF", 16 * a + k, 16 * b, 16) for k in range(1, 16)]
+                tt(tops[0], y0, R("B1", a, b), A.max)
+                mset(y0, 512.0)
+                scan(R("VF", 16 * a, 16 * b), R("DX", 16 * a, 16 * b), R("XG", 16 * a, 16 * b), A.min, A.max)
+            else:
+                tops = [R("VJ", k * L + a, k * L + b) for k in range(16)]
+                for k in range(16):
+                    tt(tops[k], R("XG", 16 * a + k, 16 * b, 16), R("B1", a, b), A.max)
+                    in_turn("judge", k)
+            mm(cnt_at(PLAN["jseg"], a, b), [(R("BO"), R("RJB", a, b))] + [(LK[k], tops[k]) for k in range(16)])
 
         def j_verdict(i, a, b, sem):
             tot, u0 = cnt_at(PLAN["jseg"], a, b), R("B1", L + a, L + b)
@@ -640,14 +713,17 @@ def rank_program(g, core, T, topo):
             tt(u0, tot, R("FL", a, b), A.subtract)
             tt(u0, u0, R("GG", a, b), A.is_le)
             tt(R("KEY", a, b), u0, R("FL", a, b), A.mult)
+            mm(R("B7", L + a, L + b), [(R("BOF"), R("KEY", a, b))])
+            act(R("RF", a, b), R("B7", L + a, L + b), AF.Sign, acc=col(12 + 2 * i))
+            if i and not last:
+                act(col(13 + 2 * i), col(12 + 2 * i), AF.Identity, bias=col(11 + 2 * i) if i > 1 else col(12))
             mm(R("B5", L + a, L + b), [(IDN, R("QJ", a, b)), (R("NI"), R("EE", a, b)), (R("R64"), R("GJ" + s, a, b)),
-                                       (R("NBOF"), R("KEY", a, b))])
+                                       (R("NI64"), R("RF", a, b)) if a else (R("NBOF"), R("KEY", a, b))])
             if PLAN["jd"][i] == "s":
                 act(R("DJ", a, b), R("B5", L + a, L + b), AF.Relu)
             else:
                 ts(R("DJ", a, b), R("B5", L + a, L + b), 0.0, A.max)
             due("jw%d" % a, done[a] + DUE["jw"])
-            mm(R("B7", L + a, L + b), [(R("BOF"), R("KEY", a, b))])
             ts(R("VS" + s, a + b, 2 * b), R("B7", L + a, L + b), 0.0, A.is_equal, 2048.0, A.add)
             pm, w = R("B0", a, b), R("B0", L + a, L + b)
             vtr(R("KEYT", a, b), R("KEY", a, b))
@@ -665,13 +741,9 @@ def rank_program(g, core, T, topo):
             due("ja%d" % a, done[a] + DUE["ja"] + EST["hop"])
 
         def j_amounts(i, a, b):
-            count, hz = col(12 + 2 * i), R("B6", L + a, L + b)
-            act(R("RF", a, b), R("B7", L + a, L + b), AF.Sign, acc=count)
-            if i and not last:
-                act(col(13 + 2 * i), count, AF.Identity, bias=col(11 + 2 * i) if i > 1 else col(12))
-                count = col(13 + 2 * i)
+            count, hz = col(11 + 2 * len(PLAN["jseg"])), R("B6", L + a, L + b)
             mm(hz, [(R("BO"), R("C32", a, b)), (IDN, R(zj, a, b)), (R("I512"), R("RF", a, b)), (IDN, R("YM", a, b))])
-            act(R("FM", a, b), hz, AF.Identity, bias=MAGIC - 256.0, scale=0.5)
+            act(R("FM", a, b), hz, AF.Identity, bias=MAGIC - 256.0 + SH / 2, scale=0.5)
             act(R("HF", a, b), R("FM", a, b), AF.Identity, bias=-MAGIC)
             mm(R("B5", a, b), [(IDN, R(zj, a, b)), (R("IN256"), R("RF", a, b))])
             tt(R("ZO" + s, a, b), R("B5", a, b), R("HF", a, b), A.max)
@@ -689,13 +761,13 @@ def rank_program(g, core, T, topo):
                     act(R("YM", a, b), ind(XW if e == "m" else R(xb, L, L + W), R("OY", a // 16, b // 16)), AF.Identity)
 
         step[0] = "j"
-        done = gather(XW, lambda a, b: R("TJ" + s, a, b), PLAN["jgat"], -128.0, "jg", tj)
+        done = gather(XW, lambda a, b: R("TJ" + s, a, b), PLAN["jgat"], ("VF", "DX", A.max), "jg", tj)
         act(R("GG"), R("GJ" + s), AF.Identity, scale=GC)
         act(R("OLD"), ind(XT, R("OJ" + s)), AF.Identity)
         mm(R("B7", 0, L), [(IDN, R("QJ")), (IDN, R("OLD"))])
-        act(R("EE"), R("B7", 0, L), AF.Relu, bias=-191.0)
-        for a, b in PLAN["jchk"]:
-            j_cmp(a, b)
+        act(R("EE"), R("B7", 0, L), AF.Relu, bias=SH - 191.0)
+        for a, b, e in PLAN.get("jchk") or PLAN["jgat"]:
+            j_cmp(a, b, e)
         for i, ((a, b), sem) in enumerate(zip(PLAN["jseg"], VSEM)):
             j_verdict(i, a, b, sem + s)
         y_m("m")
@@ -704,8 +776,14 @@ def rank_program(g, core, T, topo):
         y_m("c")
         for i, (a, b, e) in enumerate(PLAN["zseg"]):
             j_amounts(i, a, b)
-        if last:
+        if last and not SH:
             dma("y", T.ysect[:], T[xa][:, L:L + W], "ox", 16, [], [XW, R("VH" + s, 0, 2)], 1024)
+        elif last:
+            for a, b, e in PLAN["more"]:
+                moved(e, R("ST", a, b), R(xa, L + a, L + b), 128.0)
+            for h in range(2):
+                a, b = h * W // 2, (h + 1) * W // 2
+                dma("y", T.ysect[:, a:b], T.ST[:, a:b], "ox", 32, [], [R("ST", a, b), R("VH" + s, 0, 2)], 512 * (h + 1))
         else:
             mm(R("B7", 0, L), [(IDN, R("OLD")), (R("NI"), R("EE"))])
             act(R("U1"), R("B7", 0, L), AF.Identity)
@@ -730,22 +808,22 @@ def rank_program(g, core, T, topo):
                 flags = [R("VJ", k * L + a, k * L + b) for k in range(16)]
                 for k in range(16):
                     tt(flags[k], R("XG", 16 * a + k, 16 * b, 16), R("B2", a, b), A.is_gt)
-                    in_turn("home")
+                    in_turn("home", k)
             mm(cnt_at(PLAN["hseg"], a, b),
                [(R("IN32"), R("GH" + s, a, b)), (R("IP32"), R("PH", *aoff(a, b)))]
                + [(LK[k], flags[k]) for k in range(16)])
 
         def h_new(i, a, b, sem):
-            u, dif = R("B1", L + a, L + b), R("B5" if i % 2 else "B6", a, b)
-            mm(dif, [(IDN, R("PH", *voff(a, b))), (R("NI"), R("TCH", a, b))])
+            u, bank, lo = R("B1", L + a, L + b), "B5" if i % 2 else "B6", 2 * a % L
+            hi = lo + 2 * (b - a)
+            mm(R(bank, lo, hi, 2), [(IDN, R("PH", *voff(a, b))), (R("NI"), R("TCH", a, b))])
             tt(u, EF(a, b), R("PH", *aoff(a, b)), A.mult)
-            tt(R("BASE", a, b), u, R("TCH", a, b), A.add)
+            tt(R(bank, lo + 1, hi, 2), u, R("TCH", a, b), A.add)
             if PLAN["nl"][i] == "s":
                 act(R("NL", a, b), cnt_at(PLAN["hseg"], a, b), AF.Sigmoid, bias=SBH, scale=-256.0)
             else:
                 ts(R("NL", a, b), cnt_at(PLAN["hseg"], a, b), parity(zh), A.subtract, 229.0, A.is_lt)
-            tt(u, dif, R("NL", a, b), A.mult)
-            tt(R("TCH", a, b), u, R("BASE", a, b), A.add)
+            scan(R("TCHX", 2 * a, 2 * b), R("NLX", 2 * a, 2 * b), R(bank, lo, hi), A.mult, A.add)
             if last:
                 ts(R("TF", a, b), R("TCH", a, b), 2048.0, A.add)
                 dma("y", T.ytraj[:, a:b], T.TF[:, a:b], "ot", 16 * len(PLAN["hseg"]), [], [R("TF", a, b)], 64)
@@ -757,10 +835,10 @@ def rank_program(g, core, T, topo):
                 due("hn%d" % a, done[a] + DUE["hn"] + EST["hop"])
 
         step[0] = "h"
-        done = gather(XW, lambda a, b: R("VH" + s, *voff(a, b)), PLAN["hgat"], 0.0, "hg", th)
+        done = gather(XW, lambda a, b: R("VH" + s, *voff(a, b)), hgat, ("SF", "DH", A.is_gt), "hg", th)
         for a, b in PLAN["jseg"]:
             ts(R("PH", 2 * a, 2 * b), R("VH" + s, 2 * a, 2 * b), -2048.0, A.add)
-        for a, b, e in PLAN["hgat"]:
+        for a, b, e in hgat:
             h_cmp(a, b, e)
         if last:
             dma("s", T.yamt[:], R("ZH" + s, 0, L)[0], "oz", 16, [], [R("ZH" + s, 0, L)], 64)

@@ -6,10 +6,11 @@ W, L, Q, RO = 4096, 256, 1024, 3
 BF, F32, F16, I32, U16 = "bfloat16", "float32", "float16", "int32", "uint16"
 MAGIC = 12582912.0
 BIG = 1048576.0
-EST = {"cyc": 0.0009, "gat": 1.56, "sca": 3.8, "pe": 0.8, "wait": 0.12, "hop": 3.0, "issue": 0.4, "dma": 2.0,
-       "bw": 40e3, "rows": 0.5}
-SPREAD = [{}, {"gat": 1.15, "sca": 2.5, "hop": 3.5, "wait": 0.07, "pe": 1.0},
-          {"gat": 1.95, "sca": 5.0, "hop": 2.5, "pe": 0.55}, {"hop": 4.5, "wait": 0.2, "issue": 0.7, "pe": 0.55}]
+EST = {"cyc": 0.00087, "gat": 1.56, "sca": 3.8, "pe": 0.8, "wait": 0.17, "hop": 3.6, "issue": 0.5, "dma": 2.0,
+       "bw": 50e3, "rows": 0.5}
+SPREAD = [{}, {"gat": 1.15, "sca": 2.5, "hop": 4.0, "wait": 0.12, "pe": 1.0, "cyc": 0.001},
+          {"gat": 1.95, "sca": 5.0, "hop": 2.8, "wait": 0.1, "pe": 0.55, "cyc": 0.0011},
+          {"hop": 4.8, "wait": 0.25, "issue": 0.8, "pe": 0.55}]
 S2 = [(128, 256), (0, 128)]
 S4 = [(192, 256), (128, 192), (64, 128), (0, 64)]
 S5 = [(192, 256), (128, 192), (64, 128), (32, 64), (0, 32)]
@@ -29,16 +30,18 @@ PLAN = {"cgat0": GV, "cgat": by(S5, "sssss"), "jgat": GV, "jchk": by(S4, "ssss")
 DUE = {"first": 8.0, "cut": 10.0, "judge": 8.0, "home": 8.0, "cg": 7.0, "jg": 6.5, "hg": 6.5,
        "cq": 3.0, "ja": 4.0, "jw": 2.0, "jz": 4.5, "hn": 2.5}
 PLAN["hgat2"] = by(S4, "fsfs")
-PLAN["cgat"] = by(S5, "sssvs")
-PLAN["cgat0"] = GV[:4] + by(S5[3:], "vs")
+PLAN["cgat"] = by(S5, "sssfs")
+PLAN["cgat0"] = GV[:4] + by(S5[3:], "fs")
+PLAN["gseg"] = [(64, 256), (0, 64)]
 PLAN["grain"] = 1
+PLAN["split"] = 6
 PLAN["join"] = 2
 PLAN["keep0"] = "s"
 SEARCH = {"seed": 1, "many": 1, "pull": 0.6, "far": 2.0, "mix": 0.2, "warm": 0.4, "tries": 3, "dues": 1200, "moves": 9000,
           "heat": 0.1}
 FOUND = []
 MATS = ("BO", "NBO", "R15", "E15", "R64", "NR64", "DF", "NI", "I5", "I4", "IK", "IN32", "IP32", "NB8K", "I64", "I512",
-        "IN256", "NI64", "MJ")
+        "IN256", "NI64", "MJ", "MD")
 ROWS = ("DM", "NDM", "NDM2", "RST", "CSP", "SD", "ONE", "C32", "CE")
 
 
@@ -49,8 +52,8 @@ def _scratch():
         s[name] = ("sbuf", [128, n], dt)
     sb("X", W + L, BF); sb("X2", W + L, BF); sb("MV", W, I32); sb("XG", W, BF); sb("ST", W, BF); sb("VJ", W, F16)
     sb("D1", W, BF); sb("DH", W, BF); sb("SF", W, BF); sb("EQ", 16 * L, BF); sb("T32", L, I32); sb("CAPI", 8, I32)
-    sb("Z0", 272, BF); sb("ZJ0", 272, BF); sb("VF", W, F16); sb("DX", W, F16); sb("TJF", L, F16)
-    sb("XL", 2048, BF); sb("JS", 64, F32); sb("J16", 64, F16)
+    sb("Z0", 272, BF); sb("ZJ0", 272, BF); sb("TJF", L, F16); sb("KEEP", 1024, BF)
+    sb("XL", 1024, BF); sb("JS", 64, F32); sb("J16", 64, F16)
     for r in range(RO):
         for nm in ("ZC", "ZO", "ZH"):
             sb(nm + str(r), 272, BF)
@@ -85,8 +88,8 @@ def _scratch():
 
 SCRATCH = _scratch()
 TSEM, VSEM, ZSEM = (tuple(x + y for y in "abcde") for x in "tvz")
-SEMAPHORES = (["sv", "ss", "sp", "sg", "sent", "lt", "lz", "lc", "lxa", "lxb", "lm", "ox", "oz", "ot", "zj"]
-              + [nm + str(r) for r in range(RO) for nm in TSEM + VSEM + ZSEM + ("tj", "gj", "gh", "oj", "cx", "zh")])
+SEMAPHORES = (["sv", "ss", "sp", "sg", "sent", "lt", "lu", "lz", "lc", "lxa", "lxb", "lm", "ox", "oz", "ot", "zj"]
+              + [nm + str(r) for r in range(RO) for nm in TSEM + VSEM + ZSEM + ("tj", "gj", "gk", "gh", "oj", "cx", "zh")])
 
 
 def times(op, est):
@@ -135,7 +138,7 @@ def jobs_of(ops, est):
     tm = [times(op, est) for op in ops]
     head, off, length = [], [], {}
     for i, op in enumerate(ops):
-        h = head[-1] if op["grp"] and not op["grp"][0] or op["join"] else i
+        h = head[-1] if op["join"] else i
         head.append(h)
         off.append(length.get(h, 0.0))
         length[h] = off[-1] + tm[i][0]
@@ -374,7 +377,7 @@ def rank_program(g, core, T, topo):
                 rd.append(x[4][1:3])
         ops.append({"eng": eng, "fn": fn, "rd": rd, "wr": wr, "sem": sem, "need": False, "ck": ck, "grp": grp,
                     "after": after, "due": None, "join": False,
-                    "kind": (step[0], eng, (wr or rd)[0][0][:1 + (wr or rd)[0][0][1:2].isalpha()],
+                    "kind": (step[0], eng, eng == "p" and rd[1][1].bit_length(), (wr or rd)[0][0][:1 + (wr or rd)[0][0][1:2].isalpha()],
                              (wr or rd)[0][1].bit_length() // PLAN["grain"])})
         return len(ops) - 1
 
@@ -446,13 +449,18 @@ def rank_program(g, core, T, topo):
             ts(o, a, c, A.add)
 
     def mm(o, terms, after=None):
+        counts = o[1] in ("B3", "B4")
         for i, t in enumerate(terms):
             lt, rh = t[:2]
             oo = t[2] if len(t) > 2 else o
             first, end = i == 0, i == len(terms) - 1
             add("p", lambda lt=lt, rh=rh, oo=oo, first=first, end=end: g.tensor.matmul(oo[0], lt[0], rh[0], first, end),
                 [oo], [lt, rh], ("pe", max(64, rh[3]) * (4 if SCRATCH[rh[1]][2] == F32 else 1)),
-                grp=(first, end), after=(after if first else len(ops) - 1))
+                after=(after if first else len(ops) - 1))
+            ops[-1]["join"] = i % (PLAN["split"] if counts else 99) > 0
+        if counts:
+            ops[-len(terms)]["after"] = turns.get(o[1])
+            turns[o[1]] = len(ops) - 1
         return len(ops) - 1
 
     def iota(o, pat, base, cm, isint=False):
@@ -486,7 +494,8 @@ def rank_program(g, core, T, topo):
     LK = [R("WK", 15 - k, 143 - k) for k in range(16)]
 
     SH = 128.0 if PLAN["less"] else 0.0
-    dma("y", T.T32[:], T.traj[:], "lt", 16, [R("T32")], [], 128)
+    for (a, b), sem in zip(PLAN["seg0"], ("lt", "lu")):
+        dma("y", T.T32[:, a:b], T.traj[:, a:b], sem, 16, [R("T32", a, b)], [], 64)
     dma("s", R("Z0", 0, L)[0], T.amt[:], "lz", 16, [R("Z0", 0, L)], [], 64)
     dma("y", T.CAPI[:, 0:1], T.cap[:], "lc", 16, [R("CAPI", 0, 1)], [], 1)
     for h, sem in enumerate(("lxa", "lxb")):
@@ -506,9 +515,9 @@ def rank_program(g, core, T, topo):
     ts(R("COLI", 1, 2), R("COLI", 0, 1), 15, A.bitwise_and)
     ts(R("COLI", 2, 3), R("COLI", 0, 1), 112, A.bitwise_and)
     ts(R("COLI", 3, 4), R("COLI", 0, 1), 16, A.bitwise_and)
-    cp(R("TU0"), R("T32"))
     opening = []
     for i, (a, b) in enumerate(PLAN["seg0"]):
+        cp(R("TU0", a, b), R("T32", a, b))
         opening += [(R("TU0", a, b), R("TC0", a, b), nxt1, prv1, TSEM[i] + "0"),
                     (R("Z0", a or -16, b), R("ZC0", a or -16, b), nxt1, prv1, ZSEM[i] + "0")]
     opening += [(R("Z0"), R("ZJ0"), nxt2, prv2, "zj"), (R("TU0"), R("TJ0"), nxt2, prv2, "tj0")]
@@ -518,7 +527,6 @@ def rank_program(g, core, T, topo):
     cp(PMC, R("COLI", 1, 2)); cp(PG, R("COLI", 2, 3))
     ts(H0, R("COLI", 3, 4), 0.0, A.is_equal); ts(H1, R("COLI", 3, 4), 0.0, A.not_equal)
     ts(NE15, R("COLI", 1, 2), 15.0, A.not_equal); ts(EQ15, R("COLI", 1, 2), 15.0, A.is_equal)
-    ts(col(21), R("COLI", 1, 2), 0.0, A.is_equal, 1025.0, A.mult); tt(col(20), col(21), NE15, A.subtract)
     ts(col(22), R("COLI", 1, 2), 1.0, A.is_equal, 663552.0, A.mult); tt(col(23), col(22), EQ15, A.add)
     act(R("CE"), R("ONE"), AF.Identity, scale=col(23))
     ts(CAPF, R("CAPI", 0, 1), -SH, A.add); ts(C255, R("CAPI", 0, 1), -1.0, A.mult, 255.0, A.add)
@@ -545,19 +553,19 @@ def rank_program(g, core, T, topo):
     act(R("NDM"), R("DM"), AF.Identity, bias=-16384.0, scale=16384.0)
     act(R("NDM2"), R("DM"), AF.Identity, bias=-14080.0, scale=16384.0)
 
-    if PLAN["keep0"]:
-        mset(R("XL", 1024, 2048), 0.0)
-        iota(R("JS"), [[16, 64]], 15, 0)
-        cp(R("J16"), R("JS"))
-        ts(R("MJ"), R("BO"), col(20), A.mult)
-
-    def held_in(name, a):
-        return "XL" if PLAN["keep0"] and name == "cg" and a < PLAN["cseg"][-1][1] else "XG"
+    iota(R("JS"), [[16, 64]], 15, 0)
+    cp(R("J16"), R("JS"))
+    ts(R("MJ"), R("BO"), NE15, A.mult, -1.0, A.mult)
+    for a in range(0, 1024, L):
+        ts(R("KEEP", a, a + L), R("RST"), 0.0, A.is_equal)
+    ts(col(20), R("COLI", 1, 2), 0.0, A.is_equal); tt(col(21), col(20), EQ15, A.subtract)
+    ts(R("MD"), R("IW", 31, 159), EQ15, A.mult); ts(R("EQ", 0, 128), IDN, col(21), A.mult)
+    tt(R("MD"), R("MD"), R("DF"), A.subtract); tt(R("MD"), R("MD"), R("EQ", 0, 128), A.add)
 
     def gather(win, offs, parts, fused, name, t0):
         clock, done = t0, {}
         for a, b, e in parts:
-            o, src = R(held_in(name, a), 16 * a, 16 * b), ind(win, offs(a, b))
+            o, src = R("XG", 16 * a, 16 * b), ind(win, offs(a, b))
             if e == "f":
                 tt(R(fused[0], 16 * a, 16 * b), src, R(fused[1], 16 * a, 16 * b), fused[2])
             else:
@@ -598,18 +606,22 @@ def rank_program(g, core, T, topo):
         th = tj + DUE["judge"]
 
         def c_scan(a, b):
-            xg = held_in("cg", a)
-            x0 = R(xg, 16 * a, 16 * b, 16)
-            if xg == "XL":
-                copy_on(PLAN["keep0"], R("XL", 1025 + 16 * a, 1025 + 16 * b - 15, 16), x0)
+            if (a, b) in flagged:
+                scan(R("ST", 16 * a, 16 * b), R("KEEP", 0, 16 * (b - a)), R("XG", 16 * a, 16 * b), A.mult, A.max)
+                return
+            x0 = R("XG", 16 * a, 16 * b, 16)
             tt(x0, x0, R("B0", a, b), A.max)
             tt(R("D1", 16 * a, 16 * b, 16), x0, R("B0", L + a, L + b), A.min)
-            scan(R("ST", 16 * a, 16 * b), R(xg, 16 * a, 16 * b), R("D1", 16 * a, 16 * b), A.max, A.min)
+            scan(R("ST", 16 * a, 16 * b), R("XG", 16 * a, 16 * b), R("D1", 16 * a, 16 * b), A.max, A.min)
 
         def c_place(i, a, b):
             u, v, o = a // 16, b // 16, 8 * (len(PLAN["cseg"]) - i)
-            mm(cnt_at(PLAN["cseg"], a, b),
-               [(R("NBO"), R("THR1", a, b))] + [(LK[k], R("ST", 16 * a + k, 16 * b, 16)) for k in range(16)])
+            less = [(R("NBO"), R("THR1", a, b))]
+            for lo, hi in flagged:
+                if a <= lo < b:
+                    less += [(R("BO"), R("THR1", lo, hi), cnt_at(PLAN["cseg"], lo, hi)),
+                             (R("NBO"), R("ONE", lo, hi), cnt_at(PLAN["cseg"], lo, hi))]
+            mm(cnt_at(PLAN["cseg"], a, b), less + [(LK[k], R("ST", 16 * a + k, 16 * b, 16)) for k in range(16)])
             ts(R("TCC", a, b), R("TC" + s, a, b), -2048.0, A.add)
             if PLAN["ge"][i] == "s":
                 act(R("GE" + s, a, b), cnt_at(PLAN["cseg"], a, b), AF.Sigmoid, bias=SBC, scale=256.0)
@@ -635,18 +647,23 @@ def rank_program(g, core, T, topo):
             scan(R("NS", a, b), R("CSP", a, b), R("B7", a, b), A.min, A.max, BIG)
             cp(R("OS" + s, u, v), R("NS", a + 15, b, 16))
             due("cq%d" % a, done[a] + DUE["cq"])
-            if a == 0 and PLAN["keep0"]:
+            if a == 0:
                 mm(R("B5", L, L + b), [(IDN, R("J16", 0, b)), (IDN, R("NDM", 0, b)), (R("MJ"), R("GE" + s, 0, b))])
                 scan(R("JS", 0, b), R("RST", 0, b), R("B5", L, L + b), A.add, A.max, -BIG)
                 cp(R("OR", u, v), R("JS", 15, b, 16))
-                tt(R("MN", a, b), ind(R("XL"), R("OR", u, v)), R("NQC", a, b), A.min)
-                return
-            if a == 0:
-                ts(R("OR", u, v), R("SCB", o + a + 16, o + b + 1, 16), 2304.0, A.add)
-            tt(R("MN", a, b), ind(XT, R("OR" if a == 0 else "OS" + s, u, v)), R("NQC", a, b), A.min)
+                tt(R("MN", a, b), ind(R("XL", 0, 16 * b), R("OR", u, v)), R("NQC", a, b), A.min)
+            else:
+                tt(R("MN", a, b), ind(XT, R("OS" + s, u, v)), R("NQC", a, b), A.min)
 
         step[0] = "c"
-        done = gather(XW, lambda a, b: R("TC" + s, a, b), PLAN["cgat0" if r == 0 else "cgat"], None, "cg", tc)
+        cgat = PLAN["cgat0" if r == 0 else "cgat"]
+        flagged = [(a, b) for a, b, e in cgat if e == "f"]
+        for a, b in flagged:
+            act(R("D1", 16 * a, 16 * b, 16), R("THR1", a, b), AF.Identity)
+        done = gather(XW, lambda a, b: R("TC" + s, a, b), cgat, ("XG", "D1", A.is_ge), "cg", tc)
+        b = PLAN["cseg"][-1][1]
+        act(R("XL", 0, 16 * b), ind(XW, R("TC" + s, 0, b)), AF.Identity)
+        in_turn("gathers")
         act(R("QB"), R(zc, 0, L), AF.Identity, bias=159.625, scale=0.25)
         act(R("NQC"), R("QB"), AF.Identity, bias=415.0 - SH, scale=-1.0)
         act(R("QC"), R("QB"), AF.Identity, bias=-160.0)
@@ -656,7 +673,8 @@ def rank_program(g, core, T, topo):
             c_place(i, a, b)
         for a, b in PLAN["cseg"]:
             tt(ind(XT, R("OS" + s, a // 16, b // 16)), R("MN", a, b), R("QC", a, b), A.add)
-        send(R("GE" + s), R("GJ" + s), nxt1, prv1, "gj" + s)
+        for (a, b), sem in zip(PLAN["gseg"], ("gj", "gk")):
+            send(R("GE" + s, a, b), R("GJ" + s, a, b), nxt1, prv1, sem + s)
         send(R("OS" + s), R("OJ" + s), nxt1, prv1, "oj" + s)
         send(R("GE" + s), R("GH" + s), prv1, nxt1, "gh" + s)
         dma("y", T[xb][:], T[xa][:], "cx" + s, 16, [R(xb)], [XT], 1024)
@@ -665,8 +683,9 @@ def rank_program(g, core, T, topo):
                 dma("s", T.MV[:, j * Q:(j + 1) * Q], T.mv[:], "lm", 64, [R("MV", j * Q, (j + 1) * Q)], [R("ZJ0")],
                     512 * (j + 1))
         hgat = PLAN["hgat2" if last else "hgat"]
-        ts(R("TT0"), R("TJ" + s), 2.0 ** -17, A.mult)
-        vtr(R("TTS"), R("TT0"))
+        ts(R("TJF"), R("TJ" + s), -2048.0, A.add)
+        mm(R("B1", L, 2 * L), [(R("MD"), R("TJF"))])
+        vtr(R("TTS"), R("B1", L, 2 * L))
         act(GC, parity(zj), AF.Identity, bias=1.6875 - 16.0, scale=-1.0 / 16)
         act(R("RJ"), R(zj, 0, L), AF.Relu, bias=C255)
         act(R("B1", 0, L), R("RJ"), AF.Identity, bias=127.0625, scale=-1.0)
@@ -685,25 +704,12 @@ def rank_program(g, core, T, topo):
             act(R("THH", a, b), R("RH", a, b), AF.Identity, bias=255.0 - SH, scale=-1.0)
             for k in range(16):
                 copy_on(PLAN["hexp"][k % len(PLAN["hexp"])], R("DH", 16 * a + k, 16 * b, 16), R("THH", a, b))
-        for a, b in PLAN.get("jspread") or [x[:2] for x in PLAN["jgat"] if x[2] == "f"]:
-            ts(R("TJF", a, b), R("RJ", a, b), -1.0, A.mult, 127.0625, A.add)
-            for k in range(0 if SH or r == 0 else 1, 16):
-                copy_on(PLAN["jexp"][k % len(PLAN["jexp"])], R("DX", 16 * a + k, 16 * b, 16), R("TJF", a, b))
 
         def j_cmp(a, b, e):
-            if e == "f":
-                tops = [R("VF", 16 * a + k, 16 * b, 16) for k in range(16)]
-            elif e == "y":
-                y0 = R("XG", 16 * a, 16 * b, 16)
-                tops = [R("VJ", a, b)] + [R("VF", 16 * a + k, 16 * b, 16) for k in range(1, 16)]
-                tt(tops[0], y0, R("B1", a, b), A.max)
-                mset(y0, 512.0)
-                scan(R("VF", 16 * a, 16 * b), R("DX", 16 * a, 16 * b), R("XG", 16 * a, 16 * b), A.min, A.max)
-            else:
-                tops = [R("VJ", k * L + a, k * L + b) for k in range(16)]
-                for k in range(16):
-                    tt(tops[k], R("XG", 16 * a + k, 16 * b, 16), R("B1", a, b), A.max)
-                    in_turn("judge", k)
+            tops = [R("VJ", k * L + a, k * L + b) for k in range(16)]
+            for k in range(16):
+                tt(tops[k], R("XG", 16 * a + k, 16 * b, 16), R("B1", a, b), A.max)
+                in_turn("judge", k)
             mm(cnt_at(PLAN["jseg"], a, b), [(R("BO"), R("RJB", a, b))] + [(LK[k], tops[k]) for k in range(16)])
 
         def j_verdict(i, a, b, sem):
@@ -728,10 +734,9 @@ def rank_program(g, core, T, topo):
             pm, w = R("B0", a, b), R("B0", L + a, L + b)
             vtr(R("KEYT", a, b), R("KEY", a, b))
             scan(pm, R("SD", a, b), R("KEYT", a, b), A.add, A.max)
-            tt(w, pm, R("KEYT", a, b), A.subtract)
-            tt(R("DD", a, b), R("TTS", a, b), w, A.subtract)
-            scan(R("SC2", a, b), w, R("DD", a, b), A.min, A.max)
-            ts(R("RS", u, v), R("SC2", a + 15, b, 16), 2.0 ** 17, A.mult, -2048.0, A.add)
+            tt(w, pm, R("KEYT", a, b), A.is_gt)
+            scan(R("SC2", a, b), R("TTS", a, b), w, A.add, A.mult)
+            tt(R("RS", u, v), R("SC2", a + 15, b, 16), R("TTS", a, b, 16), A.add)
             for hp in range(2):
                 mm(R("B6", u + hp, v, 2),
                    [(R("IW%d" % hp, 16 - 16 * (h - hp), 144 - 16 * (h - hp)), R("RS", u + h, v, 2)) for h in range(2)])
@@ -762,7 +767,8 @@ def rank_program(g, core, T, topo):
 
         step[0] = "j"
         done = gather(XW, lambda a, b: R("TJ" + s, a, b), PLAN["jgat"], ("VF", "DX", A.max), "jg", tj)
-        act(R("GG"), R("GJ" + s), AF.Identity, scale=GC)
+        for a, b in PLAN["gseg"]:
+            act(R("GG", a, b), R("GJ" + s, a, b), AF.Identity, scale=GC)
         act(R("OLD"), ind(XT, R("OJ" + s)), AF.Identity)
         mm(R("B7", 0, L), [(IDN, R("QJ")), (IDN, R("OLD"))])
         act(R("EE"), R("B7", 0, L), AF.Relu, bias=SH - 191.0)

import math
import numpy as np
from concourse.mybir import AluOpType as A, ActivationFunctionType as AF

W, L, Q, RO = 4096, 256, 1024, 3
BF, F32, F16, I32, U16 = "bfloat16", "float32", "float16", "int32", "uint16"
MAGIC = 12582912.0
BIG = 1048576.0
EST = {"cyc": 0.00087, "gat": 1.56, "sca": 3.8, "pe": 0.8, "wait": 0.17, "hop": 3.6, "issue": 0.5, "dma": 2.0,
       "bw": 50e3, "rows": 0.5}
SPREAD = [{}, {"gat": 1.15, "sca": 2.5, "hop": 4.0, "wait": 0.12, "pe": 1.0, "cyc": 0.001},
          {"gat": 1.95, "sca": 5.0, "hop": 2.8, "wait": 0.1, "pe": 0.55, "cyc": 0.0011},
          {"hop": 4.8, "wait": 0.25, "issue": 0.8, "pe": 0.55}]
S2 = [(128, 256), (0, 128)]
S4 = [(192, 256), (128, 192), (64, 128), (0, 64)]
S5 = [(192, 256), (128, 192), (64, 128), (32, 64), (0, 32)]


def by(segs, engines):
    return [(a, b, e) for (a, b), e in zip(segs, engines)]


GV = [(224, 256, "s"), (192, 224, "v")] + by(S5[1:], "ssss")
E5 = [(224, 256), (160, 224), (96, 160), (32, 96), (0, 32)]
Q4 = [(0, 1024), (1024, 2048), (2048, 3072), (3072, 4096)]
PLAN = {"cgat0": GV, "cgat": by(S5, "sssss"), "jgat": GV, "jchk": by(S4, "ssss"), "hgat": by(S4, "fsss"), "cchk": S5,
        "cseg": S4, "jseg": S4, "hseg": S4, "zseg": by(S2, "mc"),
        "cexp0": by(S2, "vv"), "cexp": by(S2, "vv"), "hexp": "g", "jexp": "g", "seg0": S2,
        "ge": "vvvvv", "nl": "vvvvv", "jd": "sssss", "less": [], "more": by(Q4, "svss")}
DUE = {"first": 8.0, "cut": 10.0, "judge": 8.0, "home": 8.0, "cg": 7.0, "jg": 6.5, "hg": 6.5,
       "cq": 3.0, "ja": 4.0, "jw": 2.0, "jz": 4.5, "hn": 2.5}
PLAN["hgat2"] = by(S4, "fsfs")
PLAN["cgat"] = by(S5, "sssfs")
PLAN["cgat0"] = GV[:4] + by(S5[3:], "fs")
PLAN["gseg"] = [(64, 256), (0, 64)]
PLAN["grain"] = 1
PLAN["split"] = 6
PLAN["join"] = 2
PLAN["keep0"] = "s"
SEARCH = {"seed": 1, "many": 1, "pull": 0.6, "far": 2.0, "mix": 0.2, "warm": 0.4, "tries": 3, "dues": 1200, "moves": 9000,
          "heat": 0.1}
FOUND = []
MATS = ("BO", "NBO", "R15", "E15", "R64", "NR64", "DF", "NI", "I5", "I4", "IK", "IN32", "IP32", "NB8K", "I64", "I512",
        "IN256", "NI64", "MJ", "MD")
ROWS = ("DM", "NDM", "NDM2", "RST", "CSP", "SD", "ONE", "C32", "CE")


def _scratch():
    s = {}

    def sb(name, n, dt):
        s[name] = ("sbuf", [128, n], dt)
    sb("X", W + L, BF); sb("X2", W + L, BF); sb("MV", W, I32); sb("XG", W, BF); sb("ST", W, BF); sb("VJ", W, F16)
    sb("D1", W, BF); sb("DH", W, BF); sb("SF", W, BF); sb("EQ", 16 * L, BF); sb("T32", L, I32); sb("CAPI", 8, I32)
    sb("Z0", 272, BF); sb("ZJ0", 272, BF); sb("TJF", L, F16); sb("KEEP", 1024, BF)
    sb("XL", 1024, BF); sb("JS", 64, F32); sb("J16", 64, F16)
    for r in range(RO):
        for nm in ("ZC", "ZO", "ZH"):
            sb(nm + str(r), 272, BF)
        for nm in ("TU", "TC", "TJ"):
            sb(nm + str(r), L, U16)
        for nm in ("VS", "VH"):
            sb(nm + str(r), 2 * L, U16)
        for nm in ("GE", "GJ", "GH"):
            sb(nm + str(r), L, BF)
        for nm in ("OS", "OJ"):
            sb(nm + str(r), 16, U16)
    sb("OY", 16, U16); sb("OR", 16, U16); sb("RS", 16, F16); sb("PH", 2 * L, F16)
    sb("TCHX", 2 * L, F16); sb("NLX", 2 * L, BF); sb("NBOF", 128, F32)
    for nm in ("TCC", "PROD"):
        sb(nm, L, F16)
    for nm in ("TF", "RR", "RJ", "RH", "PM", "TT0", "TTS", "KEY", "KEYT", "DD", "SC2", "NS", "FM"):
        sb(nm, L, F32)
    sb("SCB", 320, F32); sb("FL", L, I32)
    for nm in ("THR1", "THH", "QB", "QB2", "QC", "NQC", "QJ", "QH", "GG", "MN", "OLD", "EE", "U1", "DJ", "RU", "YM",
               "RF", "RJB", "HF"):
        sb(nm, L, BF)
    sb("IO1", 160, F32)
    for nm in ("WK", "IW", "IW0", "IW1"):
        sb(nm, 160, BF)
    sb("CM", 128 * len(MATS), BF); sb("CR", L * len(ROWS), BF)
    sb("BOF", 128, F32); sb("COL", 24, F32); sb("COLB", 16, BF)
    sb("COLI", 8, I32)
    for b in range(8):
        s["B" + str(b)] = ("psum", [128, 512], F32)
    return s


SCRATCH = _scratch()
TSEM, VSEM, ZSEM = (tuple(x + y for y in "abcde") for x in "tvz")
SEMAPHORES = (["sv", "ss", "sp", "sg", "sent", "lt", "lu", "lz", "lc", "lxa", "lxb", "lm", "ox", "oz", "ot", "zj"]
              + [nm + str(r) for r in range(RO) for nm in TSEM + VSEM + ZSEM + ("tj", "gj", "gk", "gh", "oj", "cx", "zh")])


def times(op, est):
    kind, n = op["ck"]
    if kind in ("gat", "sca"):
        return 0.05 + n * est[kind] * est["cyc"], 0.0
    if kind == "pe":
        return n * est["pe"] * est["cyc"], 0.0
    if kind == "pool":
        return 0.17 + 2 * n * est["cyc"], 0.0
    if kind == "dma":
        return 0.1, est["dma"] + n / 280.0
    if kind == "send":
        return est["issue"], est["hop"] - est["issue"] + n / est["bw"]
    return n * est["cyc"], 0.0


def link(ops):
    hist = {}
    for i, op in enumerate(ops):
        deps = set()
        for kind, views in (("r", op["rd"]), ("w", op["wr"])):
            for name, mask in views:
                for (j, kj, mj) in hist.get(name, []):
                    if mask & mj and (kind == "w" or kj == "w"):
                        deps.add(j)
        for name, mask in op["wr"]:
            hist[name] = [(j, kj, mj & ~mask) for (j, kj, mj) in hist.get(name, []) if mj & ~mask]
        for kind, views in (("r", op["rd"]), ("w", op["wr"])):
            for name, mask in views:
                hist.setdefault(name, []).append((i, kind, mask))
        op["data"] = deps
        op["pre"] = deps | ({op["after"]} if op["after"] is not None else set())
        op["banks"] = set(x[0] for x in op["rd"] + op["wr"] if SCRATCH[x[0]][0] == "psum")


def lag(ops, tm, est, j, i):
    if ops[i]["eng"] == "x":
        return tm[j][1]
    if j not in ops[i]["data"] or ops[j]["eng"] == "p" == ops[i]["eng"]:
        return 0.0
    return tm[j][1] + est["wait"]


def jobs_of(ops, est):
    tm = [times(op, est) for op in ops]
    head, off, length = [], [], {}
    for i, op in enumerate(ops):
        h = head[-1] if op["join"] else i
        head.append(h)
        off.append(length.get(h, 0.0))
        length[h] = off[-1] + tm[i][0]
    edge, banks = {h: {} for h in length}, {h: set() for h in length}
    for i, op in enumerate(ops):
        banks[head[i]] |= op["banks"]
        for j in op["pre"]:
            if head[j] != head[i]:
                d = off[j] + tm[j][0] + lag(ops, tm, est, j, i) - off[i]
                edge[head[i]][head[j]] = max(edge[head[i]].get(head[j], d), d)
    return head, {h: (ops[h]["eng"], length[h], list(edge[h].items()), sorted(banks[h]), length[h] + tm[h][1],
                      ops[h]["ck"][1] / est["bw"] + est["rows"] if ops[h]["ck"][0] == "send" else 0.0) for h in length}


def place_jobs(jobs, holds, key):
    busy, start, rank = {}, {}, {}
    for h in sorted(jobs, key=key.get):
        before = jobs[h][2]
        hold = holds[h]
        t = top = 0.0
        for j, d in before:
            if start[j] + d > t:
                t = start[j] + d
            if rank[j] > top:
                top = rank[j]
        moved = True
        while moved:
            moved = False
            for res, o, d, gap, who in hold:
                spans = busy.setdefault(res, [])
                lo = hi = len(spans)
                if lo and spans[-1][1] + gap > t + o:
                    lo = max(0, hi - 64)
                    if spans[lo][1] + gap > t + o:
                        lo = 0
                    while lo < hi:
                        mid = (lo + hi) // 2
                        if spans[mid][1] + gap <= t + o:
                            lo = mid + 1
                        else:
                            hi = mid
                    end = len(spans)
                    while lo < end and spans[lo][0] < t + o + d + gap - 1e-9:
                        if who is None or spans[lo][2] != who:
                            t, moved = spans[lo][1] + gap - o + 1e-7, len(hold) > 1
                        lo += 1
        start[h] = t
        rank[h] = max(t, top + 1e-6)
        for res, o, d, gap, who in hold:
            spans = busy[res]
            lo = len(spans)
            while lo and spans[lo - 1][0] > t + o:
                lo -= 1
            spans.insert(lo, (t + o, t + o + d, who))
    return sorted(jobs, key=rank.get)


def run_jobs(seq, jobs, wait):
    free, used, start, why, ready = {}, {}, {}, {}, {}
    wire, worst, final = 0.0, 0.0, None
    for h in seq:
        e, n, before, banks, tail, lt = jobs[h]
        t, w = 0.0, None
        for j, d in before:
            if start[j] + d > t:
                t, w = start[j] + d, j
        ready[h] = t
        if e in free and free[e][0] > t:
            t, w = free[e]
        for b in banks:
            for e2, (t2, j) in used.setdefault(b, {}).items():
                if e2 != e and t2 + wait > t:
                    t, w = t2 + wait, j
        for b in banks:
            used[b][e] = (t + n, h)
        if e != "x":
            free[e] = (t + n, h)
        if lt:
            t = max(t, wire - n)
            wire = t + n + lt
        start[h], why[h] = t, w
        if t + tail > worst:
            worst, final = t + tail, h
    return worst, why, final, start, ready


def find_order(ops):
    rng = np.random.RandomState(SEARCH["seed"])
    ests = [dict(EST, **v) for v in SPREAD]
    views = [jobs_of(ops, est)[1] for est in ests]
    head, jobs = jobs_of(ops, EST)
    dads = {h: set(j for j, d in jobs[h][2]) for h in jobs}
    sons = {h: set() for h in jobs}
    for h in jobs:
        for j in dads[h]:
            sons[j].add(h)

    holds = {h: ([] if e == "x" else [(e, 0.0, n, 0.0, None)]) + [(b, 0.0, n, EST["wait"], e) for b in banks]
             + ([("link", n, lt, 0.0, None)] if lt else []) for h, (e, n, _b, banks, _t, lt) in jobs.items()}
    backward = [(h, ops[h]["kind"], [(j, max(d, 1e-4)) for j, d in jobs[h][2]]) for h in sorted(jobs, reverse=True)]
    dues = [(head[i], op["due"]) for i, op in enumerate(ops) if op["due"]]

    def score(seq, than=None):
        got = []
        for v, (view, est) in enumerate(zip(views, ests)):
            got.append(run_jobs(seq, view, est["wait"]))
            if than and got[v][0] > than[2][v][0] + 1.5:
                return 1e9, seq, got
        return sum(x[0] for x in got), seq, got

    names = sorted(set(op["due"][0] for op in ops if op["due"]))
    kind = {h: ops[h]["kind"] for h in jobs}

    def held_up(got):
        _t, why, h, start, ready = got[rng.randint(len(got))]
        arcs = []
        while why[h] is not None:
            if why[h] not in dads[h]:
                arcs.append((why[h], h, min(start[h] - ready[h], SEARCH["far"])))
            h = why[h]
        p = np.cumsum([x[2] + 0.05 for x in arcs])
        return arcs[int(np.searchsorted(p, rng.rand() * p[-1]))]

    best = None
    for it in list(range(SEARCH["dues"] + 1)) * SEARCH["tries"]:
        if not it:
            cur, shift = None, {}
        trial = dict(shift)
        if it and rng.rand() < SEARCH["mix"]:
            nm = names[rng.randint(len(names))]
            trial[nm] = trial.get(nm, 0.0) + rng.randn()
        elif it:
            for _ in range(1 + rng.randint(SEARCH["many"])):
                v, u, late = held_up(cur[2])
                if rng.rand() < SEARCH["pull"]:
                    trial[kind[u]] = trial.get(kind[u], 0.0) - max(0.0, kept[u] - kept[v]) - rng.rand() * late
                else:
                    trial[kind[v]] = trial.get(kind[v], 0.0) + max(0.0, kept[u] - kept[v]) + rng.rand() ** 2
        key = dict.fromkeys(jobs, 1e3)
        for h, (nm, t) in dues:
            key[h] = t + trial.get(nm, 0.0)
        for h, kd, before in backward:
            t = key[h] = key[h] + trial.get(kd, 0.0)
            for j, d in before:
                if t - d < key[j]:
                    key[j] = t - d
        for h, kd, before in backward[::-1]:
            for j, d in before:
                if key[j] >= key[h]:
                    key[h] = key[j] + 1e-6
        got = score(place_jobs(jobs, holds, key), cur)
        if cur is None or got[0] <= cur[0] - SEARCH["warm"] * (1.0 - it / SEARCH["dues"]) * math.log(1.0 - rng.rand()):
            cur, shift, kept = got, trial, key
        if best is None or got[0] < best[0]:
            best = got
    now, seq, got = best
    for it in range(SEARCH["moves"]):
        v, u, _late = held_up(got)
        a, b = seq.index(v), seq.index(u)
        more = (0, 0, 3, 10, 30)[rng.randint(5)]
        if rng.rand() < 0.5:
            a, move = max(0, a - more), {u}
            for w in reversed(seq[a:b]):
                if sons[w] & move:
                    move.add(w)
            mid = [w for w in seq[a:b + 1] if w in move] + [w for w in seq[a:b + 1] if w not in move]
        else:
            b, move = min(len(seq) - 1, b + more), {v}
            for w in seq[a + 1:b + 1]:
                if dads[w] & move:
                    move.add(w)
            mid = [w for w in seq[a:b + 1] if w not in move] + [w for w in seq[a:b + 1] if w in move]
        new = score(seq[:a] + mid + seq[b + 1:])
        if new[0] <= now - SEARCH["heat"] * (1.0 - it / SEARCH["moves"]) * math.log(1.0 - rng.rand()):
            now, seq, got = new
            if now < best[0]:
                best = new
    members = {}
    for i in range(len(ops)):
        members.setdefault(head[i], []).append(i)
    order = [i for h in best[1] for i in members[h]]
    seen, turn = {}, [set() for _ in ops]
    for i in order:
        for b in ops[i]["banks"]:
            at = seen.setdefault(b, {})
            turn[i] |= set(j for e, j in at.items() if e != ops[i]["eng"])
            at[ops[i]["eng"]] = i
    return [x[0] for x in best[2]], order, turn


def rank_program(g, core, T, topo):
    rank = T.rank_of(core)
    if rank is None:
        return
    n = len(T.cores)
    nxt1, nxt2, prv1, prv2 = (T.cores[(rank + d) % n] for d in (1, 2, -1, -2))
    queue = {"v": g.vector, "s": g.scalar, "p": g.tensor, "g": g, "y": g.sync}
    ops, step = [], ["in"]

    def R(name, a=None, b=None, st=1):
        name = {"IO2": "KEY", "IO3": "KEYT"}.get(name, name)
        if name in ("TCH", "NL"):
            name, a, b, st = name + "X", 2 * (a or 0) + 1, 2 * (b or L), 2
        if name in MATS:
            name, a, b = "CM", 128 * MATS.index(name), 128 * MATS.index(name) + 128
        if name in ROWS:
            name, a, b = "CR", L * ROWS.index(name) + (a or 0), L * ROWS.index(name) + (b or L)
        if name[0] == "Z" and a is not None:
            a, b = a + 16, b + 16
        t = T[name]
        if a is None:
            a, b = 0, t.shape[1]
        cols = range(a, b, st)
        mask = ((1 << b) - (1 << a)) if st == 1 else sum(1 << c for c in cols)
        return (t[:, a:b] if st == 1 else t[:, a:b:st], name, mask, len(cols), None)

    def parity(z):
        return R(z, -16, -15)

    def ind(win, off):
        return (win[0].indirect(off[0]), win[1], win[2], 16 * off[3], off)

    def ap(x):
        return x[0] if isinstance(x, tuple) else x

    def add(eng, fn, outs, ins, ck, sem=None, grp=None, after=None):
        rd, wr = [], []
        for x in ins:
            if isinstance(x, tuple):
                rd.append(x[1:3])
                if x[4]:
                    rd.append(x[4][1:3])
        for x in outs:
            wr.append(x[1:3])
            if x[4]:
                rd.append(x[4][1:3])
        ops.append({"eng": eng, "fn": fn, "rd": rd, "wr": wr, "sem": sem, "need": False, "ck": ck, "grp": grp,
                    "after": after, "due": None, "join": False,
                    "kind": (step[0], eng, eng == "p" and rd[1][1].bit_length(), (wr or rd)[0][0][:1 + (wr or rd)[0][0][1:2].isalpha()],
                             (wr or rd)[0][1].bit_length() // PLAN["grain"])})
        return len(ops) - 1

    def due(name, t):
        ops[-1]["due"] = (name, t)

    turns = {}

    def in_turn(kind, k=0):
        ops[-1]["after"] = turns.get(kind)
        ops[-1]["join"] = k % PLAN["join"] > 0 and turns.get(kind) == len(ops) - 2 and ops[-1]["eng"] != "g"
        turns[kind] = len(ops) - 1

    def work(o, ins, rate=None):
        if o[4]:
            return ("sca", o[3])
        if ins and ins[0][4]:
            return ("gat", o[3])
        if rate is None:
            rate = 0.5 if all(SCRATCH[x[1]][2] in (BF, F16, U16) for x in [o] + ins) else 1.0
        return ("vec", max(64, o[3] * rate))

    def tt(o, a, b, op):
        rate = 1.0 if "psum" in (SCRATCH[a[1]][0], SCRATCH[b[1]][0]) else 2.0
        add("v", lambda: g.vector.tensor_tensor(o[0], a[0], b[0], op), [o], [a, b], work(o, [a, b], rate))

    def ts(o, a, s1, op0, s2=None, op1=None):
        if op1 is None:
            add("v", lambda: g.vector.tensor_scalar(o[0], a[0], ap(s1), None, op0), [o], [a, s1], work(o, [a]))
        else:
            add("v", lambda: g.vector.tensor_scalar(o[0], a[0], ap(s1), ap(s2), op0, op1), [o], [a, s1, s2],
                work(o, [a]))

    def cp(o, a):
        add("v", lambda: g.vector.tensor_copy(o[0], a[0]), [o], [a], work(o, [a]))

    def gcp(o, a):
        add("g", lambda: g.affine_select(o[0], a[0], [[0, o[3]]], A.is_gt, 0.0, 1, 0), [o], [a], ("pool", o[3]))

    def scan(o, d0, d1, op0, op1, first=0.0):
        add("v", lambda: g.vector.tensor_tensor_scan(o[0], d0[0], d1[0], first, op0, op1), [o], [d0, d1],
            work(o, [d0, d1]))

    def vtr(o, a):
        add("v", lambda: g.vector.transpose(o[0], a[0]), [o], [a], work(o, [a]))

    def mset(o, c):
        add("v", lambda: g.vector.memset(o[0], c), [o], [], work(o, []))

    def act(o, a, f, bias=0.0, scale=1.0, acc=None):
        if acc is None:
            add("s", lambda: g.scalar.activation(o[0], a[0], f, bias=ap(bias), scale=ap(scale)), [o], [a, bias, scale],
                work(o, [a], 1.0))
        else:
            add("s", lambda: g.scalar.activation(o[0], a[0], f, bias=ap(bias), scale=ap(scale), accum_out=acc[0]),
                [o, acc], [a, bias, scale], ("vec", max(64, o[3]) + 30))

    def copy_on(e, o, a, k=0):
        if e == "s":
            act(o, a, AF.Identity)
        else:
            (cp if e == "v" else gcp)(o, a)
        in_turn("spread" + e + o[1], k)

    def moved(e, o, a, c):
        if e == "s":
            act(o, a, AF.Identity, bias=c)
        else:
            ts(o, a, c, A.add)

    def mm(o, terms, after=None):
        counts = o[1] in ("B3", "B4")
        for i, t in enumerate(terms):
            lt, rh = t[:2]
            oo = t[2] if len(t) > 2 else o
            first, end = i == 0, i == len(terms) - 1
            add("p", lambda lt=lt, rh=rh, oo=oo, first=first, end=end: g.tensor.matmul(oo[0], lt[0], rh[0], first, end),
                [oo], [lt, rh], ("pe", max(64, rh[3]) * (4 if SCRATCH[rh[1]][2] == F32 else 1)),
                after=(after if first else len(ops) - 1))
            ops[-1]["join"] = i % (PLAN["split"] if counts else 99) > 0
        if counts:
            ops[-len(terms)]["after"] = turns.get(o[1])
            turns[o[1]] = len(ops) - 1
        return len(ops) - 1

    def iota(o, pat, base, cm, isint=False):
        if isint:
            add("g", lambda: g.iota(o[0], pat, base, cm), [o], [], ("pool", o[3]))
        else:
            add("g", lambda: g.iota(o[0], pat, base, cm, allow_small_or_imprecise_dtypes=True), [o], [], ("pool", o[3]))

    totals = {}

    def dma(eng, out, in_, sem, val, outs, ins, kib):
        totals[sem] = val
        add(eng, lambda: queue[eng].dma_start(out, in_).then_inc(T.sem[sem], 16), outs, ins, ("dma", kib), (sem, val))
        in_turn("dma" + eng)

    sent = [0]

    def send(src, dst, to, frm, sem):
        rid, pid = topo.addr(to)[:2]
        mask = topo.mask(core, to)
        sent[0] += len(topo.engines(core, to))
        i = add("g", lambda: g.remote_dma(dst[0], src[0], T.sem[sem], T.sem.sent, pid, rid, mask), [], [src],
                ("send", src[3] * 256), ("sent", 0))
        val = len(topo.engines(frm, core))
        totals[sem] = val
        add("x", None, [dst], [], ("vec", 0), (sem, val), after=i)

    col = lambda j: R("COL", j, j + 1)
    PMC, CAPF, C255, NE15, EQ15, H0, H1, PG, GC, SBC, SBH = (col(j) for j in range(11))
    IDN = R("IW", 16, 144)
    LK = [R("WK", 15 - k, 143 - k) for k in range(16)]

    SH = 128.0 if PLAN["less"] else 0.0
    for (a, b), sem in zip(PLAN["seg0"], ("lt", "lu")):
        dma("y", T.T32[:, a:b], T.traj[:, a:b], sem, 16, [R("T32", a, b)], [], 64)
    dma("s", R("Z0", 0, L)[0], T.amt[:], "lz", 16, [R("Z0", 0, L)], [], 64)
    dma("y", T.CAPI[:, 0:1], T.cap[:], "lc", 16, [R("CAPI", 0, 1)], [], 1)
    for h, sem in enumerate(("lxa", "lxb")):
        a, b = h * W // 2, (h + 1) * W // 2
        dma("y", T.X[:, L + a:L + b], T.sect[:, a:b], sem, 16, [R("X", L + a, L + b)], [], 512 * (h + 1))
    for a, b, e in PLAN["less"]:
        moved(e, R("X", L + a, L + b), R("X", L + a, L + b), -128.0)
    iota(R("COLI", 0, 1), [[0, 1]], 0, 1, True)
    iota(R("IO1"), [[1, 160]], 0, -1)
    iota(R("IO2"), [[0, 16], [1, 16]], 0, 0)
    iota(R("PM", 0, 128), [[16, 8], [0, 16]], 0, 0)
    iota(R("IO3"), [[-16, 16], [0, 16]], 240, 0)
    mset(R("Z0", -16, 0), -256.0)
    for r in range(RO):
        mset(R("ZO%d" % r, -16, 0), -256.0)
    mset(R("X", 0, L), 0.0); mset(R("SCB"), -BIG); mset(R("ONE"), 1.0); mset(R("C32"), -1.0 / 32); mset(R("NLX"), 0.0)
    ts(R("COLI", 1, 2), R("COLI", 0, 1), 15, A.bitwise_and)
    ts(R("COLI", 2, 3), R("COLI", 0, 1), 112, A.bitwise_and)
    ts(R("COLI", 3, 4), R("COLI", 0, 1), 16, A.bitwise_and)
    opening = []
    for i, (a, b) in enumerate(PLAN["seg0"]):
        cp(R("TU0", a, b), R("T32", a, b))
        opening += [(R("TU0", a, b), R("TC0", a, b), nxt1, prv1, TSEM[i] + "0"),
                    (R("Z0", a or -16, b), R("ZC0", a or -16, b), nxt1, prv1, ZSEM[i] + "0")]
    opening += [(R("Z0"), R("ZJ0"), nxt2, prv2, "zj"), (R("TU0"), R("TJ0"), nxt2, prv2, "tj0")]
    for i, m in enumerate(opening):
        send(*m)
        ops[-2]["after"] = len(ops) - 4 if i else None
    cp(PMC, R("COLI", 1, 2)); cp(PG, R("COLI", 2, 3))
    ts(H0, R("COLI", 3, 4), 0.0, A.is_equal); ts(H1, R("COLI", 3, 4), 0.0, A.not_equal)
    ts(NE15, R("COLI", 1, 2), 15.0, A.not_equal); ts(EQ15, R("COLI", 1, 2), 15.0, A.is_equal)
    ts(col(22), R("COLI", 1, 2), 1.0, A.is_equal, 663552.0, A.mult); tt(col(23), col(22), EQ15, A.add)
    act(R("CE"), R("ONE"), AF.Identity, scale=col(23))
    ts(CAPF, R("CAPI", 0, 1), -SH, A.add); ts(C255, R("CAPI", 0, 1), -1.0, A.mult, 255.0, A.add)
    ts(R("WK"), R("IO1"), PMC, A.add, 15.0, A.is_equal)
    ts(R("IW"), R("IO1"), 16.0, A.is_equal)
    ts(R("BO"), R("PM", 0, 128), PG, A.is_equal)
    ts(R("DM"), R("IO2"), PMC, A.is_equal)
    ts(R("RST"), R("IO2"), 0.0, A.is_equal, -BIG, A.mult)
    ts(R("SD"), R("IO2"), 0.0, A.not_equal, 8192.0, A.mult)
    ts(R("IO3"), R("IO3"), PMC, A.add)
    tt(R("CSP"), R("IO3"), R("SD"), A.max)
    ts(R("SD"), R("RST"), 1.0 / 128, A.mult, 1.0 / 32, A.add)
    tt(R("DF"), IDN, R("IW", 15, 143), A.subtract)
    ts(R("R15"), R("BO"), EQ15, A.mult)
    ts(R("IW0"), R("IW"), H0, A.mult); ts(R("IW1"), R("IW"), H1, A.mult)
    ts(R("DF"), R("DF"), NE15, A.mult)
    ts(R("E15"), IDN, EQ15, A.mult)
    ts(R("TCH"), R("T32"), -2048.0, A.add)
    for nm, src, sc in (("NBO", R("BO"), -1.0), ("NI", IDN, -1.0), ("I5", IDN, 5.0), ("I4", IDN, 4.0),
                        ("IK", IDN, -4096.0), ("IN32", IDN, -32.0), ("IP32", IDN, 32.0), ("BOF", R("BO"), 1.0),
                        ("NI64", IDN, -64.0), ("NBOF", R("BO"), -16.0), ("R64", R("R15"), 64.0), ("NB8K", R("BO"), -8192.0),
                        ("NR64", R("R15"), -64.0), ("I64", IDN, 64.0), ("I512", IDN, 512.0), ("IN256", IDN, -256.0)):
        act(R(nm), src, AF.Identity, scale=sc)
    act(R("NDM"), R("DM"), AF.Identity, bias=-16384.0, scale=16384.0)
    act(R("NDM2"), R("DM"), AF.Identity, bias=-14080.0, scale=16384.0)

    iota(R("JS"), [[16, 64]], 15, 0)
    cp(R("J16"), R("JS"))
    ts(R("MJ"), R("BO"), NE15, A.mult, -1.0, A.mult)
    for a in range(0, 1024, L):
        ts(R("KEEP", a, a + L), R("RST"), 0.0, A.is_equal)
    ts(col(20), R("COLI", 1, 2), 0.0, A.is_equal); tt(col(21), col(20), EQ15, A.subtract)
    ts(R("MD"), R("IW", 31, 159), EQ15, A.mult); ts(R("EQ", 0, 128), IDN, col(21), A.mult)
    tt(R("MD"), R("MD"), R("DF"), A.subtract); tt(R("MD"), R("MD"), R("EQ", 0, 128), A.add)

    def gather(win, offs, parts, fused, name, t0):
        clock, done = t0, {}
        for a, b, e in parts:
            o, src = R("XG", 16 * a, 16 * b), ind(win, offs(a, b))
            if e == "f":
                tt(R(fused[0], 16 * a, 16 * b), src, R(fused[1], 16 * a, 16 * b), fused[2])
            else:
                moved(e, o, src, SH - 128.0 if name == "jg" else 0.0)
            in_turn("gather" + ops[-1]["eng"])
            due(name + str(a), clock)
            clock += DUE[name] * (b - a) / L
            done.update({lane: clock for lane in range(a, b)})
        return done

    def cut_prep(z, segs, plan):
        for a, b in segs:
            act(R("RR", a, b), R(z, a, b), AF.Relu, bias=C255)
            act(R("THR1", a, b), R("RR", a, b), AF.Identity, bias=256.0 - SH, scale=-1.0)
            act(R("B0", a, b), R("RR", a, b), AF.Identity, bias=255.0 - SH, scale=-1.0)
            act(R("B0", L + a, L + b), R("RR", a, b), AF.Identity, bias=256.0 - SH, scale=-1.0)
        if "s" in PLAN["ge"]:
            act(SBC, parity(z), AF.Identity, bias=-256.0 * 244.5, scale=-256.0)
        for a, b, e in plan:
            for k in range(1, 16):
                copy_on(e[k % len(e)], R("D1", 16 * a + k, 16 * b, 16), R("THR1", a, b), k - 1)

    def seg_of(segs, a):
        return [s[0] <= a < s[1] for s in segs].index(True)

    def cnt_at(segs, a, b):
        return R("B3" if seg_of(segs, a) % 2 == 0 else "B4", a, b)

    cut_prep("ZC0", PLAN["seg0"], PLAN["cexp0"])
    for r in range(RO):
        s = str(r)
        last = r == RO - 1
        zc, zj, zh = "ZC" + s, ("ZJ0" if r == 0 else "ZO%d" % (r - 1)), ("Z0" if r == 0 else "ZH%d" % (r - 1))
        xa, xb = ("X", "X2") if r % 2 == 0 else ("X2", "X")
        XW, XT = R(xa, L, L + W), R(xa)
        tc = DUE["first"] + r * (DUE["cut"] + DUE["judge"] + DUE["home"])
        tj = tc + DUE["cut"]
        th = tj + DUE["judge"]

        def c_scan(a, b):
            if (a, b) in flagged:
                scan(R("ST", 16 * a, 16 * b), R("KEEP", 0, 16 * (b - a)), R("XG", 16 * a, 16 * b), A.mult, A.max)
                return
            x0 = R("XG", 16 * a, 16 * b, 16)
            tt(x0, x0, R("B0", a, b), A.max)
            tt(R("D1", 16 * a, 16 * b, 16), x0, R("B0", L + a, L + b), A.min)
            scan(R("ST", 16 * a, 16 * b), R("XG", 16 * a, 16 * b), R("D1", 16 * a, 16 * b), A.max, A.min)

        def c_place(i, a, b):
            u, v, o = a // 16, b // 16, 8 * (len(PLAN["cseg"]) - i)
            less = [(R("NBO"), R("THR1", a, b))]
            for lo, hi in flagged:
                if a <= lo < b:
                    less += [(R("BO"), R("THR1", lo, hi), cnt_at(PLAN["cseg"], lo, hi)),
                             (R("NBO"), R("ONE", lo, hi), cnt_at(PLAN["cseg"], lo, hi))]
            mm(cnt_at(PLAN["cseg"], a, b), less + [(LK[k], R("ST", 16 * a + k, 16 * b, 16)) for k in range(16)])
            ts(R("TCC", a, b), R("TC" + s, a, b), -2048.0, A.add)
            if PLAN["ge"][i] == "s":
                act(R("GE" + s, a, b), cnt_at(PLAN["cseg"], a, b), AF.Sigmoid, bias=SBC, scale=256.0)
            else:
                ts(R("GE" + s, a, b), cnt_at(PLAN["cseg"], a, b), parity(zc), A.subtract, 245.0, A.is_ge)
            mm(R("B5", a, b), [(R("E15"), R("ONE", a, b)), (R("DF"), R("GE" + s, a, b))])
            tt(R("PROD", a, b), R("B5", a, b), R("TCC", a, b), A.mult)
            place = (R("BO"), R("PROD", a, b))
            got = mm(R("B6", a, b), [(IDN, R("NDM", a, b)), place])
            mm(R("B6", L + a, L + b), [place], got)
            held = lambda lo, hi: R("SCB", o + lo, o + hi)
            scan(held(a + 1, b + 1), R("RST", a, b), R("B6", a, b), A.add, A.max, -BIG)
            terms = [(IDN, R("NDM2", a, b)), place]
            for w in [15] + list(range(u, v - 1)):
                if w == 15:
                    tt(R("EQ", 15 * L + a, 15 * L + b), R("B6", L + a, L + b), held(a, b), A.is_equal)
                    lo = a
                else:
                    lo = 16 * (w + 1)
                    ts(R("EQ", w * L + lo, w * L + b), R("B6", L + lo, L + b), held(lo, lo + 1), A.is_equal)
                terms.append((R("NB8K"), R("EQ", w * L + lo, w * L + b), R("B7", lo, b)))
            mm(R("B7", a, b), terms)
            scan(R("NS", a, b), R("CSP", a, b), R("B7", a, b), A.min, A.max, BIG)
            cp(R("OS" + s, u, v), R("NS", a + 15, b, 16))
            due("cq%d" % a, done[a] + DUE["cq"])
            if a == 0:
                mm(R("B5", L, L + b), [(IDN, R("J16", 0, b)), (IDN, R("NDM", 0, b)), (R("MJ"), R("GE" + s, 0, b))])
                scan(R("JS", 0, b), R("RST", 0, b), R("B5", L, L + b), A.add, A.max, -BIG)
                cp(R("OR", u, v), R("JS", 15, b, 16))
                tt(R("MN", a, b), ind(R("XL", 0, 16 * b), R("OR", u, v)), R("NQC", a, b), A.min)
            else:
                tt(R("MN", a, b), ind(XT, R("OS" + s, u, v)), R("NQC", a, b), A.min)

        step[0] = "c"
        cgat = PLAN["cgat0" if r == 0 else "cgat"]
        flagged = [(a, b) for a, b, e in cgat if e == "f"]
        for a, b in flagged:
            act(R("D1", 16 * a, 16 * b, 16), R("THR1", a, b), AF.Identity)
        done = gather(XW, lambda a, b: R("TC" + s, a, b), cgat, ("XG", "D1", A.is_ge), "cg", tc)
        b = PLAN["cseg"][-1][1]
        act(R("XL", 0, 16 * b), ind(XW, R("TC" + s, 0, b)), AF.Identity)
        in_turn("gathers")
        act(R("QB"), R(zc, 0, L), AF.Identity, bias=159.625, scale=0.25)
        act(R("NQC"), R("QB"), AF.Identity, bias=415.0 - SH, scale=-1.0)
        act(R("QC"), R("QB"), AF.Identity, bias=-160.0)
        for a, b in PLAN["cchk"]:
            c_scan(a, b)
        for i, (a, b) in enumerate(PLAN["cseg"]):
            c_place(i, a, b)
        for a, b in PLAN["cseg"]:
            tt(ind(XT, R("OS" + s, a // 16, b // 16)), R("MN", a, b), R("QC", a, b), A.add)
        for (a, b), sem in zip(PLAN["gseg"], ("gj", "gk")):
            send(R("GE" + s, a, b), R("GJ" + s, a, b), nxt1, prv1, sem + s)
        send(R("OS" + s), R("OJ" + s), nxt1, prv1, "oj" + s)
        send(R("GE" + s), R("GH" + s), prv1, nxt1, "gh" + s)
        dma("y", T[xb][:], T[xa][:], "cx" + s, 16, [R(xb)], [XT], 1024)
        if r == 0:
            for j in range(4):
                dma("s", T.MV[:, j * Q:(j + 1) * Q], T.mv[:], "lm", 64, [R("MV", j * Q, (j + 1) * Q)], [R("ZJ0")],
                    512 * (j + 1))
        hgat = PLAN["hgat2" if last else "hgat"]
        ts(R("TJF"), R("TJ" + s), -2048.0, A.add)
        mm(R("B1", L, 2 * L), [(R("MD"), R("TJF"))])
        vtr(R("TTS"), R("B1", L, 2 * L))
        act(GC, parity(zj), AF.Identity, bias=1.6875 - 16.0, scale=-1.0 / 16)
        act(R("RJ"), R(zj, 0, L), AF.Relu, bias=C255)
        act(R("B1", 0, L), R("RJ"), AF.Identity, bias=127.0625, scale=-1.0)
        act(R("RJB"), R("RJ"), AF.Identity, bias=-127.0)
        act(R("QB2"), R(zj, 0, L), AF.Identity, bias=159.625, scale=0.25)
        act(R("QJ"), R("QB2"), AF.Identity, bias=-224.0)
        act(R("B2", 0, L), R(zh, 0, L), AF.Identity, bias=CAPF, scale=-1.0)
        EF = lambda a, b: R("B2", L + a, L + b)
        mm(EF(0, L), [(R("I5"), R("TCH")), (R("BO"), R(zh, 0, L))])
        act(R("QH"), EF(0, L), AF.Identity, bias=162.0 + 3.0 / 8192, scale=1.0 / 4096)
        mm(EF(0, L), [(R("IK"), R("QH")), (R("BO"), R("CE")), (R("I4"), R("TCH")), (R("BO"), R(zh, 0, L))])
        if "s" in PLAN["nl"]:
            act(SBH, parity(zh), AF.Identity, bias=256.0 * 228.5, scale=256.0)
        for a, b in PLAN.get("hspread2" if last else "hspread") or [x[:2] for x in hgat if x[2] == "f"]:
            act(R("RH", a, b), R(zh, a, b), AF.Relu, bias=C255)
            act(R("THH", a, b), R("RH", a, b), AF.Identity, bias=255.0 - SH, scale=-1.0)
            for k in range(16):
                copy_on(PLAN["hexp"][k % len(PLAN["hexp"])], R("DH", 16 * a + k, 16 * b, 16), R("THH", a, b))

        def j_cmp(a, b, e):
            tops = [R("VJ", k * L + a, k * L + b) for k in range(16)]
            for k in range(16):
                tt(tops[k], R("XG", 16 * a + k, 16 * b, 16), R("B1", a, b), A.max)
                in_turn("judge", k)
            mm(cnt_at(PLAN["jseg"], a, b), [(R("BO"), R("RJB", a, b))] + [(LK[k], tops[k]) for k in range(16)])

        def j_verdict(i, a, b, sem):
            tot, u0 = cnt_at(PLAN["jseg"], a, b), R("B1", L + a, L + b)
            u, v = a // 16, b // 16
            ts(R("FL", a, b), tot, -1.46875, A.add)
            tt(u0, tot, R("FL", a, b), A.subtract)
            tt(u0, u0, R("GG", a, b), A.is_le)
            tt(R("KEY", a, b), u0, R("FL", a, b), A.mult)
            mm(R("B7", L + a, L + b), [(R("BOF"), R("KEY", a, b))])
            act(R("RF", a, b), R("B7", L + a, L + b), AF.Sign, acc=col(12 + 2 * i))
            if i and not last:
                act(col(13 + 2 * i), col(12 + 2 * i), AF.Identity, bias=col(11 + 2 * i) if i > 1 else col(12))
            mm(R("B5", L + a, L + b), [(IDN, R("QJ", a, b)), (R("NI"), R("EE", a, b)), (R("R64"), R("GJ" + s, a, b)),
                                       (R("NI64"), R("RF", a, b)) if a else (R("NBOF"), R("KEY", a, b))])
            if PLAN["jd"][i] == "s":
                act(R("DJ", a, b), R("B5", L + a, L + b), AF.Relu)
            else:
                ts(R("DJ", a, b), R("B5", L + a, L + b), 0.0, A.max)
            due("jw%d" % a, done[a] + DUE["jw"])
            ts(R("VS" + s, a + b, 2 * b), R("B7", L + a, L + b), 0.0, A.is_equal, 2048.0, A.add)
            pm, w = R("B0", a, b), R("B0", L + a, L + b)
            vtr(R("KEYT", a, b), R("KEY", a, b))
            scan(pm, R("SD", a, b), R("KEYT", a, b), A.add, A.max)
            tt(w, pm, R("KEYT", a, b), A.is_gt)
            scan(R("SC2", a, b), R("TTS", a, b), w, A.add, A.mult)
            tt(R("RS", u, v), R("SC2", a + 15, b, 16), R("TTS", a, b, 16), A.add)
            for hp in range(2):
                mm(R("B6", u + hp, v, 2),
                   [(R("IW%d" % hp, 16 - 16 * (h - hp), 144 - 16 * (h - hp)), R("RS", u + h, v, 2)) for h in range(2)])
            ts(R("OY", u, v), R("B6", u, v), 2048.0, A.add)
            cp(R("VS" + s, 2 * a, a + b), ind(R("MV"), R("OY", u, v)))
            send(R("VS" + s, 2 * a, 2 * b), R("VH" + s, 2 * a, 2 * b), prv2, nxt2, sem)
            due("ja%d" % a, done[a] + DUE["ja"] + EST["hop"])

        def j_amounts(i, a, b):
            count, hz = col(11 + 2 * len(PLAN["jseg"])), R("B6", L + a, L + b)
            mm(hz, [(R("BO"), R("C32", a, b)), (IDN, R(zj, a, b)), (R("I512"), R("RF", a, b)), (IDN, R("YM", a, b))])
            act(R("FM", a, b), hz, AF.Identity, bias=MAGIC - 256.0 + SH / 2, scale=0.5)
            act(R("HF", a, b), R("FM", a, b), AF.Identity, bias=-MAGIC)
            mm(R("B5", a, b), [(IDN, R(zj, a, b)), (R("IN256"), R("RF", a, b))])
            tt(R("ZO" + s, a, b), R("B5", a, b), R("HF", a, b), A.max)
            if not last:
                if a == 0:
                    act(R("COLB", 0, 1), count, AF.Identity, bias=127.875, scale=0.5)
                    act(parity("ZO" + s), R("COLB", 0, 1), AF.Identity, bias=count, scale=-2.0)
                lo = a or -16
                send(R("ZO" + s, lo, b), R("ZC%d" % (r + 1), lo, b), prv1, nxt1, ZSEM[i] + str(r + 1))
                due("jz%d" % a, done[a] + DUE["jz"] + EST["hop"])

        def y_m(where):
            for a, b, e in PLAN["zseg"]:
                if e == where:
                    act(R("YM", a, b), ind(XW if e == "m" else R(xb, L, L + W), R("OY", a // 16, b // 16)), AF.Identity)

        step[0] = "j"
        done = gather(XW, lambda a, b: R("TJ" + s, a, b), PLAN["jgat"], ("VF", "DX", A.max), "jg", tj)
        for a, b in PLAN["gseg"]:
            act(R("GG", a, b), R("GJ" + s, a, b), AF.Identity, scale=GC)
        act(R("OLD"), ind(XT, R("OJ" + s)), AF.Identity)
        mm(R("B7", 0, L), [(IDN, R("QJ")), (IDN, R("OLD"))])
        act(R("EE"), R("B7", 0, L), AF.Relu, bias=SH - 191.0)
        for a, b, e in PLAN.get("jchk") or PLAN["jgat"]:
            j_cmp(a, b, e)
        for i, ((a, b), sem) in enumerate(zip(PLAN["jseg"], VSEM)):
            j_verdict(i, a, b, sem + s)
        y_m("m")
        for a, b in PLAN["jseg"]:
            tt(ind(XT, R("OJ" + s, a // 16, b // 16)), R("OLD", a, b), R("DJ", a, b), A.add)
        y_m("c")
        for i, (a, b, e) in enumerate(PLAN["zseg"]):
            j_amounts(i, a, b)
        if last and not SH:
            dma("y", T.ysect[:], T[xa][:, L:L + W], "ox", 16, [], [XW, R("VH" + s, 0, 2)], 1024)
        elif last:
            for a, b, e in PLAN["more"]:
                moved(e, R("ST", a, b), R(xa, L + a, L + b), 128.0)
            for h in range(2):
                a, b = h * W // 2, (h + 1) * W // 2
                dma("y", T.ysect[:, a:b], T.ST[:, a:b], "ox", 32, [], [R("ST", a, b), R("VH" + s, 0, 2)], 512 * (h + 1))
        else:
            mm(R("B7", 0, L), [(IDN, R("OLD")), (R("NI"), R("EE"))])
            act(R("U1"), R("B7", 0, L), AF.Identity)
            mm(R("B7", 0, L), [(IDN, R("EE")), (R("NR64"), R("GJ" + s)), (R("I64"), R("RF"))])
            act(R("RU"), R("B7", 0, L), AF.Relu)
            for a, b in PLAN["cseg"]:
                tt(ind(R(xb), R("OJ" + s, a // 16, b // 16)), R("U1", a, b), R("RU", a, b), A.add)
        send(R("ZO" + s), R("ZH" + s), prv2, nxt2, "zh" + s)

        def voff(a, b):
            lo = PLAN["jseg"][seg_of(PLAN["jseg"], a)][0]
            return lo + a, lo + b

        def aoff(a, b):
            hi = PLAN["jseg"][seg_of(PLAN["jseg"], a)][1]
            return hi + a, hi + b

        def h_cmp(a, b, e):
            if e == "f":
                flags = [R("SF", 16 * a + k, 16 * b, 16) for k in range(16)]
            else:
                flags = [R("VJ", k * L + a, k * L + b) for k in range(16)]
                for k in range(16):
                    tt(flags[k], R("XG", 16 * a + k, 16 * b, 16), R("B2", a, b), A.is_gt)
                    in_turn("home", k)
            mm(cnt_at(PLAN["hseg"], a, b),
               [(R("IN32"), R("GH" + s, a, b)), (R("IP32"), R("PH", *aoff(a, b)))]
               + [(LK[k], flags[k]) for k in range(16)])

        def h_new(i, a, b, sem):
            u, bank, lo = R("B1", L + a, L + b), "B5" if i % 2 else "B6", 2 * a % L
            hi = lo + 2 * (b - a)
            mm(R(bank, lo, hi, 2), [(IDN, R("PH", *voff(a, b))), (R("NI"), R("TCH", a, b))])
            tt(u, EF(a, b), R("PH", *aoff(a, b)), A.mult)
            tt(R(bank, lo + 1, hi, 2), u, R("TCH", a, b), A.add)
            if PLAN["nl"][i] == "s":
                act(R("NL", a, b), cnt_at(PLAN["hseg"], a, b), AF.Sigmoid, bias=SBH, scale=-256.0)
            else:
                ts(R("NL", a, b), cnt_at(PLAN["hseg"], a, b), parity(zh), A.subtract, 229.0, A.is_lt)
            scan(R("TCHX", 2 * a, 2 * b), R("NLX", 2 * a, 2 * b), R(bank, lo, hi), A.mult, A.add)
            if last:
                ts(R("TF", a, b), R("TCH", a, b), 2048.0, A.add)
                dma("y", T.ytraj[:, a:b], T.TF[:, a:b], "ot", 16 * len(PLAN["hseg"]), [], [R("TF", a, b)], 64)
                due("hn%d" % a, done[a] + DUE["hn"])
            else:
                nx = str(r + 1)
                ts(R("TU" + nx, a, b), R("TCH", a, b), 2048.0, A.add)
                send(R("TU" + nx, a, b), R("TC" + nx, a, b), nxt1, prv1, sem + nx)
                due("hn%d" % a, done[a] + DUE["hn"] + EST["hop"])

        step[0] = "h"
        done = gather(XW, lambda a, b: R("VH" + s, *voff(a, b)), hgat, ("SF", "DH", A.is_gt), "hg", th)
        for a, b in PLAN["jseg"]:
            ts(R("PH", 2 * a, 2 * b), R("VH" + s, 2 * a, 2 * b), -2048.0, A.add)
        for a, b, e in hgat:
            h_cmp(a, b, e)
        if last:
            dma("s", T.yamt[:], R("ZH" + s, 0, L)[0], "oz", 16, [], [R("ZH" + s, 0, L)], 64)
        for i, ((a, b), sem) in enumerate(zip(PLAN["hseg"], TSEM)):
            h_new(i, a, b, sem)
        if not last:
            nx = str(r + 1)
            send(R("TU" + nx), R("TJ" + nx), nxt2, prv2, "tj" + nx)
            cut_prep("ZC" + nx, [x[:2] for x in PLAN["zseg"]], PLAN["cexp"])

    link(ops)
    if not FOUND:
        FOUND.append(find_order(ops))
    _took, order, turn = FOUND[0]

    place = {i: p for p, i in enumerate(order)}
    known = {e: {} for e in "vspgyx"}
    for i in order:
        op = ops[i]
        kn = known[op["eng"]]
        keep = []
        for j in sorted(op["data"] | turn[i], key=lambda j: -place[j]):
            src = ops[j]["sem"][0] if ops[j]["sem"] else ops[j]["eng"]
            if src == "sent" or (src == "p" and op["eng"] == "p") or op["eng"] == "x" or kn.get(src, -1) >= place[j]:
                continue
            keep.append(j)
            ops[j]["need"] = True
            kn[src] = place[j]
            for key, v in ops[j]["knew"].items():
                kn[key] = max(kn.get(key, -1), v)
        op["deps"] = keep
        op["knew"] = {} if op["eng"] == "x" else dict(kn)
    count = {"v": 0, "s": 0, "p": 0, "g": 0}
    for i in order:
        op = ops[i]
        if op["sem"] is None and op["need"]:
            count[op["eng"]] += 1
            op["sig"] = ("s" + op["eng"], count[op["eng"]])
        else:
            op["sig"] = op["sem"]
    for i in order:
        op = ops[i]
        if op["fn"] is None:
            continue
        for j in op["deps"]:
            queue[op["eng"]].wait_ge(T.sem[ops[j]["sig"][0]], ops[j]["sig"][1])
        ins = op["fn"]()
        if op["sem"] is None and op["need"]:
            ins.then_inc(T.sem[op["sig"][0]], 1)
    for e in count:
        totals["s" + e] = count[e]
    totals["sent"] = sent[0]
    for name in SEMAPHORES:
        if totals.get(name, 0):
            g.wait_ge(T.sem[name], totals[name])
